import numpy as np
import ml_dtypes


def mxq(x, axis, fmt="e4m3"):
    dtype, down = {"e4m3": (ml_dtypes.float8_e4m3fn, 7), "e5m2": (ml_dtypes.float8_e5m2, 14)}[fmt]
    v = np.moveaxis(np.asarray(x, np.float32).astype(ml_dtypes.bfloat16).astype(np.float64), axis, -1)
    blocks = v.reshape(v.shape[:-1] + (-1, 32))
    amax = np.abs(blocks).max(-1, keepdims=True)
    byte = np.maximum(np.where(amax > 0, np.frexp(amax)[1] - 1 + 127, 0) - down, 1)
    scale = np.exp2(byte - 127.0)
    codes = (blocks / scale).astype(np.float32).astype(dtype).astype(np.float64)
    return np.moveaxis((codes * scale).reshape(v.shape), -1, axis)


WIDE = False


def mx_kscale(k):
    if not WIDE:
        return np.ones(k)
    levels = np.array([18, -18])
    if k % 512:
        return np.exp2(np.random.permutation(np.resize(levels, k // 32))).repeat(32)
    a = np.empty((k // 512, 16))
    for p in range(k // 512):
        a[p, :8] = np.random.permutation(np.resize(levels, 8))
        for g in range(8):
            far = levels[np.abs(levels - a[p, g]) >= 10]
            a[p, g + 8] = far[np.random.randint(len(far))]
    return np.exp2(a.ravel()).repeat(32)


def f64(x):
    return np.asarray(x).astype(np.float64)


def striped(idx):
    return np.tile(np.asarray(idx).reshape(-1, 16).T, (8, 1)).astype(np.uint16)


def unstriped(offs):
    return offs[:16].T.reshape(-1).astype(np.int64)


def setup_inputs():
    n = np.random.standard_normal
    uni = np.random.uniform
    idx = np.random.permutation(2048)[:512]
    f_f = mx_kscale(512)
    f_i = np.ones(2048)
    f_i[idx] = mx_kscale(512)
    f_r = mx_kscale(512)
    return {
        "qT": (n((512, 512)) * f_r[None, :]).astype(np.float32),
        "G": (n((512, 512)) / np.sqrt(512) / f_r[:, None]).astype(np.float32),
        "cT": (n((512, 2048)) * f_i[None, :]).astype(np.float32),
        "wk": (n((512, 512)) / np.sqrt(512) * f_f[None, :]).astype(np.float32),
        "ts": np.tile(uni(0.75, 1.3, 2048) / f_i, (128, 1)).astype(np.float32),
        "cf": (uni(0.75, 1.3, (512, 1)) / f_f[:, None]).astype(np.float32),
        "offs": striped(idx),
    }


def reference(qT, G, cT, wk, ts, cf, offs):
    idx = unstriped(offs)
    cT_i = f64(cT)[:, idx]
    ts_i = f64(ts)[:1][:, idx]
    b = mxq(f64(qT), 1, "e4m3") @ mxq(f64(G), 0, "e5m2")
    dk = f64(cf) * ts_i * b
    dc = mxq(f64(wk), 1, "e4m3") @ mxq(dk, 0, "e5m2")
    out_0 = np.zeros((512, 2048))
    out_0[:, idx] = dc
    out_1 = mxq(cT_i, 1, "e4m3") @ mxq(dk, 1, "e5m2").T
    return out_0, out_1

@@ -1,0 +1,231 @@
+from contextlib import ExitStack
+
+import concourse.mybir as mybir
+from concourse.masks import make_identity
+
+F32 = mybir.dt.float32
+BF16 = mybir.dt.bfloat16
+U32 = mybir.dt.uint32
+U16 = mybir.dt.uint16
+U8 = mybir.dt.uint8
+E4M3 = mybir.dt.float8_e4m3fn_x4
+E5M2 = mybir.dt.float8_e5m2_x4
+MULT = mybir.AluOpType.mult
+COPY = mybir.ActivationFunctionType.Copy
+
+P = 128
+PACK = 4
+K = P * PACK
+TOKENS = 2048
+FLOPS = 3 * 2 * K * K * K
+
+
+def tile_attend_gmla_cW_kernel(tc, qT, G, cT, wk, ts, cf, offs, out_0, out_1):
+    nc = tc.nc
+    with ExitStack() as ctx:
+        keep = ctx.enter_context(tc.tile_pool(name="keep", bufs=1))
+        psum = ctx.enter_context(tc.psum_pool(name="psum", bufs=1))
+
+        def held(shape, dtype, name, tag=None):
+            return keep.tile(shape, dtype, name=name, tag=tag or name, align_bytes=64)
+
+        def turn_bank():
+            return psum.tile([P, PACK, P], F32, name="turned", tag="turned", bufs=4)
+
+        def sum_bank():
+            return psum.tile([P, K], F32, name="sums", tag="sums", bufs=4)
+
+        def quantize(grouped, fmt, codes, scales):
+            nc.vector.quantize_mx(out=codes.bitcast(fmt), scales=scales, in_=grouped)
+
+        def interleave(engine_copy, grouped, planes):
+            engine_copy(
+                out=grouped.rearrange("p (c i t) -> p c t i", i=4, t=PACK),
+                in_=planes.rearrange("p t (c i) -> p c t i", i=4),
+            )
+
+        def turn(rows, name, tag=None):
+            words = rows.bitcast(F32)
+            bank = turn_bank()
+            for u in range(2):
+                nc.tensor.transpose(bank[:, u, :], words[:, u : K // 2 : 2], identity[:])
+            grouped = held([P, K], BF16, name + "_grouped", tag=tag)
+            nc.scalar.copy(
+                out=grouped[:].bitcast(F32).rearrange("p (r u) -> p r u", u=2),
+                in_=bank[:, 0:2, :].rearrange("p u r -> p r u"),
+            )
+            codes = held([P, P], U32, name + "_codes")
+            scales = held([P, P], U8, name + "_scales")
+            quantize(grouped[:], E4M3, codes[:], scales[:])
+            return codes, scales
+
+        def product(stationary, moving):
+            bank = sum_bank()
+            nc.tensor.matmul_mx(
+                out=bank[:],
+                lhsT=stationary[0][:].bitcast(E4M3),
+                lhsT_scale=stationary[1][:],
+                rhs=moving[0][:].bitcast(E5M2),
+                rhs_scale=moving[1][:],
+                start=True,
+                stop=True,
+            )
+            return bank
+
+        offsets = keep.tile([P, K // 16], U16, name="offsets")
+        nc.sync.dma_start(offsets[:], offs)
+
+        ts_window = held([P, TOKENS], F32, "ts_window")
+        nc.vector.memset(ts_window[0 : P - 1, :], 0.0)
+        nc.scalar.dma_start(ts_window[P - 1 : P, :], ts[0:1, :])
+        cf_sb = held([P, PACK], F32, "cf_sb")
+        nc.scalar.dma_start(cf_sb[:], cf.rearrange("(p t) o -> p (t o)", t=PACK))
+
+        g_rows = G.rearrange("(p j) i -> p j i", j=PACK)
+        g_raw = []
+        for h in range(2):
+            raw = held([P, PACK, K // 2], F32, "g_raw%d" % h)
+            nc.sync.dma_start(raw[:], g_rows[:, :, h * (K // 2) : (h + 1) * (K // 2)])
+            g_raw.append(raw)
+        q_rows = qT.rearrange("(m t) r -> m t r", t=PACK)
+        q_raw = []
+        for t in range(PACK):
+            raw = held([P, K], F32, "q_raw%d" % t)
+            nc.sync.dma_start(raw[:], q_rows[:, t, :])
+            q_raw.append(raw)
+        wk_raw = []
+        for j in range(PACK):
+            raw = held([P, K], F32, "wk_raw%d" % j)
+            nc.sync.dma_start(raw[:], wk[j * P : (j + 1) * P, :])
+            wk_raw.append(raw)
+        c_raw = []
+        for j in range(PACK):
+            raw = held([P, TOKENS], F32, "c_raw%d" % j)
+            nc.sync.dma_start(raw[:], cT[j * P : (j + 1) * P, :])
+            c_raw.append(raw)
+
+        identity = held([P, P], F32, "identity")
+        make_identity(nc, identity[:])
+
+        windows = []
+        window = held([P, TOKENS], F32, "window0")
+        nc.vector.memset(window[:], 0.0)
+        windows.append(window)
+
+        g_codes = held([P, K], U32, "g_codes")
+        g_scales = held([P, K], U8, "g_scales")
+        g_grouped = [held([P, 2 * K], BF16, "g_grouped%d" % h) for h in range(2)]
+        interleave(nc.scalar.copy, g_grouped[0][:], g_raw[0][:])
+
+        ts_listed = held([P, K], F32, "ts_listed")
+        nc.vector.tensor_copy(ts_listed[:], ts_window[:].indirect(offsets[:]))
+        interleave(nc.vector.tensor_copy, g_grouped[1][:], g_raw[1][:])
+        bank = turn_bank()
+        for c in range(PACK):
+            nc.tensor.transpose(bank[:, c, :], ts_listed[:, c * P : (c + 1) * P], identity[:])
+        ts_columns = held([P, PACK], F32, "ts_columns")
+        nc.scalar.copy(out=ts_columns[:], in_=bank[:, :, P - 1])
+        bank = turn_bank()
+        for c in range(PACK):
+            nc.tensor.transpose(bank[:, c, :], ts_columns[:, c : c + 1].to_broadcast([P, P]), identity[:])
+        ts_spread = held([P, K], F32, "ts_spread")
+        nc.scalar.copy(out=ts_spread[:], in_=bank[:].rearrange("p c n -> p (c n)"))
+
+        for h in range(2):
+            cols = slice(h * (K // 2), (h + 1) * (K // 2))
+            quantize(g_grouped[h][:], E5M2, g_codes[:, cols], g_scales[:, cols])
+
+        dk_planes = held([P, PACK, K], BF16, "dk_planes")
+        for t in range(PACK):
+            q_bf = held([P, K], BF16, "q_bf%d" % t)
+            if t < 2:
+                nc.scalar.copy(out=q_bf[:], in_=q_raw[t][:])
+            else:
+                nc.vector.tensor_copy(out=q_bf[:], in_=q_raw[t][:])
+            b = product(turn(q_bf[:], "q%d" % t, tag="after_q" if t == PACK - 1 else None), (g_codes, g_scales))
+            nc.vector.scalar_tensor_tensor(
+                out=dk_planes[:, t, :], in0=b[:], scalar=cf_sb[:, t : t + 1], in1=ts_spread[:], op0=MULT, op1=MULT
+            )
+
+        dkf_grouped = [held([P, 2 * K], BF16, "dkf_grouped%d" % h, tag=tag) for h, tag in enumerate(("late_window1", "late_gather"))]
+        for h in range(2):
+            interleave(nc.vector.tensor_copy, dkf_grouped[h][:], dk_planes[:, :, h * (K // 2) : (h + 1) * (K // 2)])
+        wk_mx = []
+        wk_bf = held([P, PACK * K], BF16, "wk_bf", tag="after_q")
+        for j in range(PACK):
+            nc.scalar.copy(out=wk_bf[:, j * K : (j + 1) * K], in_=wk_raw[j][:])
+            wk_mx.append(turn(wk_bf[:, j * K : (j + 1) * K], "wk%d" % j))
+        dkf_codes = held([P, K], U32, "dkf_codes", tag="late_cast")
+        dkf_scales = held([P, K], U8, "dkf_scales", tag="late_window2")
+        for h in range(2):
+            cols = slice(h * (K // 2), (h + 1) * (K // 2))
+            quantize(dkf_grouped[h][:], E5M2, dkf_codes[:, cols], dkf_scales[:, cols])
+
+        dc_sb = []
+        for j in range(PACK):
+            dc = product(wk_mx[j], (dkf_codes, dkf_scales))
+            sb = held([P, K], F32, "dc_sb%d" % j)
+            nc.scalar.copy(out=sb[:], in_=dc[:])
+            dc_sb.append(sb)
+
+        for w in (1, 2):
+            window = held([P, TOKENS], F32, "window%d" % w, tag="late_window%d" % w)
+            nc.gpsimd.memset(window[:], 0.0)
+            windows.append(window)
+
+        c_listed = {}
+
+        def gather_on_vector(j, tag):
+            c_listed[j] = held([P, K], BF16, "c_listed%d" % j, tag=tag)
+            nc.vector.tensor_copy(c_listed[j][:], c_raw[j][:].indirect(offsets[:]))
+
+        def gather_on_scalar(j):
+            c_listed[j] = held([P, K], BF16, "c_listed%d" % j)
+            c_bf = held([P, TOKENS], BF16, "c_bf%d" % j, tag="late_cast")
+            nc.scalar.activation(c_bf[:], c_raw[j][:], COPY)
+            nc.scalar.activation(c_listed[j][:], c_bf[:].indirect(offsets[:]), COPY)
+
+        def scatter(j):
+            window = windows[j % len(windows)]
+            nc.vector.tensor_copy(window[:].indirect(offsets[:]), dc_sb[j][:])
+            nc.sync.dma_start(out_0[j * P : (j + 1) * P, :], window[:])
+
+        def wk_gradient(j):
+            sums = product(turn(c_listed[j][:], "c%d" % j), (dki_codes, dki_scales))
+            result = held([P, K], F32, "result%d" % j)
+            nc.scalar.copy(
+                out=result[:].rearrange("p (m t) -> p m t", t=PACK),
+                in_=sums[:].rearrange("p (t m) -> p m t", t=PACK),
+            )
+            nc.scalar.dma_start(out_1[j * P : (j + 1) * P, :], result[:])
+
+        gather_on_vector(0, "late_gather")
+        scatter(0)
+
+        dki_grouped = held([P, PACK * K], BF16, "dki_grouped")
+        for half in range(2):
+            bank = turn_bank()
+            for t in range(2):
+                words = dk_planes[:, 2 * half + t, :].bitcast(F32)
+                for u in range(2):
+                    nc.tensor.transpose(bank[:, 2 * t + u, :], words[:, u : K // 2 : 2], identity[:])
+            nc.scalar.copy(
+                out=dki_grouped[:, half * 2 * K : (half + 1) * 2 * K]
+                .bitcast(F32)
+                .rearrange("p (t m u) -> p t m u", t=2, u=2),
+                in_=bank[:].rearrange("p (t u) m -> p t m u", u=2),
+            )
+        dki_codes = held([P, K], U32, "dki_codes", tag="dc_sb0")
+        dki_scales = held([P, K], U8, "dki_scales")
+        quantize(dki_grouped[:], E5M2, dki_codes[:], dki_scales[:])
+
+        wk_gradient(0)
+        gather_on_scalar(1)
+        scatter(1)
+        wk_gradient(1)
+        gather_on_scalar(2)
+        gather_on_vector(3, "dc_sb1")
+        scatter(2)
+        wk_gradient(3)
+        wk_gradient(2)
+        scatter(3)

@@ -44,7 +44,7 @@ def tile_attend_gmla_cW_kernel(tc, qT, G, cT, wk, ts, cf, offs, out_0, out_1):
                 in_=planes.rearrange("p t (c i) -> p c t i", i=4),
             )
 
-        def turn(rows, name, tag=None):
+        def turn(rows, name, tag=None, codes_tag=None):
             words = rows.bitcast(F32)
             bank = turn_bank()
             for u in range(2):
@@ -54,7 +54,7 @@ def tile_attend_gmla_cW_kernel(tc, qT, G, cT, wk, ts, cf, offs, out_0, out_1):
                 out=grouped[:].bitcast(F32).rearrange("p (r u) -> p r u", u=2),
                 in_=bank[:, 0:2, :].rearrange("p u r -> p r u"),
             )
-            codes = held([P, P], U32, name + "_codes")
+            codes = held([P, P], U32, name + "_codes", tag=codes_tag)
             scales = held([P, P], U8, name + "_scales")
             quantize(grouped[:], E4M3, codes[:], scales[:])
             return codes, scales
@@ -109,7 +109,7 @@ def tile_attend_gmla_cW_kernel(tc, qT, G, cT, wk, ts, cf, offs, out_0, out_1):
 
         windows = []
         window = held([P, TOKENS], F32, "window0")
-        nc.vector.memset(window[:], 0.0)
+        nc.gpsimd.memset(window[:], 0.0)
         windows.append(window)
 
         g_codes = held([P, K], U32, "g_codes")
@@ -138,38 +138,39 @@ def tile_attend_gmla_cW_kernel(tc, qT, G, cT, wk, ts, cf, offs, out_0, out_1):
         dk_planes = held([P, PACK, K], BF16, "dk_planes")
         for t in range(PACK):
             q_bf = held([P, K], BF16, "q_bf%d" % t)
-            if t < 2:
-                nc.scalar.copy(out=q_bf[:], in_=q_raw[t][:])
-            else:
-                nc.vector.tensor_copy(out=q_bf[:], in_=q_raw[t][:])
-            b = product(turn(q_bf[:], "q%d" % t, tag="after_q" if t == PACK - 1 else None), (g_codes, g_scales))
+            (nc.scalar.copy if t < 2 else nc.vector.tensor_copy)(out=q_bf[:], in_=q_raw[t][:])
+            b = product(turn(q_bf[:], "q%d" % t), (g_codes, g_scales))
             nc.vector.scalar_tensor_tensor(
                 out=dk_planes[:, t, :], in0=b[:], scalar=cf_sb[:, t : t + 1], in1=ts_spread[:], op0=MULT, op1=MULT
             )
 
-        dkf_grouped = [held([P, 2 * K], BF16, "dkf_grouped%d" % h, tag=tag) for h, tag in enumerate(("late_window1", "late_gather"))]
+        dkf_grouped = [held([P, 2 * K], BF16, "dkf_grouped%d" % h) for h in range(2)]
         for h in range(2):
             interleave(nc.vector.tensor_copy, dkf_grouped[h][:], dk_planes[:, :, h * (K // 2) : (h + 1) * (K // 2)])
-        wk_mx = []
-        wk_bf = held([P, PACK * K], BF16, "wk_bf", tag="after_q")
-        for j in range(PACK):
-            nc.scalar.copy(out=wk_bf[:, j * K : (j + 1) * K], in_=wk_raw[j][:])
-            wk_mx.append(turn(wk_bf[:, j * K : (j + 1) * K], "wk%d" % j))
-        dkf_codes = held([P, K], U32, "dkf_codes", tag="late_cast")
-        dkf_scales = held([P, K], U8, "dkf_scales", tag="late_window2")
+        dkf_codes = held([P, K], U32, "dkf_codes")
+        dkf_scales = held([P, K], U8, "dkf_scales")
         for h in range(2):
             cols = slice(h * (K // 2), (h + 1) * (K // 2))
             quantize(dkf_grouped[h][:], E5M2, dkf_codes[:, cols], dkf_scales[:, cols])
-
-        dc_sb = []
+        wk_mx = []
+        wk_bf = held([P, PACK * K], BF16, "wk_bf", tag="q_bf3")
         for j in range(PACK):
-            dc = product(wk_mx[j], (dkf_codes, dkf_scales))
-            sb = held([P, K], F32, "dc_sb%d" % j)
-            nc.scalar.copy(out=sb[:], in_=dc[:])
-            dc_sb.append(sb)
+            nc.scalar.copy(out=wk_bf[:, j * K : (j + 1) * K], in_=wk_raw[j][:])
+            last = j == PACK - 1
+            wk_mx.append(turn(wk_bf[:, j * K : (j + 1) * K], "wk%d" % j, codes_tag="dkf_grouped1" if last else None))
 
-        for w in (1, 2):
-            window = held([P, TOKENS], F32, "window%d" % w, tag="late_window%d" % w)
+        dc = [product(wk_mx[j], (dkf_codes, dkf_scales)) for j in range(PACK)]
+        dc_sb = {}
+
+        def dc_out_of_psum(j, tag):
+            dc_sb[j] = held([P, K], F32, "dc_sb%d" % j, tag=tag)[:]
+            nc.scalar.copy(out=dc_sb[j], in_=dc[j][:])
+
+        dc_out_of_psum(0, None)
+        dc_out_of_psum(1, None)
+
+        def late_window(tag):
+            window = held([P, TOKENS], F32, "window%d" % len(windows), tag=tag)
             nc.gpsimd.memset(window[:], 0.0)
             windows.append(window)
 
@@ -181,28 +182,31 @@ def tile_attend_gmla_cW_kernel(tc, qT, G, cT, wk, ts, cf, offs, out_0, out_1):
 
         def gather_on_scalar(j):
             c_listed[j] = held([P, K], BF16, "c_listed%d" % j)
-            c_bf = held([P, TOKENS], BF16, "c_bf%d" % j, tag="late_cast")
+            c_bf = held([P, TOKENS], BF16, "c_bf%d" % j, tag="dkf_codes")
             nc.scalar.activation(c_bf[:], c_raw[j][:], COPY)
             nc.scalar.activation(c_listed[j][:], c_bf[:].indirect(offsets[:]), COPY)
 
         def scatter(j):
-            window = windows[j % len(windows)]
-            nc.vector.tensor_copy(window[:].indirect(offsets[:]), dc_sb[j][:])
+            window = windows[j % 3]
+            nc.vector.tensor_copy(window[:].indirect(offsets[:]), dc_sb[j])
             nc.sync.dma_start(out_0[j * P : (j + 1) * P, :], window[:])
 
-        def wk_gradient(j):
-            sums = product(turn(c_listed[j][:], "c%d" % j), (dki_codes, dki_scales))
-            result = held([P, K], F32, "result%d" % j)
+        def wk_gradient(j, tag=None):
+            return product(turn(c_listed[j][:], "c%d" % j, tag=tag), (dki_codes, dki_scales))
+
+        def store_wk_gradient(j, sums, result):
             nc.scalar.copy(
-                out=result[:].rearrange("p (m t) -> p m t", t=PACK),
+                out=result.rearrange("p (m t) -> p m t", t=PACK),
                 in_=sums[:].rearrange("p (t m) -> p m t", t=PACK),
             )
-            nc.scalar.dma_start(out_1[j * P : (j + 1) * P, :], result[:])
+            nc.scalar.dma_start(out_1[j * P : (j + 1) * P, :], result)
 
-        gather_on_vector(0, "late_gather")
+        gather_on_vector(0, "wk3_grouped")
+        late_window("c_raw0")
         scatter(0)
+        gather_on_vector(1, "dc_sb0")
 
-        dki_grouped = held([P, PACK * K], BF16, "dki_grouped")
+        dki_grouped = held([P, PACK * K], BF16, "dki_grouped", tag="dkf_scales")
         for half in range(2):
             bank = turn_bank()
             for t in range(2):
@@ -215,17 +219,24 @@ def tile_attend_gmla_cW_kernel(tc, qT, G, cT, wk, ts, cf, offs, out_0, out_1):
                 .rearrange("p (t m u) -> p t m u", t=2, u=2),
                 in_=bank[:].rearrange("p (t u) m -> p t m u", u=2),
             )
-        dki_codes = held([P, K], U32, "dki_codes", tag="dc_sb0")
+        dki_codes = held([P, K], U32, "dki_codes", tag="c_raw1")
         dki_scales = held([P, K], U8, "dki_scales")
         quantize(dki_grouped[:], E5M2, dki_codes[:], dki_scales[:])
 
-        wk_gradient(0)
-        gather_on_scalar(1)
+        sums = [wk_gradient(0)]
+        late_window("dkf_scales")
         scatter(1)
-        wk_gradient(1)
         gather_on_scalar(2)
-        gather_on_vector(3, "dc_sb1")
+        sums.append(wk_gradient(1, tag="dkf_codes"))
+        sums.append(wk_gradient(2))
+        dc_out_of_psum(2, "c_listed2")
         scatter(2)
-        wk_gradient(3)
-        wk_gradient(2)
+        results = held([P, PACK * K], F32, "results", tag="c2_grouped")
+        dc_sb[3] = results[:, 3 * K : PACK * K]
+        nc.scalar.copy(out=dc_sb[3], in_=dc[3][:])
+        gather_on_scalar(3)
         scatter(3)
+        for j in range(3):
+            store_wk_gradient(j, sums[j], results[:, j * K : (j + 1) * K])
+        last_result = held([P, K], F32, "last_result")
+        store_wk_gradient(3, wk_gradient(3), last_result[:])

@@ -5,6 +5,7 @@ from concourse.masks import make_identity
 
 F32 = mybir.dt.float32
 BF16 = mybir.dt.bfloat16
+I32 = mybir.dt.int32
 U32 = mybir.dt.uint32
 U16 = mybir.dt.uint16
 U8 = mybir.dt.uint8
@@ -24,16 +25,17 @@ def tile_attend_gmla_cW_kernel(tc, qT, G, cT, wk, ts, cf, offs, out_0, out_1):
     nc = tc.nc
     with ExitStack() as ctx:
         keep = ctx.enter_context(tc.tile_pool(name="keep", bufs=1))
+        laid = ctx.enter_context(tc.tile_pool(name="laid", bufs=1))
         psum = ctx.enter_context(tc.psum_pool(name="psum", bufs=1))
 
         def held(shape, dtype, name, tag=None):
             return keep.tile(shape, dtype, name=name, tag=tag or name, align_bytes=64)
 
-        def turn_bank():
-            return psum.tile([P, PACK, P], F32, name="turned", tag="turned", bufs=4)
+        def placed(shape, dtype, name, offset):
+            return laid.tile(shape, dtype, name=name, align_bytes=64, offset=offset)
 
-        def sum_bank():
-            return psum.tile([P, K], F32, name="sums", tag="sums", bufs=4)
+        def bank_tile(number):
+            return psum.tile([P, K], F32, name="bank%d" % number, tag="bank%d" % number)
 
         def quantize(grouped, fmt, codes, scales):
             nc.vector.quantize_mx(out=codes.bitcast(fmt), scales=scales, in_=grouped)
@@ -44,27 +46,23 @@ def tile_attend_gmla_cW_kernel(tc, qT, G, cT, wk, ts, cf, offs, out_0, out_1):
                 in_=planes.rearrange("p t (c i) -> p c t i", i=4),
             )
 
-        def turn(rows, name, tag=None, codes_tag=None):
+        def turn(rows, bank, place):
             words = rows.bitcast(F32)
-            bank = turn_bank()
             for u in range(2):
-                nc.tensor.transpose(bank[:, u, :], words[:, u : K // 2 : 2], identity[:])
-            grouped = held([P, K], BF16, name + "_grouped", tag=tag)
-            nc.scalar.copy(
-                out=grouped[:].bitcast(F32).rearrange("p (r u) -> p r u", u=2),
-                in_=bank[:, 0:2, :].rearrange("p u r -> p r u"),
-            )
-            codes = held([P, P], U32, name + "_codes", tag=codes_tag)
-            scales = held([P, P], U8, name + "_scales")
-            quantize(grouped[:], E4M3, codes[:], scales[:])
-            return codes, scales
+                first = (2 * place + u) * P
+                nc.tensor.transpose(bank[:, first : first + P], words[:, u : K // 2 : 2], identity[:])
 
-        def product(stationary, moving):
-            bank = sum_bank()
+        def unload(bank, count, grouped):
+            nc.scalar.copy(
+                out=grouped.bitcast(F32).rearrange("p (j r u) -> p j r u", j=count, u=2),
+                in_=bank[:, 0 : count * 2 * P].rearrange("p (j u r) -> p j r u", j=count, u=2),
+            )
+
+        def product(bank, codes, scales, moving):
             nc.tensor.matmul_mx(
                 out=bank[:],
-                lhsT=stationary[0][:].bitcast(E4M3),
-                lhsT_scale=stationary[1][:],
+                lhsT=codes.bitcast(E4M3),
+                lhsT_scale=scales,
                 rhs=moving[0][:].bitcast(E5M2),
                 rhs_scale=moving[1][:],
                 start=True,
@@ -76,167 +74,256 @@ def tile_attend_gmla_cW_kernel(tc, qT, G, cT, wk, ts, cf, offs, out_0, out_1):
         nc.sync.dma_start(offsets[:], offs)
 
         ts_window = held([P, TOKENS], F32, "ts_window")
-        nc.vector.memset(ts_window[0 : P - 1, :], 0.0)
-        nc.scalar.dma_start(ts_window[P - 1 : P, :], ts[0:1, :])
+        nc.vector.memset(ts_window[0 : P - 1, :].bitcast(I32), 0)
+        nc.sync.dma_start(ts_window[P - 1 : P, :], ts[0:1, :])
         cf_sb = held([P, PACK], F32, "cf_sb")
         nc.scalar.dma_start(cf_sb[:], cf.rearrange("(p t) o -> p (t o)", t=PACK))
 
+        q_rows = qT.rearrange("(m t) r -> m (t r)", t=PACK)
+        q01_raw = held([P, 2 * K], F32, "q01_raw")
+        nc.sync.dma_start(q01_raw[:], q_rows[:, 0 : 2 * K])
         g_rows = G.rearrange("(p j) i -> p j i", j=PACK)
         g_raw = []
         for h in range(2):
             raw = held([P, PACK, K // 2], F32, "g_raw%d" % h)
             nc.sync.dma_start(raw[:], g_rows[:, :, h * (K // 2) : (h + 1) * (K // 2)])
             g_raw.append(raw)
-        q_rows = qT.rearrange("(m t) r -> m t r", t=PACK)
-        q_raw = []
-        for t in range(PACK):
-            raw = held([P, K], F32, "q_raw%d" % t)
-            nc.sync.dma_start(raw[:], q_rows[:, t, :])
-            q_raw.append(raw)
+        q_raw = {}
+        for t in (2, 3):
+            q_raw[t] = held([P, K], F32, "q_raw%d" % t)
+            nc.sync.dma_start(q_raw[t][:], q_rows[:, t * K : (t + 1) * K])
+        wk_rows = wk.rearrange("(p j) f -> p (j f)", j=PACK)
         wk_raw = []
-        for j in range(PACK):
-            raw = held([P, K], F32, "wk_raw%d" % j)
-            nc.sync.dma_start(raw[:], wk[j * P : (j + 1) * P, :])
+        for h in range(2):
+            raw = held([P, 2 * K], F32, "wk_raw%d" % h)
+            nc.sync.dma_start(raw[:], wk_rows[:, h * 2 * K : (h + 1) * 2 * K])
             wk_raw.append(raw)
         c_raw = []
         for j in range(PACK):
             raw = held([P, TOKENS], F32, "c_raw%d" % j)
             nc.sync.dma_start(raw[:], cT[j * P : (j + 1) * P, :])
             c_raw.append(raw)
+        out_0_rows = out_0.rearrange("(p j) n -> p j n", j=PACK)
 
         identity = held([P, P], F32, "identity")
         make_identity(nc, identity[:])
-
-        windows = []
-        window = held([P, TOKENS], F32, "window0")
-        nc.gpsimd.memset(window[:], 0.0)
-        windows.append(window)
-
-        g_codes = held([P, K], U32, "g_codes")
-        g_scales = held([P, K], U8, "g_scales")
-        g_grouped = [held([P, 2 * K], BF16, "g_grouped%d" % h) for h in range(2)]
-        interleave(nc.scalar.copy, g_grouped[0][:], g_raw[0][:])
+        windows = [held([P, TOKENS], F32, "window0")]
+        nc.gpsimd.memset(windows[0][:], 0.0)
 
         ts_listed = held([P, K], F32, "ts_listed")
         nc.vector.tensor_copy(ts_listed[:], ts_window[:].indirect(offsets[:]))
-        interleave(nc.vector.tensor_copy, g_grouped[1][:], g_raw[1][:])
-        bank = turn_bank()
-        for c in range(PACK):
-            nc.tensor.transpose(bank[:, c, :], ts_listed[:, c * P : (c + 1) * P], identity[:])
-        ts_columns = held([P, PACK], F32, "ts_columns")
-        nc.scalar.copy(out=ts_columns[:], in_=bank[:, :, P - 1])
-        bank = turn_bank()
-        for c in range(PACK):
-            nc.tensor.transpose(bank[:, c, :], ts_columns[:, c : c + 1].to_broadcast([P, P]), identity[:])
-        ts_spread = held([P, K], F32, "ts_spread")
-        nc.scalar.copy(out=ts_spread[:], in_=bank[:].rearrange("p c n -> p (c n)"))
 
+        bank = bank_tile(1)
+        for c in range(PACK):
+            nc.tensor.transpose(bank[:, c * P : (c + 1) * P], ts_listed[:, c * P : (c + 1) * P], identity[:])
+        ts_columns = held([P, PACK], F32, "ts_columns")
+        nc.scalar.copy(out=ts_columns[:], in_=bank[:, P - 1 : K : P])
+
+        bank = bank_tile(0)
+        q0_bf = held([P, K], BF16, "q0_bf")
+        nc.scalar.copy(out=q0_bf[:], in_=q01_raw[:, 0:K])
+        turn(q0_bf[:], bank, 0)
+        q1_bf = held([P, K], BF16, "q1_bf", tag="ts_window")
+        nc.vector.tensor_copy(out=q1_bf[:], in_=q01_raw[:, K : 2 * K])
+        turn(q1_bf[:], bank, 1)
+        q01_grouped = held([P, 2 * K], BF16, "q01_grouped")
+        unload(bank, 2, q01_grouped[:])
+
+        bank = bank_tile(2)
+        for c in range(PACK):
+            nc.tensor.transpose(bank[:, c * P : (c + 1) * P], ts_columns[:, c : c + 1].to_broadcast([P, P]), identity[:])
+        ts_spread = held([P, K], F32, "ts_spread")
+        nc.scalar.copy(out=ts_spread[:], in_=bank[:])
+
+        g_codes = held([P, K], U32, "g_codes")
+        g_scales = held([P, K], U8, "g_scales", tag="ts_columns")
+        g_grouped = [held([P, 2 * K], BF16, "g_grouped%d" % h) for h in range(2)]
+        interleave(nc.vector.tensor_copy, g_grouped[0][:], g_raw[0][:])
+        q01_codes = held([P, 2 * P], U32, "q01_codes", tag="g_raw0")
+        q01_scales = held([P, 2 * P], U8, "q01_scales")
+        quantize(q01_grouped[:], E4M3, q01_codes[:], q01_scales[:])
+        q_codes = {t: q01_codes[:, t * P : (t + 1) * P] for t in range(2)}
+        q_scales = {t: q01_scales[:, t * P : (t + 1) * P] for t in range(2)}
+        interleave(nc.vector.tensor_copy, g_grouped[1][:], g_raw[1][:])
         for h in range(2):
             cols = slice(h * (K // 2), (h + 1) * (K // 2))
             quantize(g_grouped[h][:], E5M2, g_codes[:, cols], g_scales[:, cols])
+        g_mx = (g_codes, g_scales)
 
-        dk_planes = held([P, PACK, K], BF16, "dk_planes")
-        for t in range(PACK):
-            q_bf = held([P, K], BF16, "q_bf%d" % t)
-            (nc.scalar.copy if t < 2 else nc.vector.tensor_copy)(out=q_bf[:], in_=q_raw[t][:])
-            b = product(turn(q_bf[:], "q%d" % t), (g_codes, g_scales))
+        dk_planes = held([P, PACK * K], BF16, "dk_planes")
+        b_bank = {0: 3, 1: 4, 2: 7, 3: 5}
+        b = {}
+
+        def b_product(t):
+            b[t] = product(bank_tile(b_bank[t]), q_codes[t], q_scales[t], g_mx)
+
+        def dk_plane(t):
             nc.vector.scalar_tensor_tensor(
-                out=dk_planes[:, t, :], in0=b[:], scalar=cf_sb[:, t : t + 1], in1=ts_spread[:], op0=MULT, op1=MULT
+                out=dk_planes[:, t * K : (t + 1) * K],
+                in0=b[t][:],
+                scalar=cf_sb[:, t : t + 1],
+                in1=ts_spread[:],
+                op0=MULT,
+                op1=MULT,
             )
 
-        dkf_grouped = [held([P, 2 * K], BF16, "dkf_grouped%d" % h) for h in range(2)]
-        for h in range(2):
-            interleave(nc.vector.tensor_copy, dkf_grouped[h][:], dk_planes[:, :, h * (K // 2) : (h + 1) * (K // 2)])
+        b_product(0)
+        b_product(1)
+        q_bank = {}
+        for t, tag, engine_copy in ((2, "q01_grouped", nc.scalar.copy), (3, "g_grouped0", nc.vector.tensor_copy)):
+            q_bf = held([P, K], BF16, "q%d_bf" % t, tag=tag)
+            engine_copy(out=q_bf[:], in_=q_raw[t][:])
+            q_bank[t] = bank_tile(2 if t == 2 else 1)
+            turn(q_bf[:], q_bank[t], 0)
+        for t in (2, 3):
+            dk_plane(t - 2)
+            grouped = held([P, K], BF16, "q%d_grouped" % t)
+            unload(q_bank[t], 1, grouped[:])
+            if t == 2:
+                q_codes[t] = held([P, P], U32, "q2_codes", tag="g_raw0")[:]
+            else:
+                q_codes[t] = placed([P, P], U32, "q3_codes", 1024)[:]
+            q_scales[t] = held([P, P], U8, "q%d_scales" % t)[:]
+            quantize(grouped[:], E4M3, q_codes[t], q_scales[t])
+            b_product(t)
+        dk_plane(2)
+        dk_plane(3)
+
+        w01_bf = held([P, 2 * K], BF16, "w01_bf", tag="g_grouped0")
+        w_grouped = {}
+        w_bank = {}
+        for j in range(2):
+            nc.scalar.copy(out=w01_bf[:, j * K : (j + 1) * K], in_=wk_raw[0][:, j * K : (j + 1) * K])
+            w_bank[j] = bank_tile(j)
+            turn(w01_bf[:, j * K : (j + 1) * K], w_bank[j], 0)
+        for j in range(2):
+            w_grouped[j] = held([P, K], BF16, "w%d_grouped" % j)
+            unload(w_bank[j], 1, w_grouped[j][:])
+        w0_codes = placed([P, P], U32, "w0_codes", 1024)
+        w0_scales = held([P, P], U8, "w0_scales")
+        quantize(w_grouped[0][:], E4M3, w0_codes[:], w0_scales[:])
+
+        planes = dk_planes[:].rearrange("p (t i) -> p t i", t=PACK)
+        shares = ((0, 256, nc.vector.tensor_copy), (256, 384, nc.vector.tensor_copy), (384, 512, nc.scalar.copy))
+        dkf_grouped = []
+        for n, (first, last, engine_copy) in enumerate(shares):
+            grouped = held([P, PACK * (last - first)], BF16, "dkf_grouped%d" % n)
+            interleave(engine_copy, grouped[:], planes[:, :, first:last])
+            dkf_grouped.append(grouped)
         dkf_codes = held([P, K], U32, "dkf_codes")
         dkf_scales = held([P, K], U8, "dkf_scales")
-        for h in range(2):
-            cols = slice(h * (K // 2), (h + 1) * (K // 2))
-            quantize(dkf_grouped[h][:], E5M2, dkf_codes[:, cols], dkf_scales[:, cols])
-        wk_mx = []
-        wk_bf = held([P, PACK * K], BF16, "wk_bf", tag="q_bf3")
-        for j in range(PACK):
-            nc.scalar.copy(out=wk_bf[:, j * K : (j + 1) * K], in_=wk_raw[j][:])
-            last = j == PACK - 1
-            wk_mx.append(turn(wk_bf[:, j * K : (j + 1) * K], "wk%d" % j, codes_tag="dkf_grouped1" if last else None))
+        for n in (0, 2, 1):
+            cols = slice(shares[n][0], shares[n][1])
+            quantize(dkf_grouped[n][:], E5M2, dkf_codes[:, cols], dkf_scales[:, cols])
+        dkf_mx = (dkf_codes, dkf_scales)
 
-        dc = [product(wk_mx[j], (dkf_codes, dkf_scales)) for j in range(PACK)]
-        dc_sb = {}
+        dc = {0: product(bank_tile(0), w0_codes[:], w0_scales[:], dkf_mx)}
 
-        def dc_out_of_psum(j, tag):
-            dc_sb[j] = held([P, K], F32, "dc_sb%d" % j, tag=tag)[:]
-            nc.scalar.copy(out=dc_sb[j], in_=dc[j][:])
+        dki_grouped = held([P, PACK * K], BF16, "dki_grouped")
+        for half in range(2):
+            bank = bank_tile((5, 2)[half])
+            for t in range(2):
+                plane = 2 * half + t
+                turn(dk_planes[:, plane * K : (plane + 1) * K], bank, t)
+            unload(bank, 2, dki_grouped[:, half * 2 * K : (half + 1) * 2 * K])
 
-        dc_out_of_psum(0, None)
-        dc_out_of_psum(1, None)
+        c_listed0 = held([P, K], BF16, "c_listed0", tag="dkf_grouped2")
+        nc.vector.tensor_copy(c_listed0[:], c_raw[0][:].indirect(offsets[:]))
+        w1_codes = held([P, P], U32, "w1_codes", tag="dkf_grouped0")
+        w1_scales = held([P, P], U8, "w1_scales")
+        quantize(w_grouped[1][:], E4M3, w1_codes[:], w1_scales[:])
+        dc[1] = product(bank_tile(6), w1_codes[:], w1_scales[:], dkf_mx)
+        dki_codes = held([P, K], U32, "dki_codes")
+        dki_scales = held([P, K], U8, "dki_scales")
+        quantize(dki_grouped[:], E5M2, dki_codes[:], dki_scales[:])
+        dki_mx = (dki_codes, dki_scales)
 
-        def late_window(tag):
-            window = held([P, TOKENS], F32, "window%d" % len(windows), tag=tag)
-            nc.gpsimd.memset(window[:], 0.0)
-            windows.append(window)
-
-        c_listed = {}
-
-        def gather_on_vector(j, tag):
-            c_listed[j] = held([P, K], BF16, "c_listed%d" % j, tag=tag)
-            nc.vector.tensor_copy(c_listed[j][:], c_raw[j][:].indirect(offsets[:]))
-
-        def gather_on_scalar(j):
-            c_listed[j] = held([P, K], BF16, "c_listed%d" % j)
-            c_bf = held([P, TOKENS], BF16, "c_bf%d" % j, tag="dkf_codes")
-            nc.scalar.activation(c_bf[:], c_raw[j][:], COPY)
-            nc.scalar.activation(c_listed[j][:], c_bf[:].indirect(offsets[:]), COPY)
+        dc_sb = {0: held([P, K], F32, "dc_sb0")[:]}
+        nc.scalar.copy(out=dc_sb[0], in_=dc[0][:])
 
         def scatter(j):
-            window = windows[j % 3]
+            window = windows[j % 2]
             nc.vector.tensor_copy(window[:].indirect(offsets[:]), dc_sb[j])
-            nc.sync.dma_start(out_0[j * P : (j + 1) * P, :], window[:])
+            nc.sync.dma_start(out_0_rows[:, j, :], window[:])
 
-        def wk_gradient(j, tag=None):
-            return product(turn(c_listed[j][:], "c%d" % j, tag=tag), (dki_codes, dki_scales))
+        scatter(0)
+        windows.append(held([P, TOKENS], F32, "window1", tag="c_raw0"))
+        nc.gpsimd.memset(windows[1][:], 0.0)
 
-        def store_wk_gradient(j, sums, result):
+        w23_bf = placed([P, 2 * K], BF16, "w23_bf", 1024)
+        nc.scalar.copy(out=w23_bf[:], in_=wk_raw[1][:])
+        bank = bank_tile(3)
+        turn(c_listed0[:], bank, 0)
+        c0_grouped = held([P, K], BF16, "c0_grouped")
+        unload(bank, 1, c0_grouped[:])
+        c0_codes = held([P, P], U32, "c0_codes")
+        c0_scales = held([P, P], U8, "c0_scales")
+        quantize(c0_grouped[:], E4M3, c0_codes[:], c0_scales[:])
+        sums = {0: product(bank_tile(7), c0_codes[:], c0_scales[:], dki_mx)}
+        bank = bank_tile(0)
+        for j in range(2):
+            turn(w23_bf[:, j * K : (j + 1) * K], bank, j)
+        w23_grouped = held([P, 2 * K], BF16, "w23_grouped")
+        unload(bank, 2, w23_grouped[:])
+        c_listed12 = held([P, 2 * K], BF16, "c_listed12", tag="wk_raw1")
+        nc.vector.tensor_copy(c_listed12[:, 0:K], c_raw[1][:].indirect(offsets[:]))
+        w23_codes = held([P, 2 * P], U32, "w23_codes")
+        w23_scales = held([P, 2 * P], U8, "w23_scales")
+        quantize(w23_grouped[:], E4M3, w23_codes[:], w23_scales[:])
+        for j in range(2):
+            dc[2 + j] = product(
+                bank_tile((2, 4)[j]), w23_codes[:, j * P : (j + 1) * P], w23_scales[:, j * P : (j + 1) * P], dkf_mx
+            )
+        dc_sb[1] = placed([P, K], F32, "dc_sb1", 0)[:]
+        nc.scalar.copy(out=dc_sb[1], in_=dc[1][:])
+        scatter(1)
+
+        c2_bf = placed([P, TOKENS], BF16, "c2_bf", 2048)
+        nc.scalar.activation(c2_bf[:], c_raw[2][:], COPY)
+        nc.scalar.activation(c_listed12[:, K : 2 * K], c2_bf[:].indirect(offsets[:]), COPY)
+
+        results = held([P, PACK * K], F32, "results", tag="c_raw2")
+
+        def store_wk_gradient(j):
+            result = results[:, j * K : (j + 1) * K]
             nc.scalar.copy(
                 out=result.rearrange("p (m t) -> p m t", t=PACK),
-                in_=sums[:].rearrange("p (t m) -> p m t", t=PACK),
+                in_=sums[j][:].rearrange("p (t m) -> p m t", t=PACK),
             )
             nc.scalar.dma_start(out_1[j * P : (j + 1) * P, :], result)
 
-        gather_on_vector(0, "wk3_grouped")
-        late_window("c_raw0")
-        scatter(0)
-        gather_on_vector(1, "dc_sb0")
-
-        dki_grouped = held([P, PACK * K], BF16, "dki_grouped", tag="dkf_scales")
-        for half in range(2):
-            bank = turn_bank()
-            for t in range(2):
-                words = dk_planes[:, 2 * half + t, :].bitcast(F32)
-                for u in range(2):
-                    nc.tensor.transpose(bank[:, 2 * t + u, :], words[:, u : K // 2 : 2], identity[:])
-            nc.scalar.copy(
-                out=dki_grouped[:, half * 2 * K : (half + 1) * 2 * K]
-                .bitcast(F32)
-                .rearrange("p (t m u) -> p t m u", t=2, u=2),
-                in_=bank[:].rearrange("p (t u) m -> p t m u", u=2),
+        store_wk_gradient(0)
+        bank = bank_tile(1)
+        for j in range(2):
+            turn(c_listed12[:, j * K : (j + 1) * K], bank, j)
+        c12_grouped = held([P, 2 * K], BF16, "c12_grouped")
+        unload(bank, 2, c12_grouped[:])
+        c12_codes = held([P, 2 * P], U32, "c12_codes")
+        c12_scales = held([P, 2 * P], U8, "c12_scales")
+        quantize(c12_grouped[:], E4M3, c12_codes[:], c12_scales[:])
+        for j in range(2):
+            sums[1 + j] = product(
+                bank_tile((3, 5)[j]), c12_codes[:, j * P : (j + 1) * P], c12_scales[:, j * P : (j + 1) * P], dki_mx
             )
-        dki_codes = held([P, K], U32, "dki_codes", tag="c_raw1")
-        dki_scales = held([P, K], U8, "dki_scales")
-        quantize(dki_grouped[:], E5M2, dki_codes[:], dki_scales[:])
-
-        sums = [wk_gradient(0)]
-        late_window("dkf_scales")
-        scatter(1)
-        gather_on_scalar(2)
-        sums.append(wk_gradient(1, tag="dkf_codes"))
-        sums.append(wk_gradient(2))
-        dc_out_of_psum(2, "c_listed2")
+        dc_sb23 = held([P, 2 * K], F32, "dc_sb23", tag="wk_raw1")
+        for j in (2, 3):
+            dc_sb[j] = dc_sb23[:, (j - 2) * K : (j - 1) * K]
+            nc.scalar.copy(out=dc_sb[j], in_=dc[j][:])
         scatter(2)
-        results = held([P, PACK * K], F32, "results", tag="c2_grouped")
-        dc_sb[3] = results[:, 3 * K : PACK * K]
-        nc.scalar.copy(out=dc_sb[3], in_=dc[3][:])
-        gather_on_scalar(3)
         scatter(3)
-        for j in range(3):
-            store_wk_gradient(j, sums[j], results[:, j * K : (j + 1) * K])
-        last_result = held([P, K], F32, "last_result")
-        store_wk_gradient(3, wk_gradient(3), last_result[:])
+
+        c3_bf = held([P, TOKENS], BF16, "c3_bf", tag="c12_grouped")
+        nc.scalar.activation(c3_bf[:], c_raw[3][:], COPY)
+        store_wk_gradient(1)
+        c_listed3 = held([P, K], BF16, "c_listed3")
+        nc.scalar.activation(c_listed3[:], c3_bf[:].indirect(offsets[:]), COPY)
+        store_wk_gradient(2)
+        bank = bank_tile(1)
+        turn(c_listed3[:], bank, 0)
+        c3_grouped = held([P, K], BF16, "c3_grouped")
+        unload(bank, 1, c3_grouped[:])
+        c3_codes = held([P, P], U32, "c3_codes")
+        c3_scales = held([P, P], U8, "c3_scales")
+        quantize(c3_grouped[:], E4M3, c3_codes[:], c3_scales[:])
+        sums[3] = product(bank_tile(6), c3_codes[:], c3_scales[:], dki_mx)
+        store_wk_gradient(3)

@@ -108,7 +108,7 @@ def tile_attend_gmla_cW_kernel(tc, qT, G, cT, wk, ts, cf, offs, out_0, out_1):
         identity = held([P, P], F32, "identity")
         make_identity(nc, identity[:])
         windows = [held([P, TOKENS], F32, "window0")]
-        nc.gpsimd.memset(windows[0][:], 0.0)
+        nc.vector.memset(windows[0][:].bitcast(I32), 0)
 
         ts_listed = held([P, K], F32, "ts_listed")
         nc.vector.tensor_copy(ts_listed[:], ts_window[:].indirect(offsets[:]))
@@ -126,6 +126,8 @@ def tile_attend_gmla_cW_kernel(tc, qT, G, cT, wk, ts, cf, offs, out_0, out_1):
         q1_bf = held([P, K], BF16, "q1_bf", tag="ts_window")
         nc.vector.tensor_copy(out=q1_bf[:], in_=q01_raw[:, K : 2 * K])
         turn(q1_bf[:], bank, 1)
+        windows.append(held([P, TOKENS], F32, "window1", tag="q01_raw"))
+        nc.vector.memset(windows[1][:].bitcast(I32), 0)
         q01_grouped = held([P, 2 * K], BF16, "q01_grouped")
         unload(bank, 2, q01_grouped[:])
 
@@ -137,7 +139,7 @@ def tile_attend_gmla_cW_kernel(tc, qT, G, cT, wk, ts, cf, offs, out_0, out_1):
 
         g_codes = held([P, K], U32, "g_codes")
         g_scales = held([P, K], U8, "g_scales", tag="ts_columns")
-        g_grouped = [held([P, 2 * K], BF16, "g_grouped%d" % h) for h in range(2)]
+        g_grouped = [held([P, 2 * K], BF16, "g_grouped0", tag="ts_window"), held([P, 2 * K], BF16, "g_grouped1")]
         interleave(nc.vector.tensor_copy, g_grouped[0][:], g_raw[0][:])
         q01_codes = held([P, 2 * P], U32, "q01_codes", tag="g_raw0")
         q01_scales = held([P, 2 * P], U8, "q01_scales")
@@ -170,7 +172,7 @@ def tile_attend_gmla_cW_kernel(tc, qT, G, cT, wk, ts, cf, offs, out_0, out_1):
         b_product(0)
         b_product(1)
         q_bank = {}
-        for t, tag, engine_copy in ((2, "q01_grouped", nc.scalar.copy), (3, "g_grouped0", nc.vector.tensor_copy)):
+        for t, tag, engine_copy in ((2, "q01_grouped", nc.scalar.copy), (3, "ts_window", nc.vector.tensor_copy)):
             q_bf = held([P, K], BF16, "q%d_bf" % t, tag=tag)
             engine_copy(out=q_bf[:], in_=q_raw[t][:])
             q_bank[t] = bank_tile(2 if t == 2 else 1)
@@ -189,7 +191,7 @@ def tile_attend_gmla_cW_kernel(tc, qT, G, cT, wk, ts, cf, offs, out_0, out_1):
         dk_plane(2)
         dk_plane(3)
 
-        w01_bf = held([P, 2 * K], BF16, "w01_bf", tag="g_grouped0")
+        w01_bf = held([P, 2 * K], BF16, "w01_bf", tag="ts_window")
         w_grouped = {}
         w_bank = {}
         for j in range(2):
@@ -247,8 +249,6 @@ def tile_attend_gmla_cW_kernel(tc, qT, G, cT, wk, ts, cf, offs, out_0, out_1):
             nc.sync.dma_start(out_0_rows[:, j, :], window[:])
 
         scatter(0)
-        windows.append(held([P, TOKENS], F32, "window1", tag="c_raw0"))
-        nc.gpsimd.memset(windows[1][:], 0.0)
 
         w23_bf = placed([P, 2 * K], BF16, "w23_bf", 1024)
         nc.scalar.copy(out=w23_bf[:], in_=wk_raw[1][:])

@@ -46,11 +46,18 @@ def tile_attend_gmla_cW_kernel(tc, qT, G, cT, wk, ts, cf, offs, out_0, out_1):
                 in_=planes.rearrange("p t (c i) -> p c t i", i=4),
             )
 
-        def turn(rows, bank, place):
+        def turn(rows, bank, place, dealt=False):
             words = rows.bitcast(F32)
             for u in range(2):
                 first = (2 * place + u) * P
-                nc.tensor.transpose(bank[:, first : first + P], words[:, u : K // 2 : 2], identity[:])
+                picked = words[:, u * P : (u + 1) * P] if dealt else words[:, u : K // 2 : 2]
+                nc.tensor.transpose(bank[:, first : first + P], picked, identity[:])
+
+        def cast_dealt(engine_copy, rows, raw, count):
+            engine_copy(
+                out=rows.rearrange("p (j u w e) -> p j u w e", j=count, u=2, e=2),
+                in_=raw.rearrange("p (j w u e) -> p j u w e", j=count, u=2, e=2),
+            )
 
         def unload(bank, count, grouped):
             nc.scalar.copy(
@@ -121,11 +128,11 @@ def tile_attend_gmla_cW_kernel(tc, qT, G, cT, wk, ts, cf, offs, out_0, out_1):
 
         bank = bank_tile(0)
         q0_bf = held([P, K], BF16, "q0_bf")
-        nc.scalar.copy(out=q0_bf[:], in_=q01_raw[:, 0:K])
-        turn(q0_bf[:], bank, 0)
+        cast_dealt(nc.scalar.copy, q0_bf[:], q01_raw[:, 0:K], 1)
+        turn(q0_bf[:], bank, 0, True)
         q1_bf = held([P, K], BF16, "q1_bf", tag="ts_window")
-        nc.vector.tensor_copy(out=q1_bf[:], in_=q01_raw[:, K : 2 * K])
-        turn(q1_bf[:], bank, 1)
+        cast_dealt(nc.vector.tensor_copy, q1_bf[:], q01_raw[:, K : 2 * K], 1)
+        turn(q1_bf[:], bank, 1, True)
         windows.append(held([P, TOKENS], F32, "window1", tag="q01_raw"))
         nc.vector.memset(windows[1][:].bitcast(I32), 0)
         q01_grouped = held([P, 2 * K], BF16, "q01_grouped")
@@ -174,9 +181,9 @@ def tile_attend_gmla_cW_kernel(tc, qT, G, cT, wk, ts, cf, offs, out_0, out_1):
         q_bank = {}
         for t, tag, engine_copy in ((2, "q01_grouped", nc.scalar.copy), (3, "ts_window", nc.vector.tensor_copy)):
             q_bf = held([P, K], BF16, "q%d_bf" % t, tag=tag)
-            engine_copy(out=q_bf[:], in_=q_raw[t][:])
+            cast_dealt(engine_copy, q_bf[:], q_raw[t][:], 1)
             q_bank[t] = bank_tile(2 if t == 2 else 1)
-            turn(q_bf[:], q_bank[t], 0)
+            turn(q_bf[:], q_bank[t], 0, True)
         for t in (2, 3):
             dk_plane(t - 2)
             grouped = held([P, K], BF16, "q%d_grouped" % t)
@@ -195,9 +202,9 @@ def tile_attend_gmla_cW_kernel(tc, qT, G, cT, wk, ts, cf, offs, out_0, out_1):
         w_grouped = {}
         w_bank = {}
         for j in range(2):
-            nc.scalar.copy(out=w01_bf[:, j * K : (j + 1) * K], in_=wk_raw[0][:, j * K : (j + 1) * K])
+            cast_dealt(nc.scalar.copy, w01_bf[:, j * K : (j + 1) * K], wk_raw[0][:, j * K : (j + 1) * K], 1)
             w_bank[j] = bank_tile(j)
-            turn(w01_bf[:, j * K : (j + 1) * K], w_bank[j], 0)
+            turn(w01_bf[:, j * K : (j + 1) * K], w_bank[j], 0, True)
         for j in range(2):
             w_grouped[j] = held([P, K], BF16, "w%d_grouped" % j)
             unload(w_bank[j], 1, w_grouped[j][:])
@@ -251,7 +258,7 @@ def tile_attend_gmla_cW_kernel(tc, qT, G, cT, wk, ts, cf, offs, out_0, out_1):
         scatter(0)
 
         w23_bf = placed([P, 2 * K], BF16, "w23_bf", 1024)
-        nc.scalar.copy(out=w23_bf[:], in_=wk_raw[1][:])
+        cast_dealt(nc.scalar.copy, w23_bf[:], wk_raw[1][:], 2)
         bank = bank_tile(3)
         turn(c_listed0[:], bank, 0)
         c0_grouped = held([P, K], BF16, "c0_grouped")
@@ -262,7 +269,7 @@ def tile_attend_gmla_cW_kernel(tc, qT, G, cT, wk, ts, cf, offs, out_0, out_1):
         sums = {0: product(bank_tile(7), c0_codes[:], c0_scales[:], dki_mx)}
         bank = bank_tile(0)
         for j in range(2):
-            turn(w23_bf[:, j * K : (j + 1) * K], bank, j)
+            turn(w23_bf[:, j * K : (j + 1) * K], bank, j, True)
         w23_grouped = held([P, 2 * K], BF16, "w23_grouped")
         unload(bank, 2, w23_grouped[:])
         c_listed12 = held([P, 2 * K], BF16, "c_listed12", tag="wk_raw1")

@@ -285,9 +285,7 @@ def tile_attend_gmla_cW_kernel(tc, qT, G, cT, wk, ts, cf, offs, out_0, out_1):
         nc.scalar.copy(out=dc_sb[1], in_=dc[1][:])
         scatter(1)
 
-        c2_bf = placed([P, TOKENS], BF16, "c2_bf", 2048)
-        nc.scalar.activation(c2_bf[:], c_raw[2][:], COPY)
-        nc.scalar.activation(c_listed12[:, K : 2 * K], c2_bf[:].indirect(offsets[:]), COPY)
+        nc.vector.tensor_copy(c_listed12[:, K : 2 * K], c_raw[2][:].indirect(offsets[:]))
 
         results = held([P, PACK * K], F32, "results", tag="c_raw2")
 

@@ -287,21 +287,23 @@ def tile_attend_gmla_cW_kernel(tc, qT, G, cT, wk, ts, cf, offs, out_0, out_1):
 
         nc.vector.tensor_copy(c_listed12[:, K : 2 * K], c_raw[2][:].indirect(offsets[:]))
 
-        results = held([P, PACK * K], F32, "results", tag="c_raw2")
+        c3_bf = placed([P, TOKENS], BF16, "c3_bf", 2048)
+        nc.scalar.activation(c3_bf[:], c_raw[3][:], COPY)
+        c_listed3 = held([P, K], BF16, "c_listed3")
+        nc.scalar.activation(c_listed3[:], c3_bf[:].indirect(offsets[:]), COPY)
 
-        def store_wk_gradient(j):
-            result = results[:, j * K : (j + 1) * K]
+        def store_wk_gradient(j, result):
             nc.scalar.copy(
                 out=result.rearrange("p (m t) -> p m t", t=PACK),
                 in_=sums[j][:].rearrange("p (t m) -> p m t", t=PACK),
             )
             nc.scalar.dma_start(out_1[j * P : (j + 1) * P, :], result)
 
-        store_wk_gradient(0)
+        store_wk_gradient(0, held([P, K], F32, "result0", tag="c_raw3")[:])
         bank = bank_tile(1)
         for j in range(2):
             turn(c_listed12[:, j * K : (j + 1) * K], bank, j)
-        c12_grouped = held([P, 2 * K], BF16, "c12_grouped")
+        c12_grouped = placed([P, 2 * K], BF16, "c12_grouped", 2048)
         unload(bank, 2, c12_grouped[:])
         c12_codes = held([P, 2 * P], U32, "c12_codes")
         c12_scales = held([P, 2 * P], U8, "c12_scales")
@@ -310,25 +312,20 @@ def tile_attend_gmla_cW_kernel(tc, qT, G, cT, wk, ts, cf, offs, out_0, out_1):
             sums[1 + j] = product(
                 bank_tile((3, 5)[j]), c12_codes[:, j * P : (j + 1) * P], c12_scales[:, j * P : (j + 1) * P], dki_mx
             )
-        dc_sb23 = held([P, 2 * K], F32, "dc_sb23", tag="wk_raw1")
+        dc_sb23 = placed([P, 2 * K], F32, "dc_sb23", 4096)
         for j in (2, 3):
             dc_sb[j] = dc_sb23[:, (j - 2) * K : (j - 1) * K]
-            nc.scalar.copy(out=dc_sb[j], in_=dc[j][:])
+        nc.scalar.copy(out=dc_sb[2], in_=dc[2][:])
         scatter(2)
-        scatter(3)
-
-        c3_bf = held([P, TOKENS], BF16, "c3_bf", tag="c12_grouped")
-        nc.scalar.activation(c3_bf[:], c_raw[3][:], COPY)
-        store_wk_gradient(1)
-        c_listed3 = held([P, K], BF16, "c_listed3")
-        nc.scalar.activation(c_listed3[:], c3_bf[:].indirect(offsets[:]), COPY)
-        store_wk_gradient(2)
-        bank = bank_tile(1)
-        turn(c_listed3[:], bank, 0)
+        nc.scalar.copy(out=dc_sb[3][:, 0 : K // 2], in_=dc[3][:, 0 : K // 2])
+        turn(c_listed3[:], dc[3], 0)
         c3_grouped = held([P, K], BF16, "c3_grouped")
-        unload(bank, 1, c3_grouped[:])
+        unload(dc[3], 1, c3_grouped[:])
         c3_codes = held([P, P], U32, "c3_codes")
         c3_scales = held([P, P], U8, "c3_scales")
         quantize(c3_grouped[:], E4M3, c3_codes[:], c3_scales[:])
         sums[3] = product(bank_tile(6), c3_codes[:], c3_scales[:], dki_mx)
-        store_wk_gradient(3)
+        nc.scalar.copy(out=dc_sb[3][:, K // 2 : K], in_=dc[3][:, K // 2 : K])
+        scatter(3)
+        for j in range(1, PACK):
+            store_wk_gradient(j, held([P, K], F32, "result%d" % j)[:])

@@ -35,7 +35,7 @@ def tile_attend_gmla_cW_kernel(tc, qT, G, cT, wk, ts, cf, offs, out_0, out_1):
             return laid.tile(shape, dtype, name=name, align_bytes=64, offset=offset)
 
         def bank_tile(number):
-            return psum.tile([P, K], F32, name="bank%d" % number, tag="bank%d" % number)
+            return psum.tile([P, K], F32, name="bank%d" % number, tag="pair" if number == 2 else "bank%d" % number)[:]
 
         def quantize(grouped, fmt, codes, scales):
             nc.vector.quantize_mx(out=codes.bitcast(fmt), scales=scales, in_=grouped)
@@ -67,7 +67,7 @@ def tile_attend_gmla_cW_kernel(tc, qT, G, cT, wk, ts, cf, offs, out_0, out_1):
 
         def product(bank, codes, scales, moving):
             nc.tensor.matmul_mx(
-                out=bank[:],
+                out=bank,
                 lhsT=codes.bitcast(E4M3),
                 lhsT_scale=scales,
                 rhs=moving[0][:].bitcast(E5M2),
@@ -160,7 +160,7 @@ def tile_attend_gmla_cW_kernel(tc, qT, G, cT, wk, ts, cf, offs, out_0, out_1):
         g_mx = (g_codes, g_scales)
 
         dk_planes = held([P, PACK * K], BF16, "dk_planes")
-        b_bank = {0: 3, 1: 4, 2: 7, 3: 5}
+        b_bank = {0: 3, 1: 4, 2: 6, 3: 5}
         b = {}
 
         def b_product(t):
@@ -266,7 +266,7 @@ def tile_attend_gmla_cW_kernel(tc, qT, G, cT, wk, ts, cf, offs, out_0, out_1):
         c0_codes = held([P, P], U32, "c0_codes")
         c0_scales = held([P, P], U8, "c0_scales")
         quantize(c0_grouped[:], E4M3, c0_codes[:], c0_scales[:])
-        sums = {0: product(bank_tile(7), c0_codes[:], c0_scales[:], dki_mx)}
+        sums = {0: product(bank_tile(5), c0_codes[:], c0_scales[:], dki_mx)}
         bank = bank_tile(0)
         for j in range(2):
             turn(w23_bf[:, j * K : (j + 1) * K], bank, j, True)
@@ -289,8 +289,6 @@ def tile_attend_gmla_cW_kernel(tc, qT, G, cT, wk, ts, cf, offs, out_0, out_1):
 
         c3_bf = placed([P, TOKENS], BF16, "c3_bf", 2048)
         nc.scalar.activation(c3_bf[:], c_raw[3][:], COPY)
-        c_listed3 = held([P, K], BF16, "c_listed3")
-        nc.scalar.activation(c_listed3[:], c3_bf[:].indirect(offsets[:]), COPY)
 
         def store_wk_gradient(j, result):
             nc.scalar.copy(
@@ -300,6 +298,8 @@ def tile_attend_gmla_cW_kernel(tc, qT, G, cT, wk, ts, cf, offs, out_0, out_1):
             nc.scalar.dma_start(out_1[j * P : (j + 1) * P, :], result)
 
         store_wk_gradient(0, held([P, K], F32, "result0", tag="c_raw3")[:])
+        c_listed3 = held([P, K], BF16, "c_listed3")
+        nc.scalar.activation(c_listed3[:], c3_bf[:].indirect(offsets[:]), COPY)
         bank = bank_tile(1)
         for j in range(2):
             turn(c_listed12[:, j * K : (j + 1) * K], bank, j)
@@ -308,16 +308,12 @@ def tile_attend_gmla_cW_kernel(tc, qT, G, cT, wk, ts, cf, offs, out_0, out_1):
         c12_codes = held([P, 2 * P], U32, "c12_codes")
         c12_scales = held([P, 2 * P], U8, "c12_scales")
         quantize(c12_grouped[:], E4M3, c12_codes[:], c12_scales[:])
-        for j in range(2):
-            sums[1 + j] = product(
-                bank_tile((3, 5)[j]), c12_codes[:, j * P : (j + 1) * P], c12_scales[:, j * P : (j + 1) * P], dki_mx
-            )
         dc_sb23 = placed([P, 2 * K], F32, "dc_sb23", 4096)
         for j in (2, 3):
             dc_sb[j] = dc_sb23[:, (j - 2) * K : (j - 1) * K]
-        nc.scalar.copy(out=dc_sb[2], in_=dc[2][:])
-        scatter(2)
         nc.scalar.copy(out=dc_sb[3][:, 0 : K // 2], in_=dc[3][:, 0 : K // 2])
+        nc.scalar.copy(out=dc_sb[2], in_=dc[2])
+        scatter(2)
         turn(c_listed3[:], dc[3], 0)
         c3_grouped = held([P, K], BF16, "c3_grouped")
         unload(dc[3], 1, c3_grouped[:])
@@ -327,5 +323,10 @@ def tile_attend_gmla_cW_kernel(tc, qT, G, cT, wk, ts, cf, offs, out_0, out_1):
         sums[3] = product(bank_tile(6), c3_codes[:], c3_scales[:], dki_mx)
         nc.scalar.copy(out=dc_sb[3][:, K // 2 : K], in_=dc[3][:, K // 2 : K])
         scatter(3)
+        pair = psum.tile([P, 2 * K], F32, name="pair", tag="pair")
+        for j in range(2):
+            sums[1 + j] = product(
+                pair[:, j * K : (j + 1) * K], c12_codes[:, j * P : (j + 1) * P], c12_scales[:, j * P : (j + 1) * P], dki_mx
+            )
         for j in range(1, PACK):
             store_wk_gradient(j, held([P, K], F32, "result%d" % j)[:])

@@ -18,6 +18,7 @@ P = 128
 PACK = 4
 K = P * PACK
 TOKENS = 2048
+BANK_BYTES = 2048
 FLOPS = 3 * 2 * K * K * K
 
 
@@ -34,8 +35,8 @@ def tile_attend_gmla_cW_kernel(tc, qT, G, cT, wk, ts, cf, offs, out_0, out_1):
         def placed(shape, dtype, name, offset):
             return laid.tile(shape, dtype, name=name, align_bytes=64, offset=offset)
 
-        def bank_tile(number):
-            return psum.tile([P, K], F32, name="bank%d" % number, tag="pair" if number == 2 else "bank%d" % number)[:]
+        def bank_tile(name, number, count=1):
+            return psum.tile([P, count * K], F32, name=name, offset=number * BANK_BYTES)[:]
 
         def quantize(grouped, fmt, codes, scales):
             nc.vector.quantize_mx(out=codes.bitcast(fmt), scales=scales, in_=grouped)
@@ -65,40 +66,48 @@ def tile_attend_gmla_cW_kernel(tc, qT, G, cT, wk, ts, cf, offs, out_0, out_1):
                 in_=bank[:, 0 : count * 2 * P].rearrange("p (j u r) -> p j r u", j=count, u=2),
             )
 
-        def product(bank, codes, scales, moving):
+        def stationary(name, grouped, count, offset=None, scales_offset=None):
+            if offset is None:
+                codes = held([P, count * P], U32, name + "_codes")
+            else:
+                codes = placed([P, count * P], U32, name + "_codes", offset)
+            if scales_offset is None:
+                scales = held([P, count * P], U8, name + "_scales")
+            else:
+                scales = placed([P, count * P], U8, name + "_scales", scales_offset)
+            quantize(grouped, E4M3, codes[:], scales[:])
+            return [(codes[:, j * P : (j + 1) * P], scales[:, j * P : (j + 1) * P]) for j in range(count)]
+
+        def product(bank, still, still_format, moving, moving_format):
             nc.tensor.matmul_mx(
                 out=bank,
-                lhsT=codes.bitcast(E4M3),
-                lhsT_scale=scales,
-                rhs=moving[0][:].bitcast(E5M2),
-                rhs_scale=moving[1][:],
+                lhsT=still[0].bitcast(still_format),
+                lhsT_scale=still[1],
+                rhs=moving[0].bitcast(moving_format),
+                rhs_scale=moving[1],
                 start=True,
                 stop=True,
             )
             return bank
 
-        offsets = keep.tile([P, K // 16], U16, name="offsets")
-        nc.sync.dma_start(offsets[:], offs)
-
-        ts_window = held([P, TOKENS], F32, "ts_window")
-        nc.vector.memset(ts_window[0 : P - 1, :].bitcast(I32), 0)
-        nc.sync.dma_start(ts_window[P - 1 : P, :], ts[0:1, :])
         cf_sb = held([P, PACK], F32, "cf_sb")
         nc.scalar.dma_start(cf_sb[:], cf.rearrange("(p t) o -> p (t o)", t=PACK))
+        ts_window = placed([P, TOKENS], F32, "ts_window", 16384)
+        nc.vector.memset(ts_window[0 : P - 1, :].bitcast(I32), 0)
+        nc.scalar.dma_start(ts_window[P - 1 : P, :], ts[0:1, :])
 
-        q_rows = qT.rearrange("(m t) r -> m (t r)", t=PACK)
-        q01_raw = held([P, 2 * K], F32, "q01_raw")
-        nc.sync.dma_start(q01_raw[:], q_rows[:, 0 : 2 * K])
+        q_rows = qT.rearrange("(m t) r -> m t r", t=PACK)
+        q_raw = [held([P, 2, K], F32, "q_raw%d" % h) for h in range(2)]
+        nc.sync.dma_start(q_raw[0][:], q_rows[:, 0:2, :])
+        offsets = keep.tile([P, K // 16], U16, name="offsets")
+        nc.sync.dma_start(offsets[:], offs)
+        nc.sync.dma_start(q_raw[1][:], q_rows[:, 2:4, :])
         g_rows = G.rearrange("(p j) i -> p j i", j=PACK)
         g_raw = []
         for h in range(2):
             raw = held([P, PACK, K // 2], F32, "g_raw%d" % h)
             nc.sync.dma_start(raw[:], g_rows[:, :, h * (K // 2) : (h + 1) * (K // 2)])
             g_raw.append(raw)
-        q_raw = {}
-        for t in (2, 3):
-            q_raw[t] = held([P, K], F32, "q_raw%d" % t)
-            nc.sync.dma_start(q_raw[t][:], q_rows[:, t * K : (t + 1) * K])
         wk_rows = wk.rearrange("(p j) f -> p (j f)", j=PACK)
         wk_raw = []
         for h in range(2):
@@ -114,219 +123,178 @@ def tile_attend_gmla_cW_kernel(tc, qT, G, cT, wk, ts, cf, offs, out_0, out_1):
 
         identity = held([P, P], F32, "identity")
         make_identity(nc, identity[:])
-        windows = [held([P, TOKENS], F32, "window0")]
+        windows = [held([P, TOKENS], F32, "window%d" % w) for w in range(2)]
         nc.vector.memset(windows[0][:].bitcast(I32), 0)
-
+        nc.vector.memset(windows[1][:].bitcast(I32), 0)
         ts_listed = held([P, K], F32, "ts_listed")
         nc.vector.tensor_copy(ts_listed[:], ts_window[:].indirect(offsets[:]))
 
-        bank = bank_tile(1)
-        for c in range(PACK):
-            nc.tensor.transpose(bank[:, c * P : (c + 1) * P], ts_listed[:, c * P : (c + 1) * P], identity[:])
+        bank = bank_tile("cf_bank", 0)
+        for t in range(PACK):
+            nc.tensor.transpose(bank[:, t * P : (t + 1) * P], cf_sb[:, t : t + 1].to_broadcast([P, P]), identity[:])
+        cf_spread = held([P, K], F32, "cf_spread")
+        nc.scalar.copy(out=cf_spread[:].rearrange("p (u m e) -> p u m e", u=2, e=2), in_=bank.rearrange("p (u e m) -> p u m e", u=2, e=2))
+
+        q_bank = [bank_tile("q_bank%d" % h, 2 + h) for h in range(2)]
+        for t in range(PACK):
+            q_bf = held([P, K], BF16, "q%d_bf" % t)
+            cast_dealt(nc.scalar.copy, q_bf[:], q_raw[t // 2][:, t % 2, :], 1)
+            turn(q_bf[:], q_bank[t // 2], t % 2, True)
+        q_grouped = [held([P, 2 * K], BF16, "q_grouped0"), placed([P, 2 * K], BF16, "q_grouped1", 28672)]
+        for h in range(2):
+            nc.scalar.copy(
+                out=q_grouped[h][:].bitcast(F32).rearrange("p (m e w) -> p m e w", e=2, w=2),
+                in_=q_bank[h].rearrange("p (e w m) -> p m e w", e=2, w=2),
+            )
+
+        bank = bank_tile("ts_bank", 1)
+        for r in range(PACK):
+            nc.tensor.transpose(bank[:, r * P : (r + 1) * P], ts_listed[:, r:K:PACK], identity[:])
         ts_columns = held([P, PACK], F32, "ts_columns")
         nc.scalar.copy(out=ts_columns[:], in_=bank[:, P - 1 : K : P])
 
-        bank = bank_tile(0)
-        q0_bf = held([P, K], BF16, "q0_bf")
-        cast_dealt(nc.scalar.copy, q0_bf[:], q01_raw[:, 0:K], 1)
-        turn(q0_bf[:], bank, 0, True)
-        q1_bf = held([P, K], BF16, "q1_bf", tag="ts_window")
-        cast_dealt(nc.vector.tensor_copy, q1_bf[:], q01_raw[:, K : 2 * K], 1)
-        turn(q1_bf[:], bank, 1, True)
-        windows.append(held([P, TOKENS], F32, "window1", tag="q01_raw"))
-        nc.vector.memset(windows[1][:].bitcast(I32), 0)
-        q01_grouped = held([P, 2 * K], BF16, "q01_grouped")
-        unload(bank, 2, q01_grouped[:])
+        q_codes = held([P, K], U32, "q_codes")
+        q_scales = held([P, K], U8, "q_scales")
+        g_grouped = placed([P, PACK * K], BF16, "g_grouped", 16384)
+        g_dealt = g_grouped[:].rearrange("p (a e h s t) -> p h a s t e", a=2, e=2, h=2, t=PACK)
+        halves = [slice(0, K // 2), slice(K // 2, K)]
+        g_columns = [g_raw[h][:].rearrange("p t (s a e) -> p a s t e", a=2, e=2) for h in range(2)]
+        nc.vector.tensor_copy(out=g_dealt[:, 0], in_=g_columns[0])
+        quantize(q_grouped[0][:], E4M3, q_codes[:, halves[0]], q_scales[:, halves[0]])
+        nc.vector.tensor_copy(out=g_dealt[:, 1], in_=g_columns[1])
+        quantize(q_grouped[1][:], E4M3, q_codes[:, halves[1]], q_scales[:, halves[1]])
+        q_mx = (q_codes[:], q_scales[:])
+        b = []
+        g_codes = placed([P, K], U32, "g_codes", 29696)
+        g_scales = held([P, K], U8, "g_scales")
+        for r in range(PACK):
+            g_mx = (g_codes[:, r * P : (r + 1) * P], g_scales[:, r * P : (r + 1) * P])
+            quantize(g_grouped[:, r * K : (r + 1) * K], E5M2, g_mx[0], g_mx[1])
+            b.append(product(bank_tile("b%d" % r, 4 + r), g_mx, E5M2, q_mx, E4M3))
 
-        bank = bank_tile(2)
-        for c in range(PACK):
-            nc.tensor.transpose(bank[:, c * P : (c + 1) * P], ts_columns[:, c : c + 1].to_broadcast([P, P]), identity[:])
-        ts_spread = held([P, K], F32, "ts_spread")
-        nc.scalar.copy(out=ts_spread[:], in_=bank[:])
+        w_bf = placed([P, PACK * K], BF16, "w_bf", 25088)
+        for j in range(PACK):
+            cast_dealt(nc.scalar.copy, w_bf[:, j * K : (j + 1) * K], wk_raw[j // 2][:, (j % 2) * K : (j % 2 + 1) * K], 1)
+        w_grouped = [held([P, 2 * K], BF16, "w_grouped%d" % h) for h in range(2)]
 
-        g_codes = held([P, K], U32, "g_codes")
-        g_scales = held([P, K], U8, "g_scales", tag="ts_columns")
-        g_grouped = [held([P, 2 * K], BF16, "g_grouped0", tag="ts_window"), held([P, 2 * K], BF16, "g_grouped1")]
-        interleave(nc.vector.tensor_copy, g_grouped[0][:], g_raw[0][:])
-        q01_codes = held([P, 2 * P], U32, "q01_codes", tag="g_raw0")
-        q01_scales = held([P, 2 * P], U8, "q01_scales")
-        quantize(q01_grouped[:], E4M3, q01_codes[:], q01_scales[:])
-        q_codes = {t: q01_codes[:, t * P : (t + 1) * P] for t in range(2)}
-        q_scales = {t: q01_scales[:, t * P : (t + 1) * P] for t in range(2)}
-        interleave(nc.vector.tensor_copy, g_grouped[1][:], g_raw[1][:])
-        for h in range(2):
-            cols = slice(h * (K // 2), (h + 1) * (K // 2))
-            quantize(g_grouped[h][:], E5M2, g_codes[:, cols], g_scales[:, cols])
-        g_mx = (g_codes, g_scales)
+        def turn_wk(h, number):
+            bank = bank_tile("w_bank%d" % h, number)
+            for j in range(2):
+                turn(w_bf[:, (2 * h + j) * K : (2 * h + j + 1) * K], bank, j, True)
+            unload(bank, 2, w_grouped[h][:])
+
+        turn_wk(0, 0)
 
         dk_planes = held([P, PACK * K], BF16, "dk_planes")
-        b_bank = {0: 3, 1: 4, 2: 6, 3: 5}
-        b = {}
-
-        def b_product(t):
-            b[t] = product(bank_tile(b_bank[t]), q_codes[t], q_scales[t], g_mx)
-
-        def dk_plane(t):
-            nc.vector.scalar_tensor_tensor(
-                out=dk_planes[:, t * K : (t + 1) * K],
-                in0=b[t][:],
-                scalar=cf_sb[:, t : t + 1],
-                in1=ts_spread[:],
-                op0=MULT,
-                op1=MULT,
-            )
-
-        b_product(0)
-        b_product(1)
-        q_bank = {}
-        for t, tag, engine_copy in ((2, "q01_grouped", nc.scalar.copy), (3, "ts_window", nc.vector.tensor_copy)):
-            q_bf = held([P, K], BF16, "q%d_bf" % t, tag=tag)
-            cast_dealt(engine_copy, q_bf[:], q_raw[t][:], 1)
-            q_bank[t] = bank_tile(2 if t == 2 else 1)
-            turn(q_bf[:], q_bank[t], 0, True)
-        for t in (2, 3):
-            dk_plane(t - 2)
-            grouped = held([P, K], BF16, "q%d_grouped" % t)
-            unload(q_bank[t], 1, grouped[:])
-            if t == 2:
-                q_codes[t] = held([P, P], U32, "q2_codes", tag="g_raw0")[:]
-            else:
-                q_codes[t] = placed([P, P], U32, "q3_codes", 1024)[:]
-            q_scales[t] = held([P, P], U8, "q%d_scales" % t)[:]
-            quantize(grouped[:], E4M3, q_codes[t], q_scales[t])
-            b_product(t)
-        dk_plane(2)
-        dk_plane(3)
-
-        w01_bf = held([P, 2 * K], BF16, "w01_bf", tag="ts_window")
-        w_grouped = {}
-        w_bank = {}
-        for j in range(2):
-            cast_dealt(nc.scalar.copy, w01_bf[:, j * K : (j + 1) * K], wk_raw[0][:, j * K : (j + 1) * K], 1)
-            w_bank[j] = bank_tile(j)
-            turn(w01_bf[:, j * K : (j + 1) * K], w_bank[j], 0, True)
-        for j in range(2):
-            w_grouped[j] = held([P, K], BF16, "w%d_grouped" % j)
-            unload(w_bank[j], 1, w_grouped[j][:])
-        w0_codes = placed([P, P], U32, "w0_codes", 1024)
-        w0_scales = held([P, P], U8, "w0_scales")
-        quantize(w_grouped[0][:], E4M3, w0_codes[:], w0_scales[:])
-
-        planes = dk_planes[:].rearrange("p (t i) -> p t i", t=PACK)
-        shares = ((0, 256, nc.vector.tensor_copy), (256, 384, nc.vector.tensor_copy), (384, 512, nc.scalar.copy))
+        planes = dk_planes[:].rearrange("p (r f) -> p r f", r=PACK)
         dkf_grouped = []
-        for n, (first, last, engine_copy) in enumerate(shares):
-            grouped = held([P, PACK * (last - first)], BF16, "dkf_grouped%d" % n)
-            interleave(engine_copy, grouped[:], planes[:, :, first:last])
-            dkf_grouped.append(grouped)
         dkf_codes = held([P, K], U32, "dkf_codes")
         dkf_scales = held([P, K], U8, "dkf_scales")
-        for n in (0, 2, 1):
-            cols = slice(shares[n][0], shares[n][1])
-            quantize(dkf_grouped[n][:], E5M2, dkf_codes[:, cols], dkf_scales[:, cols])
-        dkf_mx = (dkf_codes, dkf_scales)
 
-        dc = {0: product(bank_tile(0), w0_codes[:], w0_scales[:], dkf_mx)}
+        def dk_plane(r):
+            for cols in halves if r == PACK - 1 else [slice(0, K)]:
+                nc.vector.scalar_tensor_tensor(
+                    out=planes[:, r, cols], in0=b[r][:, cols], scalar=ts_columns[:, r : r + 1], in1=cf_spread[:, cols], op0=MULT, op1=MULT
+                )
+            bank = bank_tile("dkf_bank%d" % r, 2 + r)
+            turn(planes[:, r, :], bank, 0, True)
+            if r == PACK - 1:
+                dkf_grouped.append(placed([P, K], BF16, "dkf_grouped3", 6144))
+            else:
+                dkf_grouped.append(held([P, K], BF16, "dkf_grouped%d" % r))
+            unload(bank, 1, dkf_grouped[r][:])
 
-        dki_grouped = held([P, PACK * K], BF16, "dki_grouped")
-        for half in range(2):
-            bank = bank_tile((5, 2)[half])
-            for t in range(2):
-                plane = 2 * half + t
-                turn(dk_planes[:, plane * K : (plane + 1) * K], bank, t)
-            unload(bank, 2, dki_grouped[:, half * 2 * K : (half + 1) * 2 * K])
+        def dkf_quantize(r):
+            cols = slice(r * P, (r + 1) * P)
+            quantize(dkf_grouped[r][:], E5M2, dkf_codes[:, cols], dkf_scales[:, cols])
 
-        c_listed0 = held([P, K], BF16, "c_listed0", tag="dkf_grouped2")
-        nc.vector.tensor_copy(c_listed0[:], c_raw[0][:].indirect(offsets[:]))
-        w1_codes = held([P, P], U32, "w1_codes", tag="dkf_grouped0")
-        w1_scales = held([P, P], U8, "w1_scales")
-        quantize(w_grouped[1][:], E4M3, w1_codes[:], w1_scales[:])
-        dc[1] = product(bank_tile(6), w1_codes[:], w1_scales[:], dkf_mx)
-        dki_codes = held([P, K], U32, "dki_codes")
-        dki_scales = held([P, K], U8, "dki_scales")
-        quantize(dki_grouped[:], E5M2, dki_codes[:], dki_scales[:])
-        dki_mx = (dki_codes, dki_scales)
+        dk_plane(0)
+        dk_plane(1)
+        dk_plane(2)
+        dkf_quantize(0)
+        dk_plane(3)
+        turn_wk(1, 7)
+        dkf_quantize(1)
+        w_mx = stationary("w0", w_grouped[0][:, 0:K], 1)
+        dki_first = held([P, K], BF16, "dki_first")
+        interleave(nc.vector.tensor_copy, dki_first[:], planes[:, :, 0:P])
+        dkf_quantize(2)
+        dkf_quantize(3)
+        w_mx = w_mx + stationary("w1", w_grouped[0][:, K : 2 * K], 1, 3840, 6656) + stationary("w23", w_grouped[1][:], 2, None, 6400)
+        dkf_mx = (dkf_codes[:], dkf_scales[:])
+        dc = [product(bank_tile("dc%d" % j, (6, 1, 0, 7)[j]), w_mx[j], E4M3, dkf_mx, E5M2) for j in range(PACK)]
 
-        dc_sb = {0: held([P, K], F32, "dc_sb0")[:]}
-        nc.scalar.copy(out=dc_sb[0], in_=dc[0][:])
+        c_listed = {}
+
+        def listed_on_vector(j, tile):
+            c_listed[j] = tile
+            nc.vector.tensor_copy(tile[:], c_raw[j][:].indirect(offsets[:]))
+
+        def cast_on_scalar(j):
+            c_bf = placed([P, TOKENS], BF16, "c%d_bf" % j, 0)
+            nc.scalar.activation(c_bf[:], c_raw[j][:], COPY)
+            return c_bf
+
+        def listed_on_scalar(j, c_bf):
+            c_listed[j] = held([P, K], BF16, "c_listed%d" % j)
+            nc.scalar.activation(c_listed[j][:], c_bf[:].indirect(offsets[:]), COPY)
+
+        dc_sb = {}
+
+        def drain(j, tile):
+            dc_sb[j] = tile
+            nc.scalar.copy(out=tile[:].rearrange("p (s r) -> p s r", r=PACK), in_=dc[j].rearrange("p (r s) -> p s r", r=PACK))
 
         def scatter(j):
             window = windows[j % 2]
-            nc.vector.tensor_copy(window[:].indirect(offsets[:]), dc_sb[j])
+            nc.vector.tensor_copy(window[:].indirect(offsets[:]), dc_sb[j][:])
             nc.sync.dma_start(out_0_rows[:, j, :], window[:])
 
-        scatter(0)
-
-        w23_bf = placed([P, 2 * K], BF16, "w23_bf", 1024)
-        cast_dealt(nc.scalar.copy, w23_bf[:], wk_raw[1][:], 2)
-        bank = bank_tile(3)
-        turn(c_listed0[:], bank, 0)
-        c0_grouped = held([P, K], BF16, "c0_grouped")
-        unload(bank, 1, c0_grouped[:])
-        c0_codes = held([P, P], U32, "c0_codes")
-        c0_scales = held([P, P], U8, "c0_scales")
-        quantize(c0_grouped[:], E4M3, c0_codes[:], c0_scales[:])
-        sums = {0: product(bank_tile(5), c0_codes[:], c0_scales[:], dki_mx)}
-        bank = bank_tile(0)
-        for j in range(2):
-            turn(w23_bf[:, j * K : (j + 1) * K], bank, j, True)
-        w23_grouped = held([P, 2 * K], BF16, "w23_grouped")
-        unload(bank, 2, w23_grouped[:])
-        c_listed12 = held([P, 2 * K], BF16, "c_listed12", tag="wk_raw1")
-        nc.vector.tensor_copy(c_listed12[:, 0:K], c_raw[1][:].indirect(offsets[:]))
-        w23_codes = held([P, 2 * P], U32, "w23_codes")
-        w23_scales = held([P, 2 * P], U8, "w23_scales")
-        quantize(w23_grouped[:], E4M3, w23_codes[:], w23_scales[:])
-        for j in range(2):
-            dc[2 + j] = product(
-                bank_tile((2, 4)[j]), w23_codes[:, j * P : (j + 1) * P], w23_scales[:, j * P : (j + 1) * P], dkf_mx
-            )
-        dc_sb[1] = placed([P, K], F32, "dc_sb1", 0)[:]
-        nc.scalar.copy(out=dc_sb[1], in_=dc[1][:])
-        scatter(1)
-
-        nc.vector.tensor_copy(c_listed12[:, K : 2 * K], c_raw[2][:].indirect(offsets[:]))
-
-        c3_bf = placed([P, TOKENS], BF16, "c3_bf", 2048)
-        nc.scalar.activation(c3_bf[:], c_raw[3][:], COPY)
-
-        def store_wk_gradient(j, result):
+        def store_wk_gradient(j, number):
+            sums = product(bank_tile("sums%d" % j, number), c_mx[j], E4M3, dki_mx, E5M2)
+            result = held([P, K], F32, "result%d" % j)
             nc.scalar.copy(
-                out=result.rearrange("p (m t) -> p m t", t=PACK),
-                in_=sums[j][:].rearrange("p (t m) -> p m t", t=PACK),
+                out=result[:].rearrange("p (m u e) -> p m u e", u=2, e=2), in_=sums.rearrange("p (u m e) -> p m u e", u=2, e=2)
             )
-            nc.scalar.dma_start(out_1[j * P : (j + 1) * P, :], result)
+            nc.scalar.dma_start(out_1[j * P : (j + 1) * P, :], result[:])
 
-        store_wk_gradient(0, held([P, K], F32, "result0", tag="c_raw3")[:])
-        c_listed3 = held([P, K], BF16, "c_listed3")
-        nc.scalar.activation(c_listed3[:], c3_bf[:].indirect(offsets[:]), COPY)
-        bank = bank_tile(1)
+        dki_parts = [dki_first, placed([P, K], BF16, "dki_second", 5376)]
+        interleave(nc.scalar.copy, dki_parts[1][:], planes[:, :, P : 2 * P])
+        listed_on_vector(0, placed([P, K], BF16, "c_listed0", 6912))
+        drain(0, placed([P, K], F32, "dc_sb0", 9216))
+        scatter(0)
+        listed_on_vector(1, placed([P, K], BF16, "c_listed1", 8704))
+        c_bf = cast_on_scalar(2)
+        drain(1, held([P, K], F32, "dc_sb1"))
+        scatter(1)
+        listed_on_scalar(2, c_bf)
+        dki_parts.append(held([P, 2 * K], BF16, "dki_rest", tag="c_raw2"))
+        interleave(nc.scalar.copy, dki_parts[2][:], planes[:, :, 2 * P : K])
+        dki_codes = placed([P, K], U32, "dki_codes", 10240)
+        dki_scales = held([P, K], U8, "dki_scales")
+        for part, cols in zip(dki_parts, (slice(0, P), slice(P, 2 * P), slice(2 * P, K))):
+            quantize(part[:], E5M2, dki_codes[:, cols], dki_scales[:, cols])
+        dki_mx = (dki_codes[:], dki_scales[:])
+
+        c_grouped = [held([P, 2 * K], BF16, "c_grouped%d" % h) for h in range(2)]
+        bank = bank_tile("c01_bank", 2)
         for j in range(2):
-            turn(c_listed12[:, j * K : (j + 1) * K], bank, j)
-        c12_grouped = placed([P, 2 * K], BF16, "c12_grouped", 2048)
-        unload(bank, 2, c12_grouped[:])
-        c12_codes = held([P, 2 * P], U32, "c12_codes")
-        c12_scales = held([P, 2 * P], U8, "c12_scales")
-        quantize(c12_grouped[:], E4M3, c12_codes[:], c12_scales[:])
-        dc_sb23 = placed([P, 2 * K], F32, "dc_sb23", 4096)
-        for j in (2, 3):
-            dc_sb[j] = dc_sb23[:, (j - 2) * K : (j - 1) * K]
-        nc.scalar.copy(out=dc_sb[3][:, 0 : K // 2], in_=dc[3][:, 0 : K // 2])
-        nc.scalar.copy(out=dc_sb[2], in_=dc[2])
+            turn(c_listed[j][:], bank, j)
+        unload(bank, 2, c_grouped[0][:])
+        c_mx = stationary("c01", c_grouped[0][:], 2)
+        c_bf = cast_on_scalar(3)
+        drain(2, held([P, K], F32, "dc_sb2"))
         scatter(2)
-        turn(c_listed3[:], dc[3], 0)
-        c3_grouped = held([P, K], BF16, "c3_grouped")
-        unload(dc[3], 1, c3_grouped[:])
-        c3_codes = held([P, P], U32, "c3_codes")
-        c3_scales = held([P, P], U8, "c3_scales")
-        quantize(c3_grouped[:], E4M3, c3_codes[:], c3_scales[:])
-        sums[3] = product(bank_tile(6), c3_codes[:], c3_scales[:], dki_mx)
-        nc.scalar.copy(out=dc_sb[3][:, K // 2 : K], in_=dc[3][:, K // 2 : K])
+        listed_on_scalar(3, c_bf)
+        store_wk_gradient(0, 4)
+        bank = bank_tile("c2_bank", 3)
+        turn(c_listed[2][:], bank, 0)
+        unload(bank, 1, c_grouped[1][:, 0:K])
+        bank = bank_tile("c3_bank", 0)
+        turn(c_listed[3][:], bank, 0)
+        unload(bank, 1, c_grouped[1][:, K : 2 * K])
+        c_mx = c_mx + stationary("c23", c_grouped[1][:], 2)
+        drain(3, held([P, K], F32, "dc_sb3", tag="c_raw3"))
         scatter(3)
-        pair = psum.tile([P, 2 * K], F32, name="pair", tag="pair")
-        for j in range(2):
-            sums[1 + j] = product(
-                pair[:, j * K : (j + 1) * K], c12_codes[:, j * P : (j + 1) * P], c12_scales[:, j * P : (j + 1) * P], dki_mx
-            )
-        for j in range(1, PACK):
-            store_wk_gradient(j, held([P, K], F32, "result%d" % j)[:])
+        for j, number in ((1, 1), (2, 5), (3, 6)):
+            store_wk_gradient(j, number)

@@ -116,7 +116,7 @@ def tile_attend_gmla_cW_kernel(tc, qT, G, cT, wk, ts, cf, offs, out_0, out_1):
             wk_raw.append(raw)
         c_raw = []
         for j in range(PACK):
-            raw = held([P, TOKENS], F32, "c_raw%d" % j)
+            raw = placed([P, TOKENS], F32, "c_raw2", 45056) if j == 2 else held([P, TOKENS], F32, "c_raw%d" % j)
             nc.sync.dma_start(raw[:], cT[j * P : (j + 1) * P, :])
             c_raw.append(raw)
         out_0_rows = out_0.rearrange("(p j) n -> p j n", j=PACK)
@@ -220,7 +220,7 @@ def tile_attend_gmla_cW_kernel(tc, qT, G, cT, wk, ts, cf, offs, out_0, out_1):
         interleave(nc.vector.tensor_copy, dki_first[:], planes[:, :, 0:P])
         dkf_quantize(2)
         dkf_quantize(3)
-        w_mx = w_mx + stationary("w1", w_grouped[0][:, K : 2 * K], 1, 3840, 6656) + stationary("w23", w_grouped[1][:], 2, None, 6400)
+        w_mx = w_mx + stationary("w1", w_grouped[0][:, K : 2 * K], 1, 38400, 6656) + stationary("w23", w_grouped[1][:], 2, None, 6400)
         dkf_mx = (dkf_codes[:], dkf_scales[:])
         dc = [product(bank_tile("dc%d" % j, (6, 1, 0, 7)[j]), w_mx[j], E4M3, dkf_mx, E5M2) for j in range(PACK)]
 
@@ -231,7 +231,7 @@ def tile_attend_gmla_cW_kernel(tc, qT, G, cT, wk, ts, cf, offs, out_0, out_1):
             nc.vector.tensor_copy(tile[:], c_raw[j][:].indirect(offsets[:]))
 
         def cast_on_scalar(j):
-            c_bf = placed([P, TOKENS], BF16, "c%d_bf" % j, 0)
+            c_bf = placed([P, TOKENS], BF16, "c%d_bf" % j, {2: 36352, 3: 32768}[j])
             nc.scalar.activation(c_bf[:], c_raw[j][:], COPY)
             return c_bf
 
@@ -268,7 +268,7 @@ def tile_attend_gmla_cW_kernel(tc, qT, G, cT, wk, ts, cf, offs, out_0, out_1):
         drain(1, held([P, K], F32, "dc_sb1"))
         scatter(1)
         listed_on_scalar(2, c_bf)
-        dki_parts.append(held([P, 2 * K], BF16, "dki_rest", tag="c_raw2"))
+        dki_parts.append(placed([P, 2 * K], BF16, "dki_rest", 45056))
         interleave(nc.scalar.copy, dki_parts[2][:], planes[:, :, 2 * P : K])
         dki_codes = placed([P, K], U32, "dki_codes", 10240)
         dki_scales = held([P, K], U8, "dki_scales")
@@ -276,14 +276,14 @@ def tile_attend_gmla_cW_kernel(tc, qT, G, cT, wk, ts, cf, offs, out_0, out_1):
             quantize(part[:], E5M2, dki_codes[:, cols], dki_scales[:, cols])
         dki_mx = (dki_codes[:], dki_scales[:])
 
-        c_grouped = [held([P, 2 * K], BF16, "c_grouped%d" % h) for h in range(2)]
+        c_grouped = [placed([P, 2 * K], BF16, "c_grouped0", 39936), held([P, 2 * K], BF16, "c_grouped1")]
         bank = bank_tile("c01_bank", 2)
         for j in range(2):
             turn(c_listed[j][:], bank, j)
         unload(bank, 2, c_grouped[0][:])
         c_mx = stationary("c01", c_grouped[0][:], 2)
         c_bf = cast_on_scalar(3)
-        drain(2, held([P, K], F32, "dc_sb2"))
+        drain(2, placed([P, K], F32, "dc_sb2", 49152))
         scatter(2)
         listed_on_scalar(3, c_bf)
         store_wk_gradient(0, 4)

@@ -129,16 +129,10 @@ def tile_attend_gmla_cW_kernel(tc, qT, G, cT, wk, ts, cf, offs, out_0, out_1):
         ts_listed = held([P, K], F32, "ts_listed")
         nc.vector.tensor_copy(ts_listed[:], ts_window[:].indirect(offsets[:]))
 
-        bank = bank_tile("cf_bank", 0)
-        for t in range(PACK):
-            nc.tensor.transpose(bank[:, t * P : (t + 1) * P], cf_sb[:, t : t + 1].to_broadcast([P, P]), identity[:])
-        cf_spread = held([P, K], F32, "cf_spread")
-        nc.scalar.copy(out=cf_spread[:].rearrange("p (u m e) -> p u m e", u=2, e=2), in_=bank.rearrange("p (u e m) -> p u m e", u=2, e=2))
-
         q_bank = [bank_tile("q_bank%d" % h, 2 + h) for h in range(2)]
         for t in range(PACK):
             q_bf = held([P, K], BF16, "q%d_bf" % t)
-            cast_dealt(nc.scalar.copy, q_bf[:], q_raw[t // 2][:, t % 2, :], 1)
+            cast_dealt((nc.scalar.copy, nc.vector.tensor_copy)[t // 2], q_bf[:], q_raw[t // 2][:, t % 2, :], 1)
             turn(q_bf[:], q_bank[t // 2], t % 2, True)
         q_grouped = [held([P, 2 * K], BF16, "q_grouped0"), placed([P, 2 * K], BF16, "q_grouped1", 28672)]
         for h in range(2):
@@ -147,11 +141,17 @@ def tile_attend_gmla_cW_kernel(tc, qT, G, cT, wk, ts, cf, offs, out_0, out_1):
                 in_=q_bank[h].rearrange("p (e w m) -> p m e w", e=2, w=2),
             )
 
-        bank = bank_tile("ts_bank", 1)
+        bank = bank_tile("ts_bank", 3)
         for r in range(PACK):
             nc.tensor.transpose(bank[:, r * P : (r + 1) * P], ts_listed[:, r:K:PACK], identity[:])
         ts_columns = held([P, PACK], F32, "ts_columns")
         nc.scalar.copy(out=ts_columns[:], in_=bank[:, P - 1 : K : P])
+
+        bank = bank_tile("cf_bank", 0)
+        for t in range(PACK):
+            nc.tensor.transpose(bank[:, t * P : (t + 1) * P], cf_sb[:, t : t + 1].to_broadcast([P, P]), identity[:])
+        cf_spread = held([P, K], F32, "cf_spread")
+        nc.scalar.copy(out=cf_spread[:].rearrange("p (u m e) -> p u m e", u=2, e=2), in_=bank.rearrange("p (u e m) -> p u m e", u=2, e=2))
 
         q_codes = held([P, K], U32, "q_codes")
         q_scales = held([P, K], U8, "q_scales")
@@ -175,15 +175,10 @@ def tile_attend_gmla_cW_kernel(tc, qT, G, cT, wk, ts, cf, offs, out_0, out_1):
         w_bf = placed([P, PACK * K], BF16, "w_bf", 25088)
         for j in range(PACK):
             cast_dealt(nc.scalar.copy, w_bf[:, j * K : (j + 1) * K], wk_raw[j // 2][:, (j % 2) * K : (j % 2 + 1) * K], 1)
-        w_grouped = [held([P, 2 * K], BF16, "w_grouped%d" % h) for h in range(2)]
-
-        def turn_wk(h, number):
-            bank = bank_tile("w_bank%d" % h, number)
-            for j in range(2):
-                turn(w_bf[:, (2 * h + j) * K : (2 * h + j + 1) * K], bank, j, True)
-            unload(bank, 2, w_grouped[h][:])
-
-        turn_wk(0, 0)
+        bank = bank_tile("w0_bank", 1)
+        turn(w_bf[:, 0:K], bank, 0, True)
+        w0_grouped = held([P, K], BF16, "w0_grouped")
+        unload(bank, 1, w0_grouped[:])
 
         dk_planes = held([P, PACK * K], BF16, "dk_planes")
         planes = dk_planes[:].rearrange("p (r f) -> p r f", r=PACK)
@@ -205,24 +200,30 @@ def tile_attend_gmla_cW_kernel(tc, qT, G, cT, wk, ts, cf, offs, out_0, out_1):
             unload(bank, 1, dkf_grouped[r][:])
 
         def dkf_quantize(r):
-            cols = slice(r * P, (r + 1) * P)
-            quantize(dkf_grouped[r][:], E5M2, dkf_codes[:, cols], dkf_scales[:, cols])
+            for h in range(2):
+                cols = slice((h * PACK + r) * (P // 2), (h * PACK + r + 1) * (P // 2))
+                quantize(dkf_grouped[r][:, halves[h]], E5M2, dkf_codes[:, cols], dkf_scales[:, cols])
 
         dk_plane(0)
         dk_plane(1)
         dk_plane(2)
         dkf_quantize(0)
         dk_plane(3)
-        turn_wk(1, 7)
+        banks = bank_tile("w123_banks", 6, 2)
+        for j in range(1, PACK):
+            turn(w_bf[:, j * K : (j + 1) * K], banks, j, True)
+        w123_grouped = held([P, 3 * K], BF16, "w123_grouped")
+        unload(banks[:, K // 2 : K], 1, w123_grouped[:, 0:K])
+        unload(banks[:, K : 2 * K], 2, w123_grouped[:, K : 3 * K])
         dkf_quantize(1)
-        w_mx = stationary("w0", w_grouped[0][:, 0:K], 1)
+        w_mx = stationary("w0", w0_grouped[:], 1, 38400)
         dki_first = held([P, K], BF16, "dki_first")
         interleave(nc.vector.tensor_copy, dki_first[:], planes[:, :, 0:P])
         dkf_quantize(2)
         dkf_quantize(3)
-        w_mx = w_mx + stationary("w1", w_grouped[0][:, K : 2 * K], 1, 38400, 6656) + stationary("w23", w_grouped[1][:], 2, None, 6400)
+        w_mx = w_mx + stationary("w1", w123_grouped[:, 0:K], 1, None, 6656) + stationary("w23", w123_grouped[:, K : 3 * K], 2, None, 6400)
         dkf_mx = (dkf_codes[:], dkf_scales[:])
-        dc = [product(bank_tile("dc%d" % j, (6, 1, 0, 7)[j]), w_mx[j], E4M3, dkf_mx, E5M2) for j in range(PACK)]
+        dc = [product(bank_tile("dc%d" % j, (0, 1, 6, 7)[j]), w_mx[j], E4M3, dkf_mx, E5M2) for j in range(PACK)]
 
         c_listed = {}
 
@@ -241,18 +242,20 @@ def tile_attend_gmla_cW_kernel(tc, qT, G, cT, wk, ts, cf, offs, out_0, out_1):
 
         dc_sb = {}
 
-        def drain(j, tile):
+        def drain(j, tile, first=0, last=2):
             dc_sb[j] = tile
-            nc.scalar.copy(out=tile[:].rearrange("p (s r) -> p s r", r=PACK), in_=dc[j].rearrange("p (r s) -> p s r", r=PACK))
+            nc.scalar.copy(
+                out=tile[:].rearrange("p (h s r) -> p h s r", h=2, r=PACK)[:, first:last],
+                in_=dc[j].rearrange("p (h r s) -> p h s r", h=2, r=PACK)[:, first:last],
+            )
 
         def scatter(j):
             window = windows[j % 2]
             nc.vector.tensor_copy(window[:].indirect(offsets[:]), dc_sb[j][:])
             nc.sync.dma_start(out_0_rows[:, j, :], window[:])
 
-        def store_wk_gradient(j, number):
+        def store_wk_gradient(j, number, result):
             sums = product(bank_tile("sums%d" % j, number), c_mx[j], E4M3, dki_mx, E5M2)
-            result = held([P, K], F32, "result%d" % j)
             nc.scalar.copy(
                 out=result[:].rearrange("p (m u e) -> p m u e", u=2, e=2), in_=sums.rearrange("p (u m e) -> p m u e", u=2, e=2)
             )
@@ -261,40 +264,44 @@ def tile_attend_gmla_cW_kernel(tc, qT, G, cT, wk, ts, cf, offs, out_0, out_1):
         dki_parts = [dki_first, placed([P, K], BF16, "dki_second", 5376)]
         interleave(nc.scalar.copy, dki_parts[1][:], planes[:, :, P : 2 * P])
         listed_on_vector(0, placed([P, K], BF16, "c_listed0", 6912))
-        drain(0, placed([P, K], F32, "dc_sb0", 9216))
+        c0_bank = bank_tile("c0_bank", 2)
+        turn(c_listed[0][:], c0_bank, 0)
+        drain(0, held([P, K], F32, "dc_sb0"))
         scatter(0)
-        listed_on_vector(1, placed([P, K], BF16, "c_listed1", 8704))
         c_bf = cast_on_scalar(2)
         drain(1, held([P, K], F32, "dc_sb1"))
         scatter(1)
         listed_on_scalar(2, c_bf)
+        listed_on_vector(1, placed([P, K], BF16, "c_listed1", 37376))
         dki_parts.append(placed([P, 2 * K], BF16, "dki_rest", 45056))
         interleave(nc.scalar.copy, dki_parts[2][:], planes[:, :, 2 * P : K])
-        dki_codes = placed([P, K], U32, "dki_codes", 10240)
+        dki_codes = placed([P, K], U32, "dki_codes", 38400)
         dki_scales = held([P, K], U8, "dki_scales")
         for part, cols in zip(dki_parts, (slice(0, P), slice(P, 2 * P), slice(2 * P, K))):
             quantize(part[:], E5M2, dki_codes[:, cols], dki_scales[:, cols])
         dki_mx = (dki_codes[:], dki_scales[:])
 
-        c_grouped = [placed([P, 2 * K], BF16, "c_grouped0", 39936), held([P, 2 * K], BF16, "c_grouped1")]
-        bank = bank_tile("c01_bank", 2)
-        for j in range(2):
-            turn(c_listed[j][:], bank, j)
-        unload(bank, 2, c_grouped[0][:])
-        c_mx = stationary("c01", c_grouped[0][:], 2)
+        c0_grouped = held([P, K], BF16, "c0_grouped")
+        unload(c0_bank, 1, c0_grouped[:])
+        c_mx = stationary("c0", c0_grouped[:], 1)
+        drain(3, placed([P, K], F32, "dc_sb3", 51200), 0, 1)
         c_bf = cast_on_scalar(3)
         drain(2, placed([P, K], F32, "dc_sb2", 49152))
         scatter(2)
         listed_on_scalar(3, c_bf)
-        store_wk_gradient(0, 4)
-        bank = bank_tile("c2_bank", 3)
-        turn(c_listed[2][:], bank, 0)
-        unload(bank, 1, c_grouped[1][:, 0:K])
-        bank = bank_tile("c3_bank", 0)
-        turn(c_listed[3][:], bank, 0)
-        unload(bank, 1, c_grouped[1][:, K : 2 * K])
-        c_mx = c_mx + stationary("c23", c_grouped[1][:], 2)
-        drain(3, held([P, K], F32, "dc_sb3", tag="c_raw3"))
+        bank = bank_tile("c12_bank", 3)
+        for j in range(2):
+            turn(c_listed[1 + j][:], bank, j)
+        c12_grouped = held([P, 2 * K], BF16, "c12_grouped", tag="c_raw3")
+        unload(bank, 2, c12_grouped[:])
+        c_mx = c_mx + stationary("c12", c12_grouped[:], 2)
+        turn(c_listed[3][:], dc[3], 0)
+        c3_grouped = placed([P, K], BF16, "c3_grouped", 56832)
+        unload(dc[3], 1, c3_grouped[:])
+        c_mx = c_mx + stationary("c3", c3_grouped[:], 1)
+        drain(3, dc_sb[3], 1, 2)
         scatter(3)
-        for j, number in ((1, 1), (2, 5), (3, 6)):
-            store_wk_gradient(j, number)
+        store_wk_gradient(0, 4, held([P, K], F32, "result0"))
+        store_wk_gradient(1, 5, placed([P, K], F32, "result1", 55296))
+        store_wk_gradient(2, 0, placed([P, K], F32, "result2", 57344))
+        store_wk_gradient(3, 1, held([P, K], F32, "result3"))

@@ -97,11 +97,15 @@ def tile_attend_gmla_cW_kernel(tc, qT, G, cT, wk, ts, cf, offs, out_0, out_1):
         nc.scalar.dma_start(ts_window[P - 1 : P, :], ts[0:1, :])
 
         q_rows = qT.rearrange("(m t) r -> m t r", t=PACK)
-        q_raw = [held([P, 2, K], F32, "q_raw%d" % h) for h in range(2)]
-        nc.sync.dma_start(q_raw[0][:], q_rows[:, 0:2, :])
+        q01_raw = held([P, 2, K], F32, "q01_raw")
+        nc.sync.dma_start(q01_raw[:], q_rows[:, 0:2, :])
+        q_raw = [q01_raw[:, 0, :], q01_raw[:, 1, :]]
         offsets = keep.tile([P, K // 16], U16, name="offsets")
         nc.sync.dma_start(offsets[:], offs)
-        nc.sync.dma_start(q_raw[1][:], q_rows[:, 2:4, :])
+        for t in (2, 3):
+            raw = held([P, K], F32, "q%d_raw" % t)
+            nc.sync.dma_start(raw[:], q_rows[:, t, :])
+            q_raw.append(raw[:])
         g_rows = G.rearrange("(p j) i -> p j i", j=PACK)
         g_raw = []
         for h in range(2):
@@ -132,7 +136,7 @@ def tile_attend_gmla_cW_kernel(tc, qT, G, cT, wk, ts, cf, offs, out_0, out_1):
         q_bank = [bank_tile("q_bank%d" % h, 2 + h) for h in range(2)]
         for t in range(PACK):
             q_bf = held([P, K], BF16, "q%d_bf" % t)
-            cast_dealt((nc.scalar.copy, nc.vector.tensor_copy)[t // 2], q_bf[:], q_raw[t // 2][:, t % 2, :], 1)
+            cast_dealt(nc.vector.tensor_copy if t == PACK - 1 else nc.scalar.copy, q_bf[:], q_raw[t], 1)
             turn(q_bf[:], q_bank[t // 2], t % 2, True)
         q_grouped = [held([P, 2 * K], BF16, "q_grouped0"), placed([P, 2 * K], BF16, "q_grouped1", 28672)]
         for h in range(2):
@@ -143,7 +147,7 @@ def tile_attend_gmla_cW_kernel(tc, qT, G, cT, wk, ts, cf, offs, out_0, out_1):
 
         bank = bank_tile("ts_bank", 3)
         for r in range(PACK):
-            nc.tensor.transpose(bank[:, r * P : (r + 1) * P], ts_listed[:, r:K:PACK], identity[:])
+            nc.tensor.transpose(bank[:, r * P : (r + 1) * P], ts_listed[:, r * P : (r + 1) * P], identity[:])
         ts_columns = held([P, PACK], F32, "ts_columns")
         nc.scalar.copy(out=ts_columns[:], in_=bank[:, P - 1 : K : P])
 
@@ -155,22 +159,19 @@ def tile_attend_gmla_cW_kernel(tc, qT, G, cT, wk, ts, cf, offs, out_0, out_1):
 
         q_codes = held([P, K], U32, "q_codes")
         q_scales = held([P, K], U8, "q_scales")
-        g_grouped = placed([P, PACK * K], BF16, "g_grouped", 16384)
-        g_dealt = g_grouped[:].rearrange("p (a e h s t) -> p h a s t e", a=2, e=2, h=2, t=PACK)
+        g_grouped = [placed([P, 2 * K], BF16, "g_grouped0", 16384), held([P, 2 * K], BF16, "g_grouped1")]
+        g_codes = [held([P, 2 * P], U32, "g_codes0"), placed([P, 2 * P], U32, "g_codes1", 29696)]
+        g_scales = [held([P, 2 * P], U8, "g_scales%d" % h) for h in range(2)]
+        g_mx = [(g_codes[r // 2][:, r % 2 * P : (r % 2 + 1) * P], g_scales[r // 2][:, r % 2 * P : (r % 2 + 1) * P]) for r in range(PACK)]
         halves = [slice(0, K // 2), slice(K // 2, K)]
-        g_columns = [g_raw[h][:].rearrange("p t (s a e) -> p a s t e", a=2, e=2) for h in range(2)]
-        nc.vector.tensor_copy(out=g_dealt[:, 0], in_=g_columns[0])
+        interleave(nc.vector.tensor_copy, g_grouped[0][:], g_raw[0][:])
         quantize(q_grouped[0][:], E4M3, q_codes[:, halves[0]], q_scales[:, halves[0]])
-        nc.vector.tensor_copy(out=g_dealt[:, 1], in_=g_columns[1])
+        quantize(g_grouped[0][:], E5M2, g_codes[0][:], g_scales[0][:])
+        interleave(nc.vector.tensor_copy, g_grouped[1][:], g_raw[1][:])
         quantize(q_grouped[1][:], E4M3, q_codes[:, halves[1]], q_scales[:, halves[1]])
+        quantize(g_grouped[1][:], E5M2, g_codes[1][:], g_scales[1][:])
         q_mx = (q_codes[:], q_scales[:])
-        b = []
-        g_codes = placed([P, K], U32, "g_codes", 29696)
-        g_scales = held([P, K], U8, "g_scales")
-        for r in range(PACK):
-            g_mx = (g_codes[:, r * P : (r + 1) * P], g_scales[:, r * P : (r + 1) * P])
-            quantize(g_grouped[:, r * K : (r + 1) * K], E5M2, g_mx[0], g_mx[1])
-            b.append(product(bank_tile("b%d" % r, 4 + r), g_mx, E5M2, q_mx, E4M3))
+        b = [product(bank_tile("b%d" % r, 4 + r), g_mx[r], E5M2, q_mx, E4M3) for r in range(PACK)]
 
         w_bf = placed([P, PACK * K], BF16, "w_bf", 25088)
         for j in range(PACK):
@@ -182,7 +183,7 @@ def tile_attend_gmla_cW_kernel(tc, qT, G, cT, wk, ts, cf, offs, out_0, out_1):
 
         dk_planes = held([P, PACK * K], BF16, "dk_planes")
         planes = dk_planes[:].rearrange("p (r f) -> p r f", r=PACK)
-        dkf_grouped = []
+        dkf_grouped = held([P, PACK * K], BF16, "dkf_grouped")
         dkf_codes = held([P, K], U32, "dkf_codes")
         dkf_scales = held([P, K], U8, "dkf_scales")
 
@@ -193,16 +194,11 @@ def tile_attend_gmla_cW_kernel(tc, qT, G, cT, wk, ts, cf, offs, out_0, out_1):
                 )
             bank = bank_tile("dkf_bank%d" % r, 2 + r)
             turn(planes[:, r, :], bank, 0, True)
-            if r == PACK - 1:
-                dkf_grouped.append(placed([P, K], BF16, "dkf_grouped3", 6144))
-            else:
-                dkf_grouped.append(held([P, K], BF16, "dkf_grouped%d" % r))
-            unload(bank, 1, dkf_grouped[r][:])
+            unload(bank, 1, dkf_grouped[:, r * K : (r + 1) * K])
 
         def dkf_quantize(r):
-            for h in range(2):
-                cols = slice((h * PACK + r) * (P // 2), (h * PACK + r + 1) * (P // 2))
-                quantize(dkf_grouped[r][:, halves[h]], E5M2, dkf_codes[:, cols], dkf_scales[:, cols])
+            cols = slice(r * P, (r + 1) * P)
+            quantize(dkf_grouped[:, r * K : (r + 1) * K], E5M2, dkf_codes[:, cols], dkf_scales[:, cols])
 
         dk_plane(0)
         dk_plane(1)
@@ -212,20 +208,17 @@ def tile_attend_gmla_cW_kernel(tc, qT, G, cT, wk, ts, cf, offs, out_0, out_1):
         banks = bank_tile("w123_banks", 6, 2)
         for j in range(1, PACK):
             turn(w_bf[:, j * K : (j + 1) * K], banks, j, True)
-        w123_grouped = held([P, 3 * K], BF16, "w123_grouped")
-        unload(banks[:, K // 2 : K], 1, w123_grouped[:, 0:K])
-        unload(banks[:, K : 2 * K], 2, w123_grouped[:, K : 3 * K])
+        w1_grouped = held([P, K], BF16, "w1_grouped")
+        unload(banks[:, K // 2 : K], 1, w1_grouped[:])
+        w23_grouped = held([P, 2 * K], BF16, "w23_grouped")
+        unload(banks[:, K : 2 * K], 2, w23_grouped[:])
         dkf_quantize(1)
         w_mx = stationary("w0", w0_grouped[:], 1, 38400)
-        dki_first = held([P, K], BF16, "dki_first")
-        interleave(nc.vector.tensor_copy, dki_first[:], planes[:, :, 0:P])
         dkf_quantize(2)
         dkf_quantize(3)
-        w_mx = w_mx + stationary("w1", w123_grouped[:, 0:K], 1, None, 6656) + stationary("w23", w123_grouped[:, K : 3 * K], 2, None, 6400)
+        w_mx = w_mx + stationary("w1", w1_grouped[:], 1) + stationary("w23", w23_grouped[:], 2)
         dkf_mx = (dkf_codes[:], dkf_scales[:])
-        dc = [product(bank_tile("dc%d" % j, (0, 1, 6, 7)[j]), w_mx[j], E4M3, dkf_mx, E5M2) for j in range(PACK)]
-
-        c_listed = {}
+        dc = [product(bank_tile("dc%d" % j, j), w_mx[j], E4M3, dkf_mx, E5M2) for j in range(PACK)]
 
         def listed_on_vector(j, tile):
             c_listed[j] = tile
@@ -244,10 +237,8 @@ def tile_attend_gmla_cW_kernel(tc, qT, G, cT, wk, ts, cf, offs, out_0, out_1):
 
         def drain(j, tile, first=0, last=2):
             dc_sb[j] = tile
-            nc.scalar.copy(
-                out=tile[:].rearrange("p (h s r) -> p h s r", h=2, r=PACK)[:, first:last],
-                in_=dc[j].rearrange("p (h r s) -> p h s r", h=2, r=PACK)[:, first:last],
-            )
+            cols = slice(first * (K // 2), last * (K // 2))
+            nc.scalar.copy(out=tile[:, cols], in_=dc[j][:, cols])
 
         def scatter(j):
             window = windows[j % 2]
@@ -261,47 +252,53 @@ def tile_attend_gmla_cW_kernel(tc, qT, G, cT, wk, ts, cf, offs, out_0, out_1):
             )
             nc.scalar.dma_start(out_1[j * P : (j + 1) * P, :], result[:])
 
-        dki_parts = [dki_first, placed([P, K], BF16, "dki_second", 5376)]
-        interleave(nc.scalar.copy, dki_parts[1][:], planes[:, :, P : 2 * P])
-        listed_on_vector(0, placed([P, K], BF16, "c_listed0", 6912))
-        c0_bank = bank_tile("c0_bank", 2)
-        turn(c_listed[0][:], c0_bank, 0)
+        c_listed = {}
+        listed_on_vector(0, held([P, K], BF16, "c_listed0", tag="w1_grouped"))
+        dki_grouped = held([P, PACK * K], BF16, "dki_grouped")
+        dkf_words = dkf_grouped[:].bitcast(F32)
         drain(0, held([P, K], F32, "dc_sb0"))
         scatter(0)
-        c_bf = cast_on_scalar(2)
         drain(1, held([P, K], F32, "dc_sb1"))
         scatter(1)
-        listed_on_scalar(2, c_bf)
-        listed_on_vector(1, placed([P, K], BF16, "c_listed1", 37376))
-        dki_parts.append(placed([P, 2 * K], BF16, "dki_rest", 45056))
-        interleave(nc.scalar.copy, dki_parts[2][:], planes[:, :, 2 * P : K])
-        dki_codes = placed([P, K], U32, "dki_codes", 38400)
+        c_bf = cast_on_scalar(2)
+        listed_on_vector(1, placed([P, K], BF16, "c_listed1", 45056))
+        for u in range(2):
+            if u == 1:
+                listed_on_scalar(2, c_bf)
+            bank = bank_tile("dki_bank%d" % u, 6 + u)
+            for r in range(PACK):
+                nc.tensor.transpose(bank[:, r * P : (r + 1) * P], dkf_words[:, 2 * r + u : 2 * K : 2 * PACK], identity[:])
+            nc.scalar.copy(
+                out=dki_grouped[:, u * 2 * K : (u + 1) * 2 * K].rearrange("p (m r) -> p m r", r=PACK),
+                in_=bank.bitcast(BF16).rearrange("p (r m) -> p m r", r=PACK),
+            )
+        dki_codes = held([P, K], U32, "dki_codes")
         dki_scales = held([P, K], U8, "dki_scales")
-        for part, cols in zip(dki_parts, (slice(0, P), slice(P, 2 * P), slice(2 * P, K))):
-            quantize(part[:], E5M2, dki_codes[:, cols], dki_scales[:, cols])
+        quantize(dki_grouped[:], E5M2, dki_codes[:], dki_scales[:])
         dki_mx = (dki_codes[:], dki_scales[:])
-
-        c0_grouped = held([P, K], BF16, "c0_grouped")
-        unload(c0_bank, 1, c0_grouped[:])
+        bank = bank_tile("c0_bank", 4)
+        turn(c_listed[0][:], bank, 0)
+        c0_grouped = placed([P, K], BF16, "c0_grouped", 47104)
+        unload(bank, 1, c0_grouped[:])
         c_mx = stationary("c0", c0_grouped[:], 1)
-        drain(3, placed([P, K], F32, "dc_sb3", 51200), 0, 1)
-        c_bf = cast_on_scalar(3)
         drain(2, placed([P, K], F32, "dc_sb2", 49152))
         scatter(2)
+        c_bf = cast_on_scalar(3)
+        drain(3, placed([P, K], F32, "dc_sb3", 37376), 0, 1)
         listed_on_scalar(3, c_bf)
-        bank = bank_tile("c12_bank", 3)
+        bank = bank_tile("c12_bank", 6)
         for j in range(2):
             turn(c_listed[1 + j][:], bank, j)
         c12_grouped = held([P, 2 * K], BF16, "c12_grouped", tag="c_raw3")
         unload(bank, 2, c12_grouped[:])
         c_mx = c_mx + stationary("c12", c12_grouped[:], 2)
+        store_wk_gradient(0, 5, held([P, K], F32, "result0"))
         turn(c_listed[3][:], dc[3], 0)
         c3_grouped = placed([P, K], BF16, "c3_grouped", 56832)
         unload(dc[3], 1, c3_grouped[:])
         c_mx = c_mx + stationary("c3", c3_grouped[:], 1)
         drain(3, dc_sb[3], 1, 2)
         scatter(3)
-        store_wk_gradient(0, 4, held([P, K], F32, "result0"))
-        store_wk_gradient(1, 5, placed([P, K], F32, "result1", 55296))
+        store_wk_gradient(1, 7, placed([P, K], F32, "result1", 55296))
         store_wk_gradient(2, 0, placed([P, K], F32, "result2", 57344))
         store_wk_gradient(3, 1, held([P, K], F32, "result3"))

@@ -149,7 +149,7 @@ def tile_attend_gmla_cW_kernel(tc, qT, G, cT, wk, ts, cf, offs, out_0, out_1):
         for r in range(PACK):
             nc.tensor.transpose(bank[:, r * P : (r + 1) * P], ts_listed[:, r * P : (r + 1) * P], identity[:])
         ts_columns = held([P, PACK], F32, "ts_columns")
-        nc.scalar.copy(out=ts_columns[:], in_=bank[:, P - 1 : K : P])
+        nc.vector.tensor_copy(out=ts_columns[:], in_=bank[:, P - 1 : K : P])
 
         bank = bank_tile("cf_bank", 0)
         for t in range(PACK):
@@ -203,8 +203,10 @@ def tile_attend_gmla_cW_kernel(tc, qT, G, cT, wk, ts, cf, offs, out_0, out_1):
         dk_plane(0)
         dk_plane(1)
         dk_plane(2)
-        dkf_quantize(0)
         dk_plane(3)
+        c_listed = {0: held([P, K], BF16, "c_listed0", tag="g_codes0")}
+        nc.vector.tensor_copy(c_listed[0][:], c_raw[0][:].indirect(offsets[:]))
+        dkf_quantize(0)
         banks = bank_tile("w123_banks", 6, 2)
         for j in range(1, PACK):
             turn(w_bf[:, j * K : (j + 1) * K], banks, j, True)
@@ -252,16 +254,15 @@ def tile_attend_gmla_cW_kernel(tc, qT, G, cT, wk, ts, cf, offs, out_0, out_1):
             )
             nc.scalar.dma_start(out_1[j * P : (j + 1) * P, :], result[:])
 
-        c_listed = {}
-        listed_on_vector(0, held([P, K], BF16, "c_listed0", tag="w1_grouped"))
         dki_grouped = held([P, PACK * K], BF16, "dki_grouped")
         dkf_words = dkf_grouped[:].bitcast(F32)
+        listed_on_vector(1, held([P, K], BF16, "c_listed1", tag="w1_grouped"))
         drain(0, held([P, K], F32, "dc_sb0"))
         scatter(0)
         drain(1, held([P, K], F32, "dc_sb1"))
         scatter(1)
         c_bf = cast_on_scalar(2)
-        listed_on_vector(1, placed([P, K], BF16, "c_listed1", 45056))
+        listed_on_vector(3, placed([P, K], BF16, "c_listed3", 45056))
         for u in range(2):
             if u == 1:
                 listed_on_scalar(2, c_bf)
@@ -276,29 +277,18 @@ def tile_attend_gmla_cW_kernel(tc, qT, G, cT, wk, ts, cf, offs, out_0, out_1):
         dki_scales = held([P, K], U8, "dki_scales")
         quantize(dki_grouped[:], E5M2, dki_codes[:], dki_scales[:])
         dki_mx = (dki_codes[:], dki_scales[:])
-        bank = bank_tile("c0_bank", 4)
-        turn(c_listed[0][:], bank, 0)
-        c0_grouped = placed([P, K], BF16, "c0_grouped", 47104)
-        unload(bank, 1, c0_grouped[:])
-        c_mx = stationary("c0", c0_grouped[:], 1)
-        drain(2, placed([P, K], F32, "dc_sb2", 49152))
-        scatter(2)
-        c_bf = cast_on_scalar(3)
-        drain(3, placed([P, K], F32, "dc_sb3", 37376), 0, 1)
-        listed_on_scalar(3, c_bf)
-        bank = bank_tile("c12_bank", 6)
-        for j in range(2):
-            turn(c_listed[1 + j][:], bank, j)
-        c12_grouped = held([P, 2 * K], BF16, "c12_grouped", tag="c_raw3")
-        unload(bank, 2, c12_grouped[:])
-        c_mx = c_mx + stationary("c12", c12_grouped[:], 2)
-        store_wk_gradient(0, 5, held([P, K], F32, "result0"))
-        turn(c_listed[3][:], dc[3], 0)
-        c3_grouped = placed([P, K], BF16, "c3_grouped", 56832)
-        unload(dc[3], 1, c3_grouped[:])
-        c_mx = c_mx + stationary("c3", c3_grouped[:], 1)
-        drain(3, dc_sb[3], 1, 2)
-        scatter(3)
-        store_wk_gradient(1, 7, placed([P, K], F32, "result1", 55296))
-        store_wk_gradient(2, 0, placed([P, K], F32, "result2", 57344))
-        store_wk_gradient(3, 1, held([P, K], F32, "result3"))
+        c_mx = []
+        for h in range(2):
+            bank = bank_tile("c_bank%d" % h, 4 + h)
+            for j in range(2):
+                turn(c_listed[2 * h + j][:], bank, j)
+            grouped = placed([P, 2 * K], BF16, "c_grouped%d" % h, (47104, 36352)[h])
+            unload(bank, 2, grouped[:])
+            c_mx = c_mx + stationary("c%d" % h, grouped[:], 2)
+            drain(2 + h, placed([P, K], F32, "dc_sb%d" % (2 + h), (49152, 38400)[h]))
+            scatter(2 + h)
+            if h == 0:
+                for j in range(2):
+                    store_wk_gradient(j, j, held([P, K], F32, "result%d" % j))
+        for j in (2, 3):
+            store_wk_gradient(j, 4 + j, held([P, K], F32, "result%d" % j))

@@ -17,6 +17,7 @@ COPY = mybir.ActivationFunctionType.Copy
 P = 128
 PACK = 4
 K = P * PACK
+HALF = K // 2
 TOKENS = 2048
 BANK_BYTES = 2048
 FLOPS = 3 * 2 * K * K * K
@@ -29,48 +30,32 @@ def tile_attend_gmla_cW_kernel(tc, qT, G, cT, wk, ts, cf, offs, out_0, out_1):
         laid = ctx.enter_context(tc.tile_pool(name="laid", bufs=1))
         psum = ctx.enter_context(tc.psum_pool(name="psum", bufs=1))
 
-        def held(shape, dtype, name, tag=None):
-            return keep.tile(shape, dtype, name=name, tag=tag or name, align_bytes=64)
+        def held(shape, dtype, name):
+            return keep.tile(shape, dtype, name=name, align_bytes=64)
 
         def placed(shape, dtype, name, offset):
             return laid.tile(shape, dtype, name=name, align_bytes=64, offset=offset)
 
-        def bank_tile(name, number, count=1):
-            return psum.tile([P, count * K], F32, name=name, offset=number * BANK_BYTES)[:]
+        def bank_tile(name, number):
+            return psum.tile([P, K], F32, name=name, offset=number * BANK_BYTES)[:]
 
         def quantize(grouped, fmt, codes, scales):
             nc.vector.quantize_mx(out=codes.bitcast(fmt), scales=scales, in_=grouped)
 
-        def interleave(engine_copy, grouped, planes):
-            engine_copy(
-                out=grouped.rearrange("p (c i t) -> p c t i", i=4, t=PACK),
-                in_=planes.rearrange("p t (c i) -> p c t i", i=4),
-            )
-
-        def turn(rows, bank, place, dealt=False):
+        def turn(rows, bank, place):
             words = rows.bitcast(F32)
             for u in range(2):
                 first = (2 * place + u) * P
-                picked = words[:, u * P : (u + 1) * P] if dealt else words[:, u : K // 2 : 2]
-                nc.tensor.transpose(bank[:, first : first + P], picked, identity[:])
+                nc.tensor.transpose(bank[:, first : first + P], words[:, u : HALF : 2], identity[:])
 
-        def cast_dealt(engine_copy, rows, raw, count):
+        def unload(engine_copy, bank, count, grouped):
             engine_copy(
-                out=rows.rearrange("p (j u w e) -> p j u w e", j=count, u=2, e=2),
-                in_=raw.rearrange("p (j w u e) -> p j u w e", j=count, u=2, e=2),
-            )
-
-        def unload(bank, count, grouped):
-            nc.scalar.copy(
                 out=grouped.bitcast(F32).rearrange("p (j r u) -> p j r u", j=count, u=2),
                 in_=bank[:, 0 : count * 2 * P].rearrange("p (j u r) -> p j r u", j=count, u=2),
             )
 
-        def stationary(name, grouped, count, offset=None, scales_offset=None):
-            if offset is None:
-                codes = held([P, count * P], U32, name + "_codes")
-            else:
-                codes = placed([P, count * P], U32, name + "_codes", offset)
+        def stationary(name, grouped, count, scales_offset=None):
+            codes = held([P, count * P], U32, name + "_codes")
             if scales_offset is None:
                 scales = held([P, count * P], U8, name + "_scales")
             else:
@@ -78,39 +63,36 @@ def tile_attend_gmla_cW_kernel(tc, qT, G, cT, wk, ts, cf, offs, out_0, out_1):
             quantize(grouped, E4M3, codes[:], scales[:])
             return [(codes[:, j * P : (j + 1) * P], scales[:, j * P : (j + 1) * P]) for j in range(count)]
 
-        def product(bank, still, still_format, moving, moving_format):
+        def product(bank, still, moving):
             nc.tensor.matmul_mx(
                 out=bank,
-                lhsT=still[0].bitcast(still_format),
+                lhsT=still[0].bitcast(E4M3),
                 lhsT_scale=still[1],
-                rhs=moving[0].bitcast(moving_format),
+                rhs=moving[0].bitcast(E5M2),
                 rhs_scale=moving[1],
                 start=True,
                 stop=True,
             )
             return bank
 
-        cf_sb = held([P, PACK], F32, "cf_sb")
-        nc.scalar.dma_start(cf_sb[:], cf.rearrange("(p t) o -> p (t o)", t=PACK))
-        ts_window = placed([P, TOKENS], F32, "ts_window", 16384)
+        ts_window = placed([P, TOKENS], F32, "ts_window", 36864)
         nc.vector.memset(ts_window[0 : P - 1, :].bitcast(I32), 0)
         nc.scalar.dma_start(ts_window[P - 1 : P, :], ts[0:1, :])
-
-        q_rows = qT.rearrange("(m t) r -> m t r", t=PACK)
-        q01_raw = held([P, 2, K], F32, "q01_raw")
-        nc.sync.dma_start(q01_raw[:], q_rows[:, 0:2, :])
-        q_raw = [q01_raw[:, 0, :], q01_raw[:, 1, :]]
+        cf_sb = placed([P, PACK], F32, "cf_sb", 8192)
+        nc.scalar.dma_start(cf_sb[:], cf.rearrange("(p t) o -> p (t o)", t=PACK))
         offsets = keep.tile([P, K // 16], U16, name="offsets")
         nc.sync.dma_start(offsets[:], offs)
-        for t in (2, 3):
-            raw = held([P, K], F32, "q%d_raw" % t)
-            nc.sync.dma_start(raw[:], q_rows[:, t, :])
-            q_raw.append(raw[:])
+        q_rows = qT.rearrange("(m t) r -> m (t r)", t=PACK)
+        q_raw = []
+        for h in range(2):
+            raw = held([P, 2 * K], F32, "q_raw%d" % h)
+            nc.sync.dma_start(raw[:], q_rows[:, h * 2 * K : (h + 1) * 2 * K])
+            q_raw.append(raw)
         g_rows = G.rearrange("(p j) i -> p j i", j=PACK)
         g_raw = []
         for h in range(2):
-            raw = held([P, PACK, K // 2], F32, "g_raw%d" % h)
-            nc.sync.dma_start(raw[:], g_rows[:, :, h * (K // 2) : (h + 1) * (K // 2)])
+            raw = held([P, PACK, HALF], F32, "g_raw%d" % h)
+            nc.sync.dma_start(raw[:], g_rows[:, :, h * HALF : (h + 1) * HALF])
             g_raw.append(raw)
         wk_rows = wk.rearrange("(p j) f -> p (j f)", j=PACK)
         wk_raw = []
@@ -120,175 +102,188 @@ def tile_attend_gmla_cW_kernel(tc, qT, G, cT, wk, ts, cf, offs, out_0, out_1):
             wk_raw.append(raw)
         c_raw = []
         for j in range(PACK):
-            raw = placed([P, TOKENS], F32, "c_raw2", 45056) if j == 2 else held([P, TOKENS], F32, "c_raw%d" % j)
+            raw = held([P, TOKENS], F32, "c_raw%d" % j)
             nc.sync.dma_start(raw[:], cT[j * P : (j + 1) * P, :])
             c_raw.append(raw)
         out_0_rows = out_0.rearrange("(p j) n -> p j n", j=PACK)
 
         identity = held([P, P], F32, "identity")
         make_identity(nc, identity[:])
-        windows = [held([P, TOKENS], F32, "window%d" % w) for w in range(2)]
-        nc.vector.memset(windows[0][:].bitcast(I32), 0)
-        nc.vector.memset(windows[1][:].bitcast(I32), 0)
+        window_first = held([P, TOKENS], F32, "window_first")
+        nc.vector.memset(window_first[:].bitcast(I32), 0)
+
         ts_listed = held([P, K], F32, "ts_listed")
         nc.vector.tensor_copy(ts_listed[:], ts_window[:].indirect(offsets[:]))
-
-        q_bank = [bank_tile("q_bank%d" % h, 2 + h) for h in range(2)]
-        for t in range(PACK):
-            q_bf = held([P, K], BF16, "q%d_bf" % t)
-            cast_dealt(nc.vector.tensor_copy if t == PACK - 1 else nc.scalar.copy, q_bf[:], q_raw[t], 1)
-            turn(q_bf[:], q_bank[t // 2], t % 2, True)
-        q_grouped = [held([P, 2 * K], BF16, "q_grouped0"), placed([P, 2 * K], BF16, "q_grouped1", 28672)]
-        for h in range(2):
-            nc.scalar.copy(
-                out=q_grouped[h][:].bitcast(F32).rearrange("p (m e w) -> p m e w", e=2, w=2),
-                in_=q_bank[h].rearrange("p (e w m) -> p m e w", e=2, w=2),
-            )
-
-        bank = bank_tile("ts_bank", 3)
+        window_scalar = placed([P, TOKENS], F32, "window_scalar", 36864)
+        nc.vector.memset(window_scalar[:].bitcast(I32), 0)
+        bank = bank_tile("ts_bank", 2)
         for r in range(PACK):
             nc.tensor.transpose(bank[:, r * P : (r + 1) * P], ts_listed[:, r * P : (r + 1) * P], identity[:])
         ts_columns = held([P, PACK], F32, "ts_columns")
-        nc.vector.tensor_copy(out=ts_columns[:], in_=bank[:, P - 1 : K : P])
+        nc.scalar.copy(out=ts_columns[:], in_=bank[:, P - 1 : K : P])
 
-        bank = bank_tile("cf_bank", 0)
-        for t in range(PACK):
-            nc.tensor.transpose(bank[:, t * P : (t + 1) * P], cf_sb[:, t : t + 1].to_broadcast([P, P]), identity[:])
-        cf_spread = held([P, K], F32, "cf_spread")
-        nc.scalar.copy(out=cf_spread[:].rearrange("p (u m e) -> p u m e", u=2, e=2), in_=bank.rearrange("p (u e m) -> p u m e", u=2, e=2))
+        q_grouped = [placed([P, 2 * K], BF16, "q_grouped0", 0), held([P, 2 * K], BF16, "q_grouped1")]
+        for h in range(2):
+            q_bf = held([P, 2 * K], BF16, "q_bf%d" % h)
+            bank = bank_tile("q_bank%d" % h, h)
+            for j in range(2):
+                (nc.scalar.copy, nc.vector.tensor_copy)[h](out=q_bf[:, j * K : (j + 1) * K], in_=q_raw[h][:, j * K : (j + 1) * K])
+                turn(q_bf[:, j * K : (j + 1) * K], bank, j)
+            unload(nc.scalar.copy, bank, 2, q_grouped[h][:])
 
-        q_codes = held([P, K], U32, "q_codes")
-        q_scales = held([P, K], U8, "q_scales")
-        g_grouped = [placed([P, 2 * K], BF16, "g_grouped0", 16384), held([P, 2 * K], BF16, "g_grouped1")]
-        g_codes = [held([P, 2 * P], U32, "g_codes0"), placed([P, 2 * P], U32, "g_codes1", 29696)]
-        g_scales = [held([P, 2 * P], U8, "g_scales%d" % h) for h in range(2)]
-        g_mx = [(g_codes[r // 2][:, r % 2 * P : (r % 2 + 1) * P], g_scales[r // 2][:, r % 2 * P : (r % 2 + 1) * P]) for r in range(PACK)]
-        halves = [slice(0, K // 2), slice(K // 2, K)]
-        interleave(nc.vector.tensor_copy, g_grouped[0][:], g_raw[0][:])
-        quantize(q_grouped[0][:], E4M3, q_codes[:, halves[0]], q_scales[:, halves[0]])
-        quantize(g_grouped[0][:], E5M2, g_codes[0][:], g_scales[0][:])
-        interleave(nc.vector.tensor_copy, g_grouped[1][:], g_raw[1][:])
-        quantize(q_grouped[1][:], E4M3, q_codes[:, halves[1]], q_scales[:, halves[1]])
-        quantize(g_grouped[1][:], E5M2, g_codes[1][:], g_scales[1][:])
-        q_mx = (q_codes[:], q_scales[:])
-        b = [product(bank_tile("b%d" % r, 4 + r), g_mx[r], E5M2, q_mx, E4M3) for r in range(PACK)]
+        ts_spread = bank_tile("ts_spread", 0)
+        for r in range(PACK):
+            nc.tensor.transpose(ts_spread[:, r * P : (r + 1) * P], ts_columns[:, r : r + 1].to_broadcast([P, P]), identity[:])
+        factors = []
+        for h in range(2):
+            table = placed([P, PACK * HALF], F32, "factors%d" % h, 12288 + 4096 * h)
+            for t in range(PACK):
+                nc.scalar.activation(table[:, t * HALF : (t + 1) * HALF], ts_spread[:, h * HALF : (h + 1) * HALF], COPY, scale=cf_sb[:, t : t + 1])
+            factors.append(table)
 
-        w_bf = placed([P, PACK * K], BF16, "w_bf", 25088)
-        for j in range(PACK):
-            cast_dealt(nc.scalar.copy, w_bf[:, j * K : (j + 1) * K], wk_raw[j // 2][:, (j % 2) * K : (j % 2 + 1) * K], 1)
-        bank = bank_tile("w0_bank", 1)
-        turn(w_bf[:, 0:K], bank, 0, True)
-        w0_grouped = held([P, K], BF16, "w0_grouped")
-        unload(bank, 1, w0_grouped[:])
+        def g_interleave(h, grouped):
+            nc.vector.tensor_copy(
+                out=grouped[:].rearrange("p (c i t) -> p c t i", i=4, t=PACK),
+                in_=g_raw[h][:].rearrange("p t (c i) -> p c t i", i=4),
+            )
 
-        dk_planes = held([P, PACK * K], BF16, "dk_planes")
-        planes = dk_planes[:].rearrange("p (r f) -> p r f", r=PACK)
+        def g_quantize(h, grouped):
+            codes = held([P, HALF], U32, "g_codes%d" % h)
+            scales = held([P, HALF], U8, "g_scales%d" % h)
+            quantize(grouped[:], E5M2, codes[:], scales[:])
+            return [(codes[:, k * P : (k + 1) * P], scales[:, k * P : (k + 1) * P]) for k in range(2)]
+
+        def scores(k):
+            bank = bank_tile("b%d" % k, 4 + k)
+            for t in range(PACK):
+                product(bank[:, t * P : (t + 1) * P], q_mx[t], g_mx[k])
+            return bank
+
+        g_grouped0 = held([P, 2 * K], BF16, "g_grouped0")
+        g_interleave(0, g_grouped0)
+        q_mx = stationary("q01", q_grouped[0][:], 2)
+        g_mx = g_quantize(0, g_grouped0)
+        q_mx = q_mx + stationary("q23", q_grouped[1][:], 2)
+        b = [scores(0), scores(1)]
+        g_grouped1 = placed([P, 2 * K], BF16, "g_grouped1", 0)
+        g_interleave(1, g_grouped1)
+        g_mx = g_mx + g_quantize(1, g_grouped1)
+        b = b + [scores(2), scores(3)]
+
+        window_second = placed([P, TOKENS], F32, "window_second", 0)
+        nc.gpsimd.memset(window_second[:].bitcast(I32), 0)
+
         dkf_grouped = held([P, PACK * K], BF16, "dkf_grouped")
+        for k in range(PACK):
+            table = factors[k // 2][:].rearrange("p (t i) -> p t i", t=PACK)[:, :, k % 2 * P : (k % 2 + 1) * P]
+            nc.vector.tensor_tensor(
+                out=dkf_grouped[:, k * K : (k + 1) * K].rearrange("p (c i t) -> p c t i", i=4, t=PACK),
+                in0=b[k].rearrange("p (t c i) -> p c t i", t=PACK, i=4),
+                in1=table.rearrange("p t (c i) -> p c t i", i=4),
+                op=MULT,
+            )
         dkf_codes = held([P, K], U32, "dkf_codes")
         dkf_scales = held([P, K], U8, "dkf_scales")
-
-        def dk_plane(r):
-            for cols in halves if r == PACK - 1 else [slice(0, K)]:
-                nc.vector.scalar_tensor_tensor(
-                    out=planes[:, r, cols], in0=b[r][:, cols], scalar=ts_columns[:, r : r + 1], in1=cf_spread[:, cols], op0=MULT, op1=MULT
-                )
-            bank = bank_tile("dkf_bank%d" % r, 2 + r)
-            turn(planes[:, r, :], bank, 0, True)
-            unload(bank, 1, dkf_grouped[:, r * K : (r + 1) * K])
-
-        def dkf_quantize(r):
-            cols = slice(r * P, (r + 1) * P)
-            quantize(dkf_grouped[:, r * K : (r + 1) * K], E5M2, dkf_codes[:, cols], dkf_scales[:, cols])
-
-        dk_plane(0)
-        dk_plane(1)
-        dk_plane(2)
-        dk_plane(3)
-        c_listed = {0: held([P, K], BF16, "c_listed0", tag="g_codes0")}
-        nc.vector.tensor_copy(c_listed[0][:], c_raw[0][:].indirect(offsets[:]))
-        dkf_quantize(0)
-        banks = bank_tile("w123_banks", 6, 2)
-        for j in range(1, PACK):
-            turn(w_bf[:, j * K : (j + 1) * K], banks, j, True)
-        w1_grouped = held([P, K], BF16, "w1_grouped")
-        unload(banks[:, K // 2 : K], 1, w1_grouped[:])
-        w23_grouped = held([P, 2 * K], BF16, "w23_grouped")
-        unload(banks[:, K : 2 * K], 2, w23_grouped[:])
-        dkf_quantize(1)
-        w_mx = stationary("w0", w0_grouped[:], 1, 38400)
-        dkf_quantize(2)
-        dkf_quantize(3)
-        w_mx = w_mx + stationary("w1", w1_grouped[:], 1) + stationary("w23", w23_grouped[:], 2)
+        quantize(dkf_grouped[:], E5M2, dkf_codes[:], dkf_scales[:])
         dkf_mx = (dkf_codes[:], dkf_scales[:])
-        dc = [product(bank_tile("dc%d" % j, j), w_mx[j], E4M3, dkf_mx, E5M2) for j in range(PACK)]
 
-        def listed_on_vector(j, tile):
-            c_listed[j] = tile
-            nc.vector.tensor_copy(tile[:], c_raw[j][:].indirect(offsets[:]))
+        w_bf = placed([P, PACK * K], BF16, "w_bf", 8192)
+        w_grouped = [held([P, K], BF16, "w0_grouped")[:], placed([P, K], BF16, "w1_grouped", 45056)[:]]
+        w23_grouped = held([P, 2 * K], BF16, "w23_grouped")
+        w_grouped = w_grouped + [w23_grouped[:, 0:K], w23_grouped[:, K : 2 * K]]
+        w_banks = {}
 
-        def cast_on_scalar(j):
-            c_bf = placed([P, TOKENS], BF16, "c%d_bf" % j, {2: 36352, 3: 32768}[j])
-            nc.scalar.activation(c_bf[:], c_raw[j][:], COPY)
-            return c_bf
+        def w_cast(j):
+            nc.scalar.copy(out=w_bf[:, j * K : (j + 1) * K], in_=wk_raw[j // 2][:, j % 2 * K : (j % 2 + 1) * K])
+            w_banks[j] = bank_tile("w_bank%d" % j, 1 + j % 3)
+            turn(w_bf[:, j * K : (j + 1) * K], w_banks[j], 0)
 
-        def listed_on_scalar(j, c_bf):
-            c_listed[j] = held([P, K], BF16, "c_listed%d" % j)
-            nc.scalar.activation(c_listed[j][:], c_bf[:].indirect(offsets[:]), COPY)
+        def w_unload(j):
+            unload(nc.scalar.copy, w_banks[j], 1, w_grouped[j])
 
-        dc_sb = {}
+        w_cast(0)
+        w_cast(1)
+        w_unload(0)
+        w_mx = stationary("w0", w_grouped[0], 1, 16384)
+        dc = [product(bank_tile("dc0", 0), w_mx[0], dkf_mx)]
+        w_cast(2)
+        w_unload(1)
+        w_mx = w_mx + stationary("w1", w_grouped[1], 1, 16384 + P)
+        dc.append(product(bank_tile("dc1", 4), w_mx[1], dkf_mx))
+        window_last = placed([P, TOKENS], F32, "window_last", 45056)
+        nc.vector.memset(window_last[:].bitcast(I32), 0)
+        w_cast(3)
+        w_unload(2)
+        w_unload(3)
 
-        def drain(j, tile, first=0, last=2):
-            dc_sb[j] = tile
-            cols = slice(first * (K // 2), last * (K // 2))
-            nc.scalar.copy(out=tile[:, cols], in_=dc[j][:, cols])
+        dc_sb = [placed([P, K], F32, "dc_sb%d" % j, offset) for j, offset in enumerate((20480, 22528, 25600, 32768))]
 
-        def scatter(j):
-            window = windows[j % 2]
+        def scatter_on_vector(j, window):
             nc.vector.tensor_copy(window[:].indirect(offsets[:]), dc_sb[j][:])
             nc.sync.dma_start(out_0_rows[:, j, :], window[:])
 
-        def store_wk_gradient(j, number, result):
-            sums = product(bank_tile("sums%d" % j, number), c_mx[j], E4M3, dki_mx, E5M2)
-            nc.scalar.copy(
-                out=result[:].rearrange("p (m u e) -> p m u e", u=2, e=2), in_=sums.rearrange("p (u m e) -> p m u e", u=2, e=2)
-            )
-            nc.scalar.dma_start(out_1[j * P : (j + 1) * P, :], result[:])
+        def scatter_on_scalar(j, window):
+            for h in range(2):
+                nc.scalar.activation(
+                    window[:].indirect(offsets[:, h * HALF // 16 : (h + 1) * HALF // 16]), dc_sb[j][:, h * HALF : (h + 1) * HALF], COPY
+                )
+            nc.scalar.dma_start(out_0_rows[:, j, :], window[:])
 
-        dki_grouped = held([P, PACK * K], BF16, "dki_grouped")
+        nc.vector.tensor_copy(dc_sb[0][:], dc[0])
+        nc.scalar.copy(out=dc_sb[1][:], in_=dc[1])
+        w_mx = w_mx + stationary("w23", w23_grouped[:], 2, 16384 + 2 * P)
+        dc = dc + [product(bank_tile("dc%d" % j, 3 + j), w_mx[j], dkf_mx) for j in (2, 3)]
+        scatter_on_vector(0, window_first)
+        scatter_on_scalar(1, window_scalar)
+        nc.vector.tensor_copy(dc_sb[2][:], dc[2])
+        nc.scalar.copy(out=dc_sb[3][:], in_=dc[3])
+
+        c_listed = [placed([P, K], BF16, "c_listed%d" % j, offset) for j, offset in enumerate((20480, 25088, 27136, 33280))]
+
+        def listed_on_vector(j):
+            nc.vector.tensor_copy(c_listed[j][:], c_raw[j][:].indirect(offsets[:]))
+
+        listed_on_vector(0)
+        scatter_on_vector(2, window_second)
+        scatter_on_scalar(3, window_last)
+        listed_on_vector(1)
+        listed_on_vector(2)
+
+        dki_grouped = placed([P, PACK * K], BF16, "dki_grouped", 29184)
         dkf_words = dkf_grouped[:].bitcast(F32)
-        listed_on_vector(1, held([P, K], BF16, "c_listed1", tag="w1_grouped"))
-        drain(0, held([P, K], F32, "dc_sb0"))
-        scatter(0)
-        drain(1, held([P, K], F32, "dc_sb1"))
-        scatter(1)
-        c_bf = cast_on_scalar(2)
-        listed_on_vector(3, placed([P, K], BF16, "c_listed3", 45056))
         for u in range(2):
-            if u == 1:
-                listed_on_scalar(2, c_bf)
-            bank = bank_tile("dki_bank%d" % u, 6 + u)
+            bank = bank_tile("dki_bank%d" % u, 4 * u)
             for r in range(PACK):
                 nc.tensor.transpose(bank[:, r * P : (r + 1) * P], dkf_words[:, 2 * r + u : 2 * K : 2 * PACK], identity[:])
             nc.scalar.copy(
                 out=dki_grouped[:, u * 2 * K : (u + 1) * 2 * K].rearrange("p (m r) -> p m r", r=PACK),
                 in_=bank.bitcast(BF16).rearrange("p (r m) -> p m r", r=PACK),
             )
-        dki_codes = held([P, K], U32, "dki_codes")
-        dki_scales = held([P, K], U8, "dki_scales")
-        quantize(dki_grouped[:], E5M2, dki_codes[:], dki_scales[:])
-        dki_mx = (dki_codes[:], dki_scales[:])
-        c_mx = []
-        for h in range(2):
-            bank = bank_tile("c_bank%d" % h, 4 + h)
+        nc.scalar.activation(c_listed[3][:], c_raw[3][:].indirect(offsets[:]), COPY)
+
+        def c_turned(h, grouped):
+            bank = bank_tile("c_bank%d" % h, 2 + h)
             for j in range(2):
                 turn(c_listed[2 * h + j][:], bank, j)
-            grouped = placed([P, 2 * K], BF16, "c_grouped%d" % h, (47104, 36352)[h])
-            unload(bank, 2, grouped[:])
-            c_mx = c_mx + stationary("c%d" % h, grouped[:], 2)
-            drain(2 + h, placed([P, K], F32, "dc_sb%d" % (2 + h), (49152, 38400)[h]))
-            scatter(2 + h)
-            if h == 0:
-                for j in range(2):
-                    store_wk_gradient(j, j, held([P, K], F32, "result%d" % j))
-        for j in (2, 3):
-            store_wk_gradient(j, 4 + j, held([P, K], F32, "result%d" % j))
+            unload(nc.scalar.copy, bank, 2, grouped[:])
+
+        c01_grouped = placed([P, 2 * K], BF16, "c01_grouped", 34304)
+        c_turned(0, c01_grouped)
+        c23_grouped = held([P, 2 * K], BF16, "c23_grouped")
+        c_turned(1, c23_grouped)
+
+        dki_codes = held([P, K], U32, "dki_codes")
+        dki_scales = placed([P, K], U8, "dki_scales", 26112)
+        quantize(dki_grouped[:], E5M2, dki_codes[:], dki_scales[:])
+        dki_mx = (dki_codes[:], dki_scales[:])
+        c_mx = stationary("c01", c01_grouped[:], 2, 26624)
+        c_mx = c_mx + stationary("c23", c23_grouped[:], 2)
+
+        for j, number in enumerate((7, 1, 5, 6)):
+            sums = product(bank_tile("sums%d" % j, number), c_mx[j], dki_mx)
+            result = held([P, K], F32, "result%d" % j)
+            engine_copy = nc.scalar.copy if j % 2 == 0 else nc.vector.tensor_copy
+            engine_copy(
+                out=result[:].rearrange("p (m u e) -> p m u e", u=2, e=2), in_=sums.rearrange("p (u m e) -> p m u e", u=2, e=2)
+            )
+            nc.sync.dma_start(out_1[j * P : (j + 1) * P, :], result[:])

@@ -97,12 +97,12 @@ def tile_attend_gmla_cW_kernel(tc, qT, G, cT, wk, ts, cf, offs, out_0, out_1):
         wk_rows = wk.rearrange("(p j) f -> p (j f)", j=PACK)
         wk_raw = []
         for h in range(2):
-            raw = held([P, 2 * K], F32, "wk_raw%d" % h)
+            raw = placed([P, 2 * K], F32, "wk_raw1", 45056) if h else held([P, 2 * K], F32, "wk_raw0")
             nc.sync.dma_start(raw[:], wk_rows[:, h * 2 * K : (h + 1) * 2 * K])
             wk_raw.append(raw)
         c_raw = []
         for j in range(PACK):
-            raw = held([P, TOKENS], F32, "c_raw%d" % j)
+            raw = placed([P, TOKENS], F32, "c_raw1", 57344) if j == 1 else held([P, TOKENS], F32, "c_raw%d" % j)
             nc.sync.dma_start(raw[:], cT[j * P : (j + 1) * P, :])
             c_raw.append(raw)
         out_0_rows = out_0.rearrange("(p j) n -> p j n", j=PACK)
@@ -114,32 +114,40 @@ def tile_attend_gmla_cW_kernel(tc, qT, G, cT, wk, ts, cf, offs, out_0, out_1):
 
         ts_listed = held([P, K], F32, "ts_listed")
         nc.vector.tensor_copy(ts_listed[:], ts_window[:].indirect(offsets[:]))
+        ts_bank = bank_tile("ts_bank", 2)
+        for r in range(PACK):
+            nc.tensor.transpose(ts_bank[:, r * P : (r + 1) * P], ts_listed[:, r * P : (r + 1) * P], identity[:])
         window_scalar = placed([P, TOKENS], F32, "window_scalar", 36864)
         nc.vector.memset(window_scalar[:].bitcast(I32), 0)
-        bank = bank_tile("ts_bank", 2)
-        for r in range(PACK):
-            nc.tensor.transpose(bank[:, r * P : (r + 1) * P], ts_listed[:, r * P : (r + 1) * P], identity[:])
+
+        q_bf = [held([P, 2 * K], BF16, "q_bf%d" % h) for h in range(2)]
+        q_bank = [bank_tile("q_bank%d" % j, j) for j in range(2)]
+        q_grouped = [placed([P, 2 * K], BF16, "q_grouped0", 0), placed([P, 2 * K], BF16, "q_grouped1", 53248)]
+        for j in range(2):
+            nc.scalar.copy(out=q_bf[0][:, j * K : (j + 1) * K], in_=q_raw[0][:, j * K : (j + 1) * K])
+            turn(q_bf[0][:, j * K : (j + 1) * K], q_bank[j], 0)
         ts_columns = held([P, PACK], F32, "ts_columns")
-        nc.scalar.copy(out=ts_columns[:], in_=bank[:, P - 1 : K : P])
-
-        q_grouped = [placed([P, 2 * K], BF16, "q_grouped0", 0), held([P, 2 * K], BF16, "q_grouped1")]
-        for h in range(2):
-            q_bf = held([P, 2 * K], BF16, "q_bf%d" % h)
-            bank = bank_tile("q_bank%d" % h, h)
-            for j in range(2):
-                (nc.scalar.copy, nc.vector.tensor_copy)[h](out=q_bf[:, j * K : (j + 1) * K], in_=q_raw[h][:, j * K : (j + 1) * K])
-                turn(q_bf[:, j * K : (j + 1) * K], bank, j)
-            unload(nc.scalar.copy, bank, 2, q_grouped[h][:])
-
-        ts_spread = bank_tile("ts_spread", 0)
+        nc.scalar.copy(out=ts_columns[:], in_=ts_bank[:, P - 1 : K : P])
+        ts_spread = [q_bank[h][:, HALF:K] for h in range(2)]
         for r in range(PACK):
-            nc.tensor.transpose(ts_spread[:, r * P : (r + 1) * P], ts_columns[:, r : r + 1].to_broadcast([P, P]), identity[:])
-        factors = []
-        for h in range(2):
-            table = placed([P, PACK * HALF], F32, "factors%d" % h, 12288 + 4096 * h)
-            for t in range(PACK):
-                nc.scalar.activation(table[:, t * HALF : (t + 1) * HALF], ts_spread[:, h * HALF : (h + 1) * HALF], COPY, scale=cf_sb[:, t : t + 1])
-            factors.append(table)
+            nc.tensor.transpose(
+                ts_spread[r // 2][:, r % 2 * P : (r % 2 + 1) * P], ts_columns[:, r : r + 1].to_broadcast([P, P]), identity[:]
+            )
+        for j in range(2):
+            unload(nc.scalar.copy, q_bank[j], 1, q_grouped[0][:, j * K : (j + 1) * K])
+        nc.vector.tensor_copy(q_bf[1][:], q_raw[1][:])
+        bank = bank_tile("q23_bank", 3)
+        for j in range(2):
+            turn(q_bf[1][:, j * K : (j + 1) * K], bank, j)
+        factors = [placed([P, PACK * HALF], F32, "factors%d" % h, 12288 + 4096 * h) for h in range(2)]
+
+        def factor_rows(h, t):
+            nc.scalar.activation(factors[h][:, t * HALF : (t + 1) * HALF], ts_spread[h], COPY, scale=cf_sb[:, t : t + 1])
+
+        factor_rows(0, 0)
+        unload(nc.scalar.copy, bank, 2, q_grouped[1][:])
+        for n in range(1, 2 * PACK):
+            factor_rows(n // PACK, n % PACK)
 
         def g_interleave(h, grouped):
             nc.vector.tensor_copy(
@@ -147,9 +155,7 @@ def tile_attend_gmla_cW_kernel(tc, qT, G, cT, wk, ts, cf, offs, out_0, out_1):
                 in_=g_raw[h][:].rearrange("p t (c i) -> p c t i", i=4),
             )
 
-        def g_quantize(h, grouped):
-            codes = held([P, HALF], U32, "g_codes%d" % h)
-            scales = held([P, HALF], U8, "g_scales%d" % h)
+        def g_quantize(grouped, codes, scales):
             quantize(grouped[:], E5M2, codes[:], scales[:])
             return [(codes[:, k * P : (k + 1) * P], scales[:, k * P : (k + 1) * P]) for k in range(2)]
 
@@ -162,13 +168,14 @@ def tile_attend_gmla_cW_kernel(tc, qT, G, cT, wk, ts, cf, offs, out_0, out_1):
         g_grouped0 = held([P, 2 * K], BF16, "g_grouped0")
         g_interleave(0, g_grouped0)
         q_mx = stationary("q01", q_grouped[0][:], 2)
-        g_mx = g_quantize(0, g_grouped0)
-        q_mx = q_mx + stationary("q23", q_grouped[1][:], 2)
-        b = [scores(0), scores(1)]
+        g_mx = g_quantize(g_grouped0, held([P, HALF], U32, "g_codes0"), held([P, HALF], U8, "g_scales0"))
         g_grouped1 = placed([P, 2 * K], BF16, "g_grouped1", 0)
         g_interleave(1, g_grouped1)
-        g_mx = g_mx + g_quantize(1, g_grouped1)
-        b = b + [scores(2), scores(3)]
+        q_mx = q_mx + stationary("q23", q_grouped[1][:], 2)
+        g_mx = g_mx + g_quantize(g_grouped1, held([P, HALF], U32, "g_codes1"), placed([P, HALF], U8, "g_scales1", 53248))
+        w_bf = [placed([P, 2 * K], BF16, "w01_bf", 53248 + 512), placed([P, 2 * K], BF16, "w23_bf", 8192)]
+        nc.vector.tensor_copy(w_bf[0][:], wk_raw[0][:])
+        b = [scores(k) for k in range(PACK)]
 
         window_second = placed([P, TOKENS], F32, "window_second", 0)
         nc.gpsimd.memset(window_second[:].bitcast(I32), 0)
@@ -182,108 +189,117 @@ def tile_attend_gmla_cW_kernel(tc, qT, G, cT, wk, ts, cf, offs, out_0, out_1):
                 in1=table.rearrange("p t (c i) -> p c t i", i=4),
                 op=MULT,
             )
+
+        nc.scalar.copy(out=w_bf[1][:], in_=wk_raw[1][:])
+        w_grouped = [placed([P, 2 * K], BF16, "w01_grouped", 45056), placed([P, 2 * K], BF16, "w23_grouped", 69632)]
+        for h in range(2):
+            bank = bank_tile("w_bank%d" % h, 2 - 2 * h)
+            for j in range(2):
+                turn(w_bf[h][:, j * K : (j + 1) * K], bank, j)
+            unload(nc.scalar.copy, bank, 2, w_grouped[h][:])
         dkf_codes = held([P, K], U32, "dkf_codes")
         dkf_scales = held([P, K], U8, "dkf_scales")
         quantize(dkf_grouped[:], E5M2, dkf_codes[:], dkf_scales[:])
         dkf_mx = (dkf_codes[:], dkf_scales[:])
-
-        w_bf = placed([P, PACK * K], BF16, "w_bf", 8192)
-        w_grouped = [held([P, K], BF16, "w0_grouped")[:], placed([P, K], BF16, "w1_grouped", 45056)[:]]
-        w23_grouped = held([P, 2 * K], BF16, "w23_grouped")
-        w_grouped = w_grouped + [w23_grouped[:, 0:K], w23_grouped[:, K : 2 * K]]
-        w_banks = {}
-
-        def w_cast(j):
-            nc.scalar.copy(out=w_bf[:, j * K : (j + 1) * K], in_=wk_raw[j // 2][:, j % 2 * K : (j % 2 + 1) * K])
-            w_banks[j] = bank_tile("w_bank%d" % j, 1 + j % 3)
-            turn(w_bf[:, j * K : (j + 1) * K], w_banks[j], 0)
-
-        def w_unload(j):
-            unload(nc.scalar.copy, w_banks[j], 1, w_grouped[j])
-
-        w_cast(0)
-        w_cast(1)
-        w_unload(0)
-        w_mx = stationary("w0", w_grouped[0], 1, 16384)
-        dc = [product(bank_tile("dc0", 0), w_mx[0], dkf_mx)]
-        w_cast(2)
-        w_unload(1)
-        w_mx = w_mx + stationary("w1", w_grouped[1], 1, 16384 + P)
-        dc.append(product(bank_tile("dc1", 4), w_mx[1], dkf_mx))
+        w_mx = stationary("w01", w_grouped[0][:], 2, 16384) + stationary("w23", w_grouped[1][:], 2, 16384 + 2 * P)
+        dc = [product(bank_tile("dc%d" % j, number), w_mx[j], dkf_mx) for j, number in enumerate((0, 4, 5, 6))]
         window_last = placed([P, TOKENS], F32, "window_last", 45056)
         nc.vector.memset(window_last[:].bitcast(I32), 0)
-        w_cast(3)
-        w_unload(2)
-        w_unload(3)
 
-        dc_sb = [placed([P, K], F32, "dc_sb%d" % j, offset) for j, offset in enumerate((20480, 22528, 25600, 32768))]
+        dc_sb = {j: placed([P, K], F32, "dc_sb%d" % j, offset) for j, offset in ((0, 20480), (2, 25600))}
+        dc_halves = {j: [placed([P, HALF], F32, "dc_sb%d_%d" % (j, h), offset + 1024 * h) for h in range(2)] for j, offset in ((1, 22528), (3, 32768))}
+
+        def store_window(j, window):
+            nc.sync.dma_start(out_0_rows[:, j, :], window[:])
 
         def scatter_on_vector(j, window):
             nc.vector.tensor_copy(window[:].indirect(offsets[:]), dc_sb[j][:])
-            nc.sync.dma_start(out_0_rows[:, j, :], window[:])
+            store_window(j, window)
 
-        def scatter_on_scalar(j, window):
-            for h in range(2):
-                nc.scalar.activation(
-                    window[:].indirect(offsets[:, h * HALF // 16 : (h + 1) * HALF // 16]), dc_sb[j][:, h * HALF : (h + 1) * HALF], COPY
-                )
-            nc.scalar.dma_start(out_0_rows[:, j, :], window[:])
+        def scatter_on_scalar(window, h, values):
+            nc.scalar.activation(window[:].indirect(offsets[:, h * HALF // 16 : (h + 1) * HALF // 16]), values, COPY)
 
-        nc.vector.tensor_copy(dc_sb[0][:], dc[0])
-        nc.scalar.copy(out=dc_sb[1][:], in_=dc[1])
-        w_mx = w_mx + stationary("w23", w23_grouped[:], 2, 16384 + 2 * P)
-        dc = dc + [product(bank_tile("dc%d" % j, 3 + j), w_mx[j], dkf_mx) for j in (2, 3)]
-        scatter_on_vector(0, window_first)
-        scatter_on_scalar(1, window_scalar)
-        nc.vector.tensor_copy(dc_sb[2][:], dc[2])
-        nc.scalar.copy(out=dc_sb[3][:], in_=dc[3])
-
-        c_listed = [placed([P, K], BF16, "c_listed%d" % j, offset) for j, offset in enumerate((20480, 25088, 27136, 33280))]
-
-        def listed_on_vector(j):
-            nc.vector.tensor_copy(c_listed[j][:], c_raw[j][:].indirect(offsets[:]))
-
-        listed_on_vector(0)
-        scatter_on_vector(2, window_second)
-        scatter_on_scalar(3, window_last)
-        listed_on_vector(1)
-        listed_on_vector(2)
-
-        dki_grouped = placed([P, PACK * K], BF16, "dki_grouped", 29184)
+        dki_grouped = held([P, PACK * K], BF16, "dki_grouped")
         dkf_words = dkf_grouped[:].bitcast(F32)
-        for u in range(2):
+
+        def dki_turn(u):
             bank = bank_tile("dki_bank%d" % u, 4 * u)
             for r in range(PACK):
                 nc.tensor.transpose(bank[:, r * P : (r + 1) * P], dkf_words[:, 2 * r + u : 2 * K : 2 * PACK], identity[:])
+            return bank
+
+        def dki_unload(u, bank):
             nc.scalar.copy(
                 out=dki_grouped[:, u * 2 * K : (u + 1) * 2 * K].rearrange("p (m r) -> p m r", r=PACK),
                 in_=bank.bitcast(BF16).rearrange("p (r m) -> p m r", r=PACK),
             )
-        nc.scalar.activation(c_listed[3][:], c_raw[3][:].indirect(offsets[:]), COPY)
 
-        def c_turned(h, grouped):
-            bank = bank_tile("c_bank%d" % h, 2 + h)
-            for j in range(2):
-                turn(c_listed[2 * h + j][:], bank, j)
-            unload(nc.scalar.copy, bank, 2, grouped[:])
+        def listed_on_vector(j, offset):
+            c_listed[j] = placed([P, K], BF16, "c_listed%d" % j, offset)
+            nc.vector.tensor_copy(c_listed[j][:], c_raw[j][:].indirect(offsets[:]))
 
-        c01_grouped = placed([P, 2 * K], BF16, "c01_grouped", 34304)
-        c_turned(0, c01_grouped)
-        c23_grouped = held([P, 2 * K], BF16, "c23_grouped")
-        c_turned(1, c23_grouped)
+        def drain_halves(j):
+            for h in range(2):
+                nc.scalar.copy(out=dc_halves[j][h][:], in_=dc[j][:, h * HALF : (h + 1) * HALF])
+
+        def c_turn(j, bank, place):
+            turn(c_listed[j][:], bank, place)
+
+        c_listed = {0: placed([P, K], BF16, "c_listed0", 69632)}
+        nc.scalar.activation(c_listed[0][:], c_raw[0][:].indirect(offsets[:]), COPY)
+        nc.vector.tensor_copy(dc_sb[0][:], dc[0])
+        drain_halves(1)
+        scatter_on_vector(0, window_first)
+        scatter_on_scalar(window_scalar, 0, dc_halves[1][0][:])
+        dki_unload(0, dki_turn(0))
+        scatter_on_scalar(window_scalar, 1, dc_halves[1][1][:])
+        store_window(1, window_scalar)
+        nc.vector.tensor_copy(dc_sb[2][:], dc[2])
+        drain_halves(3)
+        dki_bank = dki_turn(1)
+        listed_on_vector(1, 20480)
+        scatter_on_vector(2, window_last)
+        scatter_on_scalar(window_second, 0, dc_halves[3][0][:])
+        dki_unload(1, dki_bank)
+        scatter_on_scalar(window_second, 1, dc_halves[3][1][:])
+        store_window(3, window_second)
+        bank = bank_tile("c01_bank", 2)
+        for j in range(2):
+            c_turn(j, bank, j)
+        c01_grouped = placed([P, 2 * K], BF16, "c01_grouped", 31232)
+        unload(nc.scalar.copy, bank, 2, c01_grouped[:])
+        listed_on_vector(2, 57344)
 
         dki_codes = held([P, K], U32, "dki_codes")
         dki_scales = placed([P, K], U8, "dki_scales", 26112)
         quantize(dki_grouped[:], E5M2, dki_codes[:], dki_scales[:])
         dki_mx = (dki_codes[:], dki_scales[:])
         c_mx = stationary("c01", c01_grouped[:], 2, 26624)
-        c_mx = c_mx + stationary("c23", c23_grouped[:], 2)
+        listed_on_vector(3, 27136)
 
-        for j, number in enumerate((7, 1, 5, 6)):
-            sums = product(bank_tile("sums%d" % j, number), c_mx[j], dki_mx)
-            result = held([P, K], F32, "result%d" % j)
-            engine_copy = nc.scalar.copy if j % 2 == 0 else nc.vector.tensor_copy
+        def wk_gradient(j, number):
+            return product(bank_tile("sums%d" % j, number), c_mx[j], dki_mx)
+
+        def store_wk_gradient(j, sums, engine_copy, result):
             engine_copy(
                 out=result[:].rearrange("p (m u e) -> p m u e", u=2, e=2), in_=sums.rearrange("p (u m e) -> p m u e", u=2, e=2)
             )
             nc.sync.dma_start(out_1[j * P : (j + 1) * P, :], result[:])
+
+        bank = bank_tile("c2_bank", 3)
+        c_turn(2, bank, 0)
+        c2_grouped = placed([P, K], BF16, "c2_grouped", 33792)
+        unload(nc.scalar.copy, bank, 1, c2_grouped[:])
+        sums = [wk_gradient(0, 7), wk_gradient(1, 1)]
+        c_mx = c_mx + stationary("c2", c2_grouped[:], 1)
+        bank = bank_tile("c3_bank", 0)
+        c_turn(3, bank, 0)
+        sums.append(wk_gradient(2, 5))
+        for j in range(2):
+            store_wk_gradient(j, sums[j], nc.scalar.copy, held([P, K], F32, "result%d" % j))
+        c3_grouped = held([P, K], BF16, "c3_grouped")
+        unload(nc.vector.tensor_copy, bank, 1, c3_grouped[:])
+        c_mx = c_mx + stationary("c3", c3_grouped[:], 1)
+        sums.append(wk_gradient(3, 6))
+        store_wk_gradient(2, sums[2], nc.vector.tensor_copy, held([P, K], F32, "result2"))
+        store_wk_gradient(3, sums[3], nc.scalar.copy, held([P, K], F32, "result3"))

@@ -36,8 +36,8 @@ def tile_attend_gmla_cW_kernel(tc, qT, G, cT, wk, ts, cf, offs, out_0, out_1):
         def placed(shape, dtype, name, offset):
             return laid.tile(shape, dtype, name=name, align_bytes=64, offset=offset)
 
-        def bank_tile(name, number):
-            return psum.tile([P, K], F32, name=name, offset=number * BANK_BYTES)[:]
+        def bank_tile(name, number, count=1):
+            return psum.tile([P, count * K], F32, name=name, offset=number * BANK_BYTES)[:]
 
         def quantize(grouped, fmt, codes, scales):
             nc.vector.quantize_mx(out=codes.bitcast(fmt), scales=scales, in_=grouped)
@@ -75,19 +75,23 @@ def tile_attend_gmla_cW_kernel(tc, qT, G, cT, wk, ts, cf, offs, out_0, out_1):
             )
             return bank
 
-        ts_window = placed([P, TOKENS], F32, "ts_window", 36864)
+        warm = held([P, 16], F32, "warm")
+        nc.gpsimd.memset(warm[:, 0:8], 0.0)
+        identity = held([P, P], F32, "identity")
+        make_identity(nc, identity[:])
+
+        ts_window = held([P, TOKENS], F32, "ts_window")
         nc.vector.memset(ts_window[0 : P - 1, :].bitcast(I32), 0)
-        nc.scalar.dma_start(ts_window[P - 1 : P, :], ts[0:1, :])
-        cf_sb = placed([P, PACK], F32, "cf_sb", 8192)
+        nc.sync.dma_start(ts_window[P - 1 : P, :], ts[0:1, :])
+        cf_sb = held([P, PACK], F32, "cf_sb")
         nc.scalar.dma_start(cf_sb[:], cf.rearrange("(p t) o -> p (t o)", t=PACK))
+        nc.scalar.activation(warm[:, 8:16], warm[:, 0:8], COPY)
         offsets = keep.tile([P, K // 16], U16, name="offsets")
-        nc.sync.dma_start(offsets[:], offs)
         q_rows = qT.rearrange("(m t) r -> m (t r)", t=PACK)
-        q_raw = []
-        for h in range(2):
-            raw = held([P, 2 * K], F32, "q_raw%d" % h)
-            nc.sync.dma_start(raw[:], q_rows[:, h * 2 * K : (h + 1) * 2 * K])
-            q_raw.append(raw)
+        q_raw = [placed([P, 2 * K], F32, "q_raw0", 49152), held([P, 2 * K], F32, "q_raw1")]
+        nc.sync.dma_start(offsets[:], offs)
+        nc.sync.dma_start(q_raw[0][:], q_rows[:, 0 : 2 * K])
+        nc.sync.dma_start(q_raw[1][:], q_rows[:, 2 * K : 4 * K])
         g_rows = G.rearrange("(p j) i -> p j i", j=PACK)
         g_raw = []
         for h in range(2):
@@ -97,56 +101,54 @@ def tile_attend_gmla_cW_kernel(tc, qT, G, cT, wk, ts, cf, offs, out_0, out_1):
         wk_rows = wk.rearrange("(p j) f -> p (j f)", j=PACK)
         wk_raw = []
         for h in range(2):
-            raw = placed([P, 2 * K], F32, "wk_raw1", 45056) if h else held([P, 2 * K], F32, "wk_raw0")
+            raw = held([P, 2 * K], F32, "wk_raw%d" % h)
             nc.sync.dma_start(raw[:], wk_rows[:, h * 2 * K : (h + 1) * 2 * K])
             wk_raw.append(raw)
         c_raw = []
         for j in range(PACK):
-            raw = placed([P, TOKENS], F32, "c_raw1", 57344) if j == 1 else held([P, TOKENS], F32, "c_raw%d" % j)
+            raw = placed([P, TOKENS], F32, "c_raw3", 65536) if j == 3 else held([P, TOKENS], F32, "c_raw%d" % j)
             nc.sync.dma_start(raw[:], cT[j * P : (j + 1) * P, :])
             c_raw.append(raw)
         out_0_rows = out_0.rearrange("(p j) n -> p j n", j=PACK)
 
-        identity = held([P, P], F32, "identity")
-        make_identity(nc, identity[:])
-        window_first = held([P, TOKENS], F32, "window_first")
-        nc.vector.memset(window_first[:].bitcast(I32), 0)
+        windows = {j: held([P, TOKENS], F32, "window%d" % j) for j in range(2)}
+        for j in range(2):
+            nc.vector.memset(windows[j][:].bitcast(I32), 0)
 
         ts_listed = held([P, K], F32, "ts_listed")
-        nc.vector.tensor_copy(ts_listed[:], ts_window[:].indirect(offsets[:]))
+        nc.scalar.activation(ts_listed[:], ts_window[:].indirect(offsets[:]), COPY)
         ts_bank = bank_tile("ts_bank", 2)
         for r in range(PACK):
             nc.tensor.transpose(ts_bank[:, r * P : (r + 1) * P], ts_listed[:, r * P : (r + 1) * P], identity[:])
-        window_scalar = placed([P, TOKENS], F32, "window_scalar", 36864)
-        nc.vector.memset(window_scalar[:].bitcast(I32), 0)
 
         q_bf = [held([P, 2 * K], BF16, "q_bf%d" % h) for h in range(2)]
-        q_bank = [bank_tile("q_bank%d" % j, j) for j in range(2)]
-        q_grouped = [placed([P, 2 * K], BF16, "q_grouped0", 0), placed([P, 2 * K], BF16, "q_grouped1", 53248)]
+        q_bank = [bank_tile("q_bank0", 0), bank_tile("q_bank1", 3)]
+        q_grouped = [placed([P, 2 * K], BF16, "q_grouped0", 8192), placed([P, 2 * K], BF16, "q_grouped1", 16384)]
+        nc.vector.tensor_copy(q_bf[0][:], q_raw[0][:])
         for j in range(2):
-            nc.scalar.copy(out=q_bf[0][:, j * K : (j + 1) * K], in_=q_raw[0][:, j * K : (j + 1) * K])
-            turn(q_bf[0][:, j * K : (j + 1) * K], q_bank[j], 0)
+            turn(q_bf[0][:, j * K : (j + 1) * K], q_bank[0], j)
         ts_columns = held([P, PACK], F32, "ts_columns")
         nc.scalar.copy(out=ts_columns[:], in_=ts_bank[:, P - 1 : K : P])
-        ts_spread = [q_bank[h][:, HALF:K] for h in range(2)]
+        spread_bank = bank_tile("ts_spread", 1)
+        ts_spread = [spread_bank[:, h * HALF : (h + 1) * HALF] for h in range(2)]
         for r in range(PACK):
-            nc.tensor.transpose(
-                ts_spread[r // 2][:, r % 2 * P : (r % 2 + 1) * P], ts_columns[:, r : r + 1].to_broadcast([P, P]), identity[:]
-            )
-        for j in range(2):
-            unload(nc.scalar.copy, q_bank[j], 1, q_grouped[0][:, j * K : (j + 1) * K])
+            nc.tensor.transpose(spread_bank[:, r * P : (r + 1) * P], ts_columns[:, r : r + 1].to_broadcast([P, P]), identity[:])
+        unload(nc.scalar.copy, q_bank[0], 2, q_grouped[0][:])
         nc.vector.tensor_copy(q_bf[1][:], q_raw[1][:])
-        bank = bank_tile("q23_bank", 3)
+        windows[2] = placed([P, TOKENS], F32, "window2", 49152)
+        nc.vector.memset(windows[2][:].bitcast(I32), 0)
+        bank = q_bank[1]
         for j in range(2):
             turn(q_bf[1][:, j * K : (j + 1) * K], bank, j)
-        factors = [placed([P, PACK * HALF], F32, "factors%d" % h, 12288 + 4096 * h) for h in range(2)]
+        factors = [held([P, PACK * HALF], F32, "factors0"), placed([P, PACK * HALF], F32, "factors1", 57344)]
 
         def factor_rows(h, t):
             nc.scalar.activation(factors[h][:, t * HALF : (t + 1) * HALF], ts_spread[h], COPY, scale=cf_sb[:, t : t + 1])
 
         factor_rows(0, 0)
+        factor_rows(0, 1)
         unload(nc.scalar.copy, bank, 2, q_grouped[1][:])
-        for n in range(1, 2 * PACK):
+        for n in range(2, 2 * PACK):
             factor_rows(n // PACK, n % PACK)
 
         def g_interleave(h, grouped):
@@ -155,7 +157,9 @@ def tile_attend_gmla_cW_kernel(tc, qT, G, cT, wk, ts, cf, offs, out_0, out_1):
                 in_=g_raw[h][:].rearrange("p t (c i) -> p c t i", i=4),
             )
 
-        def g_quantize(grouped, codes, scales):
+        def g_quantize(h, grouped):
+            codes = held([P, HALF], U32, "g_codes%d" % h)
+            scales = held([P, HALF], U8, "g_scales%d" % h)
             quantize(grouped[:], E5M2, codes[:], scales[:])
             return [(codes[:, k * P : (k + 1) * P], scales[:, k * P : (k + 1) * P]) for k in range(2)]
 
@@ -165,22 +169,22 @@ def tile_attend_gmla_cW_kernel(tc, qT, G, cT, wk, ts, cf, offs, out_0, out_1):
                 product(bank[:, t * P : (t + 1) * P], q_mx[t], g_mx[k])
             return bank
 
-        g_grouped0 = held([P, 2 * K], BF16, "g_grouped0")
+        g_grouped0 = placed([P, 2 * K], BF16, "g_grouped0", 22528)
         g_interleave(0, g_grouped0)
         q_mx = stationary("q01", q_grouped[0][:], 2)
-        g_mx = g_quantize(g_grouped0, held([P, HALF], U32, "g_codes0"), held([P, HALF], U8, "g_scales0"))
-        g_grouped1 = placed([P, 2 * K], BF16, "g_grouped1", 0)
+        g_mx = g_quantize(0, g_grouped0)
+        g_grouped1 = placed([P, 2 * K], BF16, "g_grouped1", 8192)
         g_interleave(1, g_grouped1)
         q_mx = q_mx + stationary("q23", q_grouped[1][:], 2)
-        g_mx = g_mx + g_quantize(g_grouped1, held([P, HALF], U32, "g_codes1"), placed([P, HALF], U8, "g_scales1", 53248))
-        w_bf = [placed([P, 2 * K], BF16, "w01_bf", 53248 + 512), placed([P, 2 * K], BF16, "w23_bf", 8192)]
+        g_mx = g_mx + g_quantize(1, g_grouped1)
+        w_bf = [placed([P, 2 * K], BF16, "w01_bf", 16384 - 1984), placed([P, 2 * K], BF16, "w23_bf", 16384 + 64)]
         nc.vector.tensor_copy(w_bf[0][:], wk_raw[0][:])
         b = [scores(k) for k in range(PACK)]
 
-        window_second = placed([P, TOKENS], F32, "window_second", 0)
-        nc.gpsimd.memset(window_second[:].bitcast(I32), 0)
+        windows[3] = placed([P, TOKENS], F32, "window3", 2048)
+        nc.gpsimd.memset(windows[3][:].bitcast(I32), 0)
 
-        dkf_grouped = held([P, PACK * K], BF16, "dkf_grouped")
+        dkf_grouped = placed([P, PACK * K], BF16, "dkf_grouped", 36864)
         for k in range(PACK):
             table = factors[k // 2][:].rearrange("p (t i) -> p t i", t=PACK)[:, :, k % 2 * P : (k % 2 + 1) * P]
             nc.vector.tensor_tensor(
@@ -191,39 +195,17 @@ def tile_attend_gmla_cW_kernel(tc, qT, G, cT, wk, ts, cf, offs, out_0, out_1):
             )
 
         nc.scalar.copy(out=w_bf[1][:], in_=wk_raw[1][:])
-        w_grouped = [placed([P, 2 * K], BF16, "w01_grouped", 45056), placed([P, 2 * K], BF16, "w23_grouped", 69632)]
+        w_grouped = [held([P, 2 * K], BF16, "w01_grouped"), held([P, 2 * K], BF16, "w23_grouped")]
         for h in range(2):
-            bank = bank_tile("w_bank%d" % h, 2 - 2 * h)
+            bank = bank_tile("w_bank%d" % h, 2 + h)
             for j in range(2):
                 turn(w_bf[h][:, j * K : (j + 1) * K], bank, j)
             unload(nc.scalar.copy, bank, 2, w_grouped[h][:])
-        dkf_codes = held([P, K], U32, "dkf_codes")
-        dkf_scales = held([P, K], U8, "dkf_scales")
-        quantize(dkf_grouped[:], E5M2, dkf_codes[:], dkf_scales[:])
-        dkf_mx = (dkf_codes[:], dkf_scales[:])
-        w_mx = stationary("w01", w_grouped[0][:], 2, 16384) + stationary("w23", w_grouped[1][:], 2, 16384 + 2 * P)
-        dc = [product(bank_tile("dc%d" % j, number), w_mx[j], dkf_mx) for j, number in enumerate((0, 4, 5, 6))]
-        window_last = placed([P, TOKENS], F32, "window_last", 45056)
-        nc.vector.memset(window_last[:].bitcast(I32), 0)
-
-        dc_sb = {j: placed([P, K], F32, "dc_sb%d" % j, offset) for j, offset in ((0, 20480), (2, 25600))}
-        dc_halves = {j: [placed([P, HALF], F32, "dc_sb%d_%d" % (j, h), offset + 1024 * h) for h in range(2)] for j, offset in ((1, 22528), (3, 32768))}
-
-        def store_window(j, window):
-            nc.sync.dma_start(out_0_rows[:, j, :], window[:])
-
-        def scatter_on_vector(j, window):
-            nc.vector.tensor_copy(window[:].indirect(offsets[:]), dc_sb[j][:])
-            store_window(j, window)
-
-        def scatter_on_scalar(window, h, values):
-            nc.scalar.activation(window[:].indirect(offsets[:, h * HALF // 16 : (h + 1) * HALF // 16]), values, COPY)
-
         dki_grouped = held([P, PACK * K], BF16, "dki_grouped")
         dkf_words = dkf_grouped[:].bitcast(F32)
 
-        def dki_turn(u):
-            bank = bank_tile("dki_bank%d" % u, 4 * u)
+        def dki_turn(u, number):
+            bank = bank_tile("dki_bank%d" % u, number)
             for r in range(PACK):
                 nc.tensor.transpose(bank[:, r * P : (r + 1) * P], dkf_words[:, 2 * r + u : 2 * K : 2 * PACK], identity[:])
             return bank
@@ -234,72 +216,119 @@ def tile_attend_gmla_cW_kernel(tc, qT, G, cT, wk, ts, cf, offs, out_0, out_1):
                 in_=bank.bitcast(BF16).rearrange("p (r m) -> p m r", r=PACK),
             )
 
-        def listed_on_vector(j, offset):
-            c_listed[j] = placed([P, K], BF16, "c_listed%d" % j, offset)
-            nc.vector.tensor_copy(c_listed[j][:], c_raw[j][:].indirect(offsets[:]))
+        dki_unload(0, dki_turn(0, 0))
+        dkf_codes = held([P, K], U32, "dkf_codes")
+        dkf_scales = held([P, K], U8, "dkf_scales")
+        for h in range(2):
+            cols = slice(h * HALF, (h + 1) * HALF)
+            quantize(dkf_grouped[:, h * 2 * K : (h + 1) * 2 * K], E5M2, dkf_codes[:, cols], dkf_scales[:, cols])
+        dkf_mx = (dkf_codes[:], dkf_scales[:])
+        w_mx = stationary("w01", w_grouped[0][:], 2, 57344)
+        dc = {0: product(bank_tile("dc0", 4), w_mx[0], dkf_mx)}
+        dc_halves = {}
+        for h in range(2):
+            cols = slice(h * HALF, (h + 1) * HALF)
+            dc_halves[1, h] = product(bank_tile("dc1_%d" % h, 5 + h)[:, 0:HALF], w_mx[1], (dkf_codes[:, cols], dkf_scales[:, cols]))
 
-        def drain_halves(j):
-            for h in range(2):
-                nc.scalar.copy(out=dc_halves[j][h][:], in_=dc[j][:, h * HALF : (h + 1) * HALF])
+        c_listed = {}
 
-        def c_turn(j, bank, place):
+        def listed(j, engine, tile):
+            c_listed[j] = tile
+            if engine == "vector":
+                nc.vector.tensor_copy(tile[:], c_raw[j][:].indirect(offsets[:]))
+            else:
+                nc.scalar.activation(tile[:], c_raw[j][:].indirect(offsets[:]), COPY)
+
+        def store_window(j):
+            nc.sync.dma_start(out_0_rows[:, j, :], windows[j][:])
+
+        def drain_on_vector(j, offset):
+            dc_sb[j] = placed([P, K], F32, "dc_sb%d" % j, offset)
+            nc.vector.tensor_copy(dc_sb[j][:], dc[j])
+
+        def scatter_on_vector(j):
+            nc.vector.tensor_copy(windows[j][:].indirect(offsets[:]), dc_sb[j][:])
+            store_window(j)
+
+        def drain_on_scalar(j, h, offset):
+            dc_sb[j, h] = placed([P, HALF], F32, "dc_sb%d_%d" % (j, h), offset)
+            nc.scalar.copy(out=dc_sb[j, h][:], in_=dc_halves[j, h])
+
+        def scatter_on_scalar(j, h):
+            nc.scalar.activation(windows[j][:].indirect(offsets[:, h * HALF // 16 : (h + 1) * HALF // 16]), dc_sb[j, h][:], COPY)
+            if h == 1:
+                store_window(j)
+
+        c_grouped = {}
+
+        def c_turned(j, bank, place, engine_copy, offset=None):
             turn(c_listed[j][:], bank, place)
+            if offset is None:
+                c_grouped[j] = held([P, K], BF16, "c_grouped%d" % j)
+            else:
+                c_grouped[j] = placed([P, K], BF16, "c_grouped%d" % j, offset)
+            unload(engine_copy, bank[:, place * HALF : (place + 1) * HALF], 1, c_grouped[j][:])
 
-        c_listed = {0: placed([P, K], BF16, "c_listed0", 69632)}
-        nc.scalar.activation(c_listed[0][:], c_raw[0][:].indirect(offsets[:]), COPY)
-        nc.vector.tensor_copy(dc_sb[0][:], dc[0])
-        drain_halves(1)
-        scatter_on_vector(0, window_first)
-        scatter_on_scalar(window_scalar, 0, dc_halves[1][0][:])
-        dki_unload(0, dki_turn(0))
-        scatter_on_scalar(window_scalar, 1, dc_halves[1][1][:])
-        store_window(1, window_scalar)
-        nc.vector.tensor_copy(dc_sb[2][:], dc[2])
-        drain_halves(3)
-        dki_bank = dki_turn(1)
-        listed_on_vector(1, 20480)
-        scatter_on_vector(2, window_last)
-        scatter_on_scalar(window_second, 0, dc_halves[3][0][:])
-        dki_unload(1, dki_bank)
-        scatter_on_scalar(window_second, 1, dc_halves[3][1][:])
-        store_window(3, window_second)
-        bank = bank_tile("c01_bank", 2)
-        for j in range(2):
-            c_turn(j, bank, j)
-        c01_grouped = placed([P, 2 * K], BF16, "c01_grouped", 31232)
-        unload(nc.scalar.copy, bank, 2, c01_grouped[:])
-        listed_on_vector(2, 57344)
+        sums = {}
 
-        dki_codes = held([P, K], U32, "dki_codes")
-        dki_scales = placed([P, K], U8, "dki_scales", 26112)
-        quantize(dki_grouped[:], E5M2, dki_codes[:], dki_scales[:])
-        dki_mx = (dki_codes[:], dki_scales[:])
-        c_mx = stationary("c01", c01_grouped[:], 2, 26624)
-        listed_on_vector(3, 27136)
+        c_mx = {}
+
+        def c_quantize(first, count, scales_offset=None):
+            for j, operand in enumerate(stationary("c%d" % first, c_grouped[first][:], count, scales_offset)):
+                c_mx[first + j] = operand
 
         def wk_gradient(j, number):
-            return product(bank_tile("sums%d" % j, number), c_mx[j], dki_mx)
+            sums[j] = product(bank_tile("sums%d" % j, number), c_mx[j], dki_mx)
 
-        def store_wk_gradient(j, sums, engine_copy, result):
+        def store_wk_gradient(j, engine_copy, offset=None):
+            result = held([P, K], F32, "result%d" % j) if offset is None else placed([P, K], F32, "result%d" % j, offset)
             engine_copy(
-                out=result[:].rearrange("p (m u e) -> p m u e", u=2, e=2), in_=sums.rearrange("p (u m e) -> p m u e", u=2, e=2)
+                out=result[:].rearrange("p (m u e) -> p m u e", u=2, e=2), in_=sums[j].rearrange("p (u m e) -> p m u e", u=2, e=2)
             )
             nc.sync.dma_start(out_1[j * P : (j + 1) * P, :], result[:])
 
-        bank = bank_tile("c2_bank", 3)
-        c_turn(2, bank, 0)
-        c2_grouped = placed([P, K], BF16, "c2_grouped", 33792)
-        unload(nc.scalar.copy, bank, 1, c2_grouped[:])
-        sums = [wk_gradient(0, 7), wk_gradient(1, 1)]
-        c_mx = c_mx + stationary("c2", c2_grouped[:], 1)
-        bank = bank_tile("c3_bank", 0)
-        c_turn(3, bank, 0)
-        sums.append(wk_gradient(2, 5))
-        for j in range(2):
-            store_wk_gradient(j, sums[j], nc.scalar.copy, held([P, K], F32, "result%d" % j))
-        c3_grouped = held([P, K], BF16, "c3_grouped")
-        unload(nc.vector.tensor_copy, bank, 1, c3_grouped[:])
-        c_mx = c_mx + stationary("c3", c3_grouped[:], 1)
-        sums.append(wk_gradient(3, 6))
-        store_wk_gradient(2, sums[2], nc.vector.tensor_copy, held([P, K], F32, "result2"))
-        store_wk_gradient(3, sums[3], nc.scalar.copy, held([P, K], F32, "result3"))
+        dc_sb = {}
+        listed(0, "vector", placed([P, K], BF16, "c_listed0", 57344 + 1024))
+        drain_on_vector(0, 28672)
+        drain_on_scalar(1, 0, 34816)
+        c_turned(0, bank_tile("c0_bank", 1), 0, nc.scalar.copy)
+        dki_bank = dki_turn(1, 4)
+        w_mx = w_mx + stationary("w23", w_grouped[1][:], 2, 57344 + 256)
+        scatter_on_vector(0)
+        scatter_on_scalar(1, 0)
+        dc[2] = product(bank_tile("dc2", 5), w_mx[2], dkf_mx)
+        dc[3] = product(bank_tile("dc3", 7), w_mx[3], dkf_mx)
+        for h in range(2):
+            dc_halves[3, h] = dc[3][:, h * HALF : (h + 1) * HALF]
+        drain_on_scalar(1, 1, 36864)
+        dki_unload(1, dki_bank)
+        drain_on_scalar(3, 0, 37888)
+        scatter_on_scalar(1, 1)
+        drain_on_vector(2, 30720)
+        dki_codes = held([P, K], U32, "dki_codes")
+        dki_scales = placed([P, K], U8, "dki_scales", 28672)
+        quantize(dki_grouped[:], E5M2, dki_codes[:], dki_scales[:])
+        dki_mx = (dki_codes[:], dki_scales[:])
+        c_quantize(0, 1, 38912)
+        scatter_on_vector(2)
+        listed(1, "scalar", placed([P, K], BF16, "c_listed1", 39872))
+        scatter_on_scalar(3, 0)
+        drain_on_scalar(3, 1, 36864)
+        wk_gradient(0, 7)
+        c13_bank = bank_tile("c13_bank", 3)
+        c_turned(1, c13_bank, 0, nc.scalar.copy, 37888)
+        scatter_on_scalar(3, 1)
+        listed(2, "vector", placed([P, K], BF16, "c_listed2", 39360))
+        listed(3, "vector", placed([P, K], BF16, "c_listed3", 40384))
+        c_quantize(1, 1)
+        c_turned(2, bank_tile("c2_bank", 2), 0, nc.vector.tensor_copy, 65536)
+        store_wk_gradient(0, nc.scalar.copy, 36864 - 1984)
+        c_turned(3, c13_bank, 1, nc.scalar.copy)
+        wk_gradient(1, 4)
+        c_quantize(2, 1, 40960)
+        wk_gradient(2, 1)
+        c_quantize(3, 1)
+        wk_gradient(3, 5)
+        store_wk_gradient(1, nc.scalar.copy)
+        store_wk_gradient(2, nc.vector.tensor_copy)
+        store_wk_gradient(3, nc.scalar.copy)

@@ -75,20 +75,17 @@ def tile_attend_gmla_cW_kernel(tc, qT, G, cT, wk, ts, cf, offs, out_0, out_1):
             )
             return bank
 
-        warm = held([P, 16], F32, "warm")
-        nc.gpsimd.memset(warm[:, 0:8], 0.0)
         identity = held([P, P], F32, "identity")
         make_identity(nc, identity[:])
 
-        ts_window = held([P, TOKENS], F32, "ts_window")
+        ts_window = placed([P, TOKENS], F32, "ts_window", 77824)
         nc.vector.memset(ts_window[0 : P - 1, :].bitcast(I32), 0)
-        nc.sync.dma_start(ts_window[P - 1 : P, :], ts[0:1, :])
+        nc.scalar.dma_start(ts_window[P - 1 : P, :], ts[0:1, :])
         cf_sb = held([P, PACK], F32, "cf_sb")
         nc.scalar.dma_start(cf_sb[:], cf.rearrange("(p t) o -> p (t o)", t=PACK))
-        nc.scalar.activation(warm[:, 8:16], warm[:, 0:8], COPY)
         offsets = keep.tile([P, K // 16], U16, name="offsets")
         q_rows = qT.rearrange("(m t) r -> m (t r)", t=PACK)
-        q_raw = [placed([P, 2 * K], F32, "q_raw0", 49152), held([P, 2 * K], F32, "q_raw1")]
+        q_raw = [held([P, 2 * K], F32, "q_raw0"), held([P, 2 * K], F32, "q_raw1")]
         nc.sync.dma_start(offsets[:], offs)
         nc.sync.dma_start(q_raw[0][:], q_rows[:, 0 : 2 * K])
         nc.sync.dma_start(q_raw[1][:], q_rows[:, 2 * K : 4 * K])
@@ -101,7 +98,7 @@ def tile_attend_gmla_cW_kernel(tc, qT, G, cT, wk, ts, cf, offs, out_0, out_1):
         wk_rows = wk.rearrange("(p j) f -> p (j f)", j=PACK)
         wk_raw = []
         for h in range(2):
-            raw = held([P, 2 * K], F32, "wk_raw%d" % h)
+            raw = held([P, 2 * K], F32, "wk_raw1") if h else placed([P, 2 * K], F32, "wk_raw0", 0)
             nc.sync.dma_start(raw[:], wk_rows[:, h * 2 * K : (h + 1) * 2 * K])
             wk_raw.append(raw)
         c_raw = []
@@ -111,44 +108,43 @@ def tile_attend_gmla_cW_kernel(tc, qT, G, cT, wk, ts, cf, offs, out_0, out_1):
             c_raw.append(raw)
         out_0_rows = out_0.rearrange("(p j) n -> p j n", j=PACK)
 
-        windows = {j: held([P, TOKENS], F32, "window%d" % j) for j in range(2)}
-        for j in range(2):
-            nc.vector.memset(windows[j][:].bitcast(I32), 0)
+        windows = {0: held([P, TOKENS], F32, "window0")}
+        nc.vector.memset(windows[0][:].bitcast(I32), 0)
 
         ts_listed = held([P, K], F32, "ts_listed")
-        nc.scalar.activation(ts_listed[:], ts_window[:].indirect(offsets[:]), COPY)
+        nc.vector.tensor_copy(ts_listed[:], ts_window[:].indirect(offsets[:]))
         ts_bank = bank_tile("ts_bank", 2)
         for r in range(PACK):
             nc.tensor.transpose(ts_bank[:, r * P : (r + 1) * P], ts_listed[:, r * P : (r + 1) * P], identity[:])
+        for j in (1, 2):
+            windows[j] = placed([P, TOKENS], F32, "window%d" % j, 73728 + (j - 1) * 8192)
+            nc.vector.memset(windows[j][:].bitcast(I32), 0)
 
-        q_bf = [held([P, 2 * K], BF16, "q_bf%d" % h) for h in range(2)]
         q_bank = [bank_tile("q_bank0", 0), bank_tile("q_bank1", 3)]
         q_grouped = [placed([P, 2 * K], BF16, "q_grouped0", 8192), placed([P, 2 * K], BF16, "q_grouped1", 16384)]
-        nc.vector.tensor_copy(q_bf[0][:], q_raw[0][:])
         for j in range(2):
-            turn(q_bf[0][:, j * K : (j + 1) * K], q_bank[0], j)
+            q_bf = held([P, K], BF16, "q_bf%d" % j)
+            nc.scalar.copy(out=q_bf[:], in_=q_raw[0][:, j * K : (j + 1) * K])
+            turn(q_bf[:], q_bank[0], j)
+        q_bf = held([P, 2 * K], BF16, "q_bf23")
+        nc.scalar.copy(out=q_bf[:], in_=q_raw[1][:])
         ts_columns = held([P, PACK], F32, "ts_columns")
         nc.scalar.copy(out=ts_columns[:], in_=ts_bank[:, P - 1 : K : P])
+        unload(nc.scalar.copy, q_bank[0], 2, q_grouped[0][:])
+        bank = q_bank[1]
+        for j in range(2):
+            turn(q_bf[:, j * K : (j + 1) * K], bank, j)
         spread_bank = bank_tile("ts_spread", 1)
         ts_spread = [spread_bank[:, h * HALF : (h + 1) * HALF] for h in range(2)]
         for r in range(PACK):
             nc.tensor.transpose(spread_bank[:, r * P : (r + 1) * P], ts_columns[:, r : r + 1].to_broadcast([P, P]), identity[:])
-        unload(nc.scalar.copy, q_bank[0], 2, q_grouped[0][:])
-        nc.vector.tensor_copy(q_bf[1][:], q_raw[1][:])
-        windows[2] = placed([P, TOKENS], F32, "window2", 49152)
-        nc.vector.memset(windows[2][:].bitcast(I32), 0)
-        bank = q_bank[1]
-        for j in range(2):
-            turn(q_bf[1][:, j * K : (j + 1) * K], bank, j)
         factors = [held([P, PACK * HALF], F32, "factors0"), placed([P, PACK * HALF], F32, "factors1", 57344)]
 
         def factor_rows(h, t):
             nc.scalar.activation(factors[h][:, t * HALF : (t + 1) * HALF], ts_spread[h], COPY, scale=cf_sb[:, t : t + 1])
 
-        factor_rows(0, 0)
-        factor_rows(0, 1)
         unload(nc.scalar.copy, bank, 2, q_grouped[1][:])
-        for n in range(2, 2 * PACK):
+        for n in range(2 * PACK):
             factor_rows(n // PACK, n % PACK)
 
         def g_interleave(h, grouped):
@@ -181,7 +177,7 @@ def tile_attend_gmla_cW_kernel(tc, qT, G, cT, wk, ts, cf, offs, out_0, out_1):
         nc.vector.tensor_copy(w_bf[0][:], wk_raw[0][:])
         b = [scores(k) for k in range(PACK)]
 
-        windows[3] = placed([P, TOKENS], F32, "window3", 2048)
+        windows[3] = placed([P, TOKENS], F32, "window3", 0)
         nc.gpsimd.memset(windows[3][:].bitcast(I32), 0)
 
         dkf_grouped = placed([P, PACK * K], BF16, "dkf_grouped", 36864)
@@ -261,13 +257,15 @@ def tile_attend_gmla_cW_kernel(tc, qT, G, cT, wk, ts, cf, offs, out_0, out_1):
 
         c_grouped = {}
 
-        def c_turned(j, bank, place, engine_copy, offset=None):
-            turn(c_listed[j][:], bank, place)
+        def c_turned(first, count, number, offset=None):
+            bank = bank_tile("c_bank%d" % first, number)
+            for j in range(count):
+                turn(c_listed[first + j][:], bank, j)
             if offset is None:
-                c_grouped[j] = held([P, K], BF16, "c_grouped%d" % j)
+                c_grouped[first] = held([P, count * K], BF16, "c_grouped%d" % first)
             else:
-                c_grouped[j] = placed([P, K], BF16, "c_grouped%d" % j, offset)
-            unload(engine_copy, bank[:, place * HALF : (place + 1) * HALF], 1, c_grouped[j][:])
+                c_grouped[first] = placed([P, count * K], BF16, "c_grouped%d" % first, offset)
+            unload(nc.scalar.copy, bank, count, c_grouped[first][:])
 
         sums = {}
 
@@ -291,7 +289,7 @@ def tile_attend_gmla_cW_kernel(tc, qT, G, cT, wk, ts, cf, offs, out_0, out_1):
         listed(0, "vector", placed([P, K], BF16, "c_listed0", 57344 + 1024))
         drain_on_vector(0, 28672)
         drain_on_scalar(1, 0, 34816)
-        c_turned(0, bank_tile("c0_bank", 1), 0, nc.scalar.copy)
+        c_turned(0, 1, 1)
         dki_bank = dki_turn(1, 4)
         w_mx = w_mx + stationary("w23", w_grouped[1][:], 2, 57344 + 256)
         scatter_on_vector(0)
@@ -302,30 +300,27 @@ def tile_attend_gmla_cW_kernel(tc, qT, G, cT, wk, ts, cf, offs, out_0, out_1):
             dc_halves[3, h] = dc[3][:, h * HALF : (h + 1) * HALF]
         drain_on_scalar(1, 1, 36864)
         dki_unload(1, dki_bank)
+        dc_sb[2] = placed([P, K], F32, "dc_sb2", 40960 - 64)
+        nc.scalar.copy(out=dc_sb[2][:], in_=dc[2])
         drain_on_scalar(3, 0, 37888)
         scatter_on_scalar(1, 1)
-        drain_on_vector(2, 30720)
+        c_quantize(0, 1, 38912)
         dki_codes = held([P, K], U32, "dki_codes")
         dki_scales = placed([P, K], U8, "dki_scales", 28672)
         quantize(dki_grouped[:], E5M2, dki_codes[:], dki_scales[:])
         dki_mx = (dki_codes[:], dki_scales[:])
-        c_quantize(0, 1, 38912)
         scatter_on_vector(2)
-        listed(1, "scalar", placed([P, K], BF16, "c_listed1", 39872))
+        wk_gradient(0, 0)
         scatter_on_scalar(3, 0)
-        drain_on_scalar(3, 1, 36864)
-        wk_gradient(0, 7)
-        c13_bank = bank_tile("c13_bank", 3)
-        c_turned(1, c13_bank, 0, nc.scalar.copy, 37888)
+        drain_on_scalar(3, 1, 35904)
+        store_wk_gradient(0, nc.scalar.copy, 38336)
         scatter_on_scalar(3, 1)
-        listed(2, "vector", placed([P, K], BF16, "c_listed2", 39360))
-        listed(3, "vector", placed([P, K], BF16, "c_listed3", 40384))
-        c_quantize(1, 1)
-        c_turned(2, bank_tile("c2_bank", 2), 0, nc.vector.tensor_copy, 65536)
-        store_wk_gradient(0, nc.scalar.copy, 36864 - 1984)
-        c_turned(3, c13_bank, 1, nc.scalar.copy)
+        for j, offset in ((1, 40384), (2, 41408), (3, 42432)):
+            listed(j, "vector", placed([P, K], BF16, "c_listed%d" % j, offset))
+        c_turned(1, 2, 3, 35904 - 1984)
+        c_turned(3, 1, 2, 35904 + 64)
+        c_quantize(1, 2, 65536)
         wk_gradient(1, 4)
-        c_quantize(2, 1, 40960)
         wk_gradient(2, 1)
         c_quantize(3, 1)
         wk_gradient(3, 5)

@@ -42,11 +42,18 @@ def tile_attend_gmla_cW_kernel(tc, qT, G, cT, wk, ts, cf, offs, out_0, out_1):
         def quantize(grouped, fmt, codes, scales):
             nc.vector.quantize_mx(out=codes.bitcast(fmt), scales=scales, in_=grouped)
 
-        def turn(rows, bank, place):
+        def turn(rows, bank, place, dealt=False):
             words = rows.bitcast(F32)
             for u in range(2):
                 first = (2 * place + u) * P
-                nc.tensor.transpose(bank[:, first : first + P], words[:, u : HALF : 2], identity[:])
+                picked = words[:, u * P : (u + 1) * P] if dealt else words[:, u : HALF : 2]
+                nc.tensor.transpose(bank[:, first : first + P], picked, identity[:])
+
+        def cast_dealt(engine_copy, rows, raw, count):
+            engine_copy(
+                out=rows.rearrange("p (j u w e) -> p j u w e", j=count, u=2, e=2),
+                in_=raw.rearrange("p (j w u e) -> p j u w e", j=count, u=2, e=2),
+            )
 
         def unload(engine_copy, bank, count, grouped):
             engine_copy(
@@ -180,7 +187,7 @@ def tile_attend_gmla_cW_kernel(tc, qT, G, cT, wk, ts, cf, offs, out_0, out_1):
         windows[3] = placed([P, TOKENS], F32, "window3", 0)
         nc.gpsimd.memset(windows[3][:].bitcast(I32), 0)
 
-        dkf_grouped = placed([P, PACK * K], BF16, "dkf_grouped", 36864)
+        dkf_grouped = held([P, PACK * K], BF16, "dkf_grouped")
         for k in range(PACK):
             table = factors[k // 2][:].rearrange("p (t i) -> p t i", t=PACK)[:, :, k % 2 * P : (k % 2 + 1) * P]
             nc.vector.tensor_tensor(
@@ -191,13 +198,14 @@ def tile_attend_gmla_cW_kernel(tc, qT, G, cT, wk, ts, cf, offs, out_0, out_1):
             )
 
         nc.scalar.copy(out=w_bf[1][:], in_=wk_raw[1][:])
-        w_grouped = [held([P, 2 * K], BF16, "w01_grouped"), held([P, 2 * K], BF16, "w23_grouped")]
+        w_grouped = [held([P, 2 * K], BF16, "w%d_grouped" % h) for h in range(2)]
+        w_banks = [bank_tile("w_bank%d" % h, 2 + h) for h in range(2)]
         for h in range(2):
-            bank = bank_tile("w_bank%d" % h, 2 + h)
             for j in range(2):
-                turn(w_bf[h][:, j * K : (j + 1) * K], bank, j)
-            unload(nc.scalar.copy, bank, 2, w_grouped[h][:])
-        dki_grouped = held([P, PACK * K], BF16, "dki_grouped")
+                turn(w_bf[h][:, j * K : (j + 1) * K], w_banks[h], j)
+        for h in range(2):
+            unload(nc.scalar.copy, w_banks[h], 2, w_grouped[h][:])
+        dki_grouped = placed([P, PACK * K], BF16, "dki_grouped", 39872)
         dkf_words = dkf_grouped[:].bitcast(F32)
 
         def dki_turn(u, number):
@@ -212,7 +220,6 @@ def tile_attend_gmla_cW_kernel(tc, qT, G, cT, wk, ts, cf, offs, out_0, out_1):
                 in_=bank.bitcast(BF16).rearrange("p (r m) -> p m r", r=PACK),
             )
 
-        dki_unload(0, dki_turn(0, 0))
         dkf_codes = held([P, K], U32, "dkf_codes")
         dkf_scales = held([P, K], U8, "dkf_scales")
         for h in range(2):
@@ -288,42 +295,43 @@ def tile_attend_gmla_cW_kernel(tc, qT, G, cT, wk, ts, cf, offs, out_0, out_1):
         dc_sb = {}
         listed(0, "vector", placed([P, K], BF16, "c_listed0", 57344 + 1024))
         drain_on_vector(0, 28672)
-        drain_on_scalar(1, 0, 34816)
-        c_turned(0, 1, 1)
-        dki_bank = dki_turn(1, 4)
+        drain_on_scalar(1, 0, 33792)
+        drain_on_scalar(1, 1, 38912)
         w_mx = w_mx + stationary("w23", w_grouped[1][:], 2, 57344 + 256)
         scatter_on_vector(0)
         scatter_on_scalar(1, 0)
-        dc[2] = product(bank_tile("dc2", 5), w_mx[2], dkf_mx)
+        c_turned(0, 1, 5)
+        dc[2] = product(bank_tile("dc2", 4), w_mx[2], dkf_mx)
         dc[3] = product(bank_tile("dc3", 7), w_mx[3], dkf_mx)
         for h in range(2):
             dc_halves[3, h] = dc[3][:, h * HALF : (h + 1) * HALF]
-        drain_on_scalar(1, 1, 36864)
-        dki_unload(1, dki_bank)
-        dc_sb[2] = placed([P, K], F32, "dc_sb2", 40960 - 64)
+        dc_sb[2] = placed([P, K], F32, "dc_sb2", 33792 - 1984)
         nc.scalar.copy(out=dc_sb[2][:], in_=dc[2])
-        drain_on_scalar(3, 0, 37888)
+        drain_on_scalar(3, 0, 33792 + 64)
+        dki_banks = [dki_turn(0, 5), dki_turn(1, 4)]
         scatter_on_scalar(1, 1)
-        c_quantize(0, 1, 38912)
+        c_quantize(0, 1, 28672)
+        scatter_on_vector(2)
+        scatter_on_scalar(3, 0)
+        dki_unload(0, dki_banks[0])
+        drain_on_scalar(3, 1, 37952)
+        dki_unload(1, dki_banks[1])
+        scatter_on_scalar(3, 1)
+        for j, offset in ((1, 31296), (2, 32320), (3, 33344)):
+            listed(j, "vector", placed([P, K], BF16, "c_listed%d" % j, offset))
         dki_codes = held([P, K], U32, "dki_codes")
-        dki_scales = placed([P, K], U8, "dki_scales", 28672)
+        dki_scales = held([P, K], U8, "dki_scales")
         quantize(dki_grouped[:], E5M2, dki_codes[:], dki_scales[:])
         dki_mx = (dki_codes[:], dki_scales[:])
-        scatter_on_vector(2)
+        c_turned(1, 2, 3, 36800)
+        c_turned(3, 1, 2, 38848)
         wk_gradient(0, 0)
-        scatter_on_scalar(3, 0)
-        drain_on_scalar(3, 1, 35904)
-        store_wk_gradient(0, nc.scalar.copy, 38336)
-        scatter_on_scalar(3, 1)
-        for j, offset in ((1, 40384), (2, 41408), (3, 42432)):
-            listed(j, "vector", placed([P, K], BF16, "c_listed%d" % j, offset))
-        c_turned(1, 2, 3, 35904 - 1984)
-        c_turned(3, 1, 2, 35904 + 64)
         c_quantize(1, 2, 65536)
-        wk_gradient(1, 4)
+        wk_gradient(1, 6)
         wk_gradient(2, 1)
         c_quantize(3, 1)
         wk_gradient(3, 5)
-        store_wk_gradient(1, nc.scalar.copy)
-        store_wk_gradient(2, nc.vector.tensor_copy)
-        store_wk_gradient(3, nc.scalar.copy)
+        store_wk_gradient(0, nc.scalar.copy)
+        store_wk_gradient(1, nc.vector.tensor_copy)
+        store_wk_gradient(2, nc.scalar.copy)
+        store_wk_gradient(3, nc.vector.tensor_copy)

@@ -92,27 +92,28 @@ def tile_attend_gmla_cW_kernel(tc, qT, G, cT, wk, ts, cf, offs, out_0, out_1):
         nc.scalar.dma_start(cf_sb[:], cf.rearrange("(p t) o -> p (t o)", t=PACK))
         offsets = keep.tile([P, K // 16], U16, name="offsets")
         q_rows = qT.rearrange("(m t) r -> m (t r)", t=PACK)
-        q_raw = [held([P, 2 * K], F32, "q_raw0"), held([P, 2 * K], F32, "q_raw1")]
+        q_raw = [placed([P, 2 * K], F32, "q_raw0", 0), placed([P, 2 * K], F32, "q_raw1", 90112)]
         nc.sync.dma_start(offsets[:], offs)
         nc.sync.dma_start(q_raw[0][:], q_rows[:, 0 : 2 * K])
         nc.sync.dma_start(q_raw[1][:], q_rows[:, 2 * K : 4 * K])
         g_rows = G.rearrange("(p j) i -> p j i", j=PACK)
         g_raw = []
         for h in range(2):
-            raw = held([P, PACK, HALF], F32, "g_raw%d" % h)
+            raw = held([P, PACK, HALF], F32, "g_raw1") if h else placed([P, PACK, HALF], F32, "g_raw0", 94208)
             nc.sync.dma_start(raw[:], g_rows[:, :, h * HALF : (h + 1) * HALF])
             g_raw.append(raw)
         wk_rows = wk.rearrange("(p j) f -> p (j f)", j=PACK)
-        wk_raw = []
-        for h in range(2):
-            raw = held([P, 2 * K], F32, "wk_raw1") if h else placed([P, 2 * K], F32, "wk_raw0", 0)
-            nc.sync.dma_start(raw[:], wk_rows[:, h * 2 * K : (h + 1) * 2 * K])
-            wk_raw.append(raw)
-        c_raw = []
-        for j in range(PACK):
-            raw = placed([P, TOKENS], F32, "c_raw3", 65536) if j == 3 else held([P, TOKENS], F32, "c_raw%d" % j)
-            nc.sync.dma_start(raw[:], cT[j * P : (j + 1) * P, :])
-            c_raw.append(raw)
+        wk_raw = {}
+        c_raw = {}
+
+        def load_wk(h, offset):
+            wk_raw[h] = placed([P, 2 * K], F32, "wk_raw%d" % h, offset)
+            nc.sync.dma_start(wk_raw[h][:], wk_rows[:, h * 2 * K : (h + 1) * 2 * K])
+
+        def load_latents(j, offset):
+            c_raw[j] = placed([P, TOKENS], F32, "c_raw%d" % j, offset)
+            nc.sync.dma_start(c_raw[j][:], cT[j * P : (j + 1) * P, :])
+
         out_0_rows = out_0.rearrange("(p j) n -> p j n", j=PACK)
 
         windows = {0: held([P, TOKENS], F32, "window0")}
@@ -128,13 +129,15 @@ def tile_attend_gmla_cW_kernel(tc, qT, G, cT, wk, ts, cf, offs, out_0, out_1):
             nc.vector.memset(windows[j][:].bitcast(I32), 0)
 
         q_bank = [bank_tile("q_bank0", 0), bank_tile("q_bank1", 3)]
-        q_grouped = [placed([P, 2 * K], BF16, "q_grouped0", 8192), placed([P, 2 * K], BF16, "q_grouped1", 16384)]
+        q_grouped = [placed([P, 2 * K], BF16, "q_grouped0", 102400), placed([P, 2 * K], BF16, "q_grouped1", 16384)]
         for j in range(2):
             q_bf = held([P, K], BF16, "q_bf%d" % j)
             nc.scalar.copy(out=q_bf[:], in_=q_raw[0][:, j * K : (j + 1) * K])
             turn(q_bf[:], q_bank[0], j)
         q_bf = held([P, 2 * K], BF16, "q_bf23")
         nc.scalar.copy(out=q_bf[:], in_=q_raw[1][:])
+        load_wk(0, 0)
+        load_wk(1, 90112)
         ts_columns = held([P, PACK], F32, "ts_columns")
         nc.scalar.copy(out=ts_columns[:], in_=ts_bank[:, P - 1 : K : P])
         unload(nc.scalar.copy, q_bank[0], 2, q_grouped[0][:])
@@ -145,7 +148,7 @@ def tile_attend_gmla_cW_kernel(tc, qT, G, cT, wk, ts, cf, offs, out_0, out_1):
         ts_spread = [spread_bank[:, h * HALF : (h + 1) * HALF] for h in range(2)]
         for r in range(PACK):
             nc.tensor.transpose(spread_bank[:, r * P : (r + 1) * P], ts_columns[:, r : r + 1].to_broadcast([P, P]), identity[:])
-        factors = [held([P, PACK * HALF], F32, "factors0"), placed([P, PACK * HALF], F32, "factors1", 57344)]
+        factors = [placed([P, PACK * HALF], F32, "factors0", 110592), placed([P, PACK * HALF], F32, "factors1", 57344)]
 
         def factor_rows(h, t):
             nc.scalar.activation(factors[h][:, t * HALF : (t + 1) * HALF], ts_spread[h], COPY, scale=cf_sb[:, t : t + 1])
@@ -174,12 +177,14 @@ def tile_attend_gmla_cW_kernel(tc, qT, G, cT, wk, ts, cf, offs, out_0, out_1):
 
         g_grouped0 = placed([P, 2 * K], BF16, "g_grouped0", 22528)
         g_interleave(0, g_grouped0)
+        load_latents(0, 94208)
         q_mx = stationary("q01", q_grouped[0][:], 2)
         g_mx = g_quantize(0, g_grouped0)
-        g_grouped1 = placed([P, 2 * K], BF16, "g_grouped1", 8192)
+        g_grouped1 = placed([P, 2 * K], BF16, "g_grouped1", 102400)
         g_interleave(1, g_grouped1)
         q_mx = q_mx + stationary("q23", q_grouped[1][:], 2)
         g_mx = g_mx + g_quantize(1, g_grouped1)
+        load_latents(1, 102400)
         w_bf = [placed([P, 2 * K], BF16, "w01_bf", 16384 - 1984), placed([P, 2 * K], BF16, "w23_bf", 16384 + 64)]
         nc.vector.tensor_copy(w_bf[0][:], wk_raw[0][:])
         b = [scores(k) for k in range(PACK)]
@@ -197,8 +202,10 @@ def tile_attend_gmla_cW_kernel(tc, qT, G, cT, wk, ts, cf, offs, out_0, out_1):
                 op=MULT,
             )
 
+        load_latents(2, 110592)
+
         nc.scalar.copy(out=w_bf[1][:], in_=wk_raw[1][:])
-        w_grouped = [held([P, 2 * K], BF16, "w%d_grouped" % h) for h in range(2)]
+        w_grouped = [placed([P, 2 * K], BF16, "w0_grouped", 65536), held([P, 2 * K], BF16, "w1_grouped")]
         w_banks = [bank_tile("w_bank%d" % h, 2 + h) for h in range(2)]
         for h in range(2):
             for j in range(2):
@@ -227,6 +234,7 @@ def tile_attend_gmla_cW_kernel(tc, qT, G, cT, wk, ts, cf, offs, out_0, out_1):
             quantize(dkf_grouped[:, h * 2 * K : (h + 1) * 2 * K], E5M2, dkf_codes[:, cols], dkf_scales[:, cols])
         dkf_mx = (dkf_codes[:], dkf_scales[:])
         w_mx = stationary("w01", w_grouped[0][:], 2, 57344)
+        load_latents(3, 65536)
         dc = {0: product(bank_tile("dc0", 4), w_mx[0], dkf_mx)}
         dc_halves = {}
         for h in range(2):
@@ -332,6 +340,6 @@ def tile_attend_gmla_cW_kernel(tc, qT, G, cT, wk, ts, cf, offs, out_0, out_1):
         c_quantize(3, 1)
         wk_gradient(3, 5)
         store_wk_gradient(0, nc.scalar.copy)
-        store_wk_gradient(1, nc.vector.tensor_copy)
-        store_wk_gradient(2, nc.scalar.copy)
-        store_wk_gradient(3, nc.vector.tensor_copy)
+        store_wk_gradient(1, nc.scalar.copy)
+        store_wk_gradient(2, nc.vector.tensor_copy)
+        store_wk_gradient(3, nc.scalar.copy)

@@ -196,9 +196,9 @@ def tile_attend_gmla_cW_kernel(tc, qT, G, cT, wk, ts, cf, offs, out_0, out_1):
         for k in range(PACK):
             table = factors[k // 2][:].rearrange("p (t i) -> p t i", t=PACK)[:, :, k % 2 * P : (k % 2 + 1) * P]
             nc.vector.tensor_tensor(
-                out=dkf_grouped[:, k * K : (k + 1) * K].rearrange("p (c i t) -> p c t i", i=4, t=PACK),
-                in0=b[k].rearrange("p (t c i) -> p c t i", t=PACK, i=4),
-                in1=table.rearrange("p t (c i) -> p c t i", i=4),
+                out=dkf_grouped[:, k * K : (k + 1) * K].rearrange("p (c i t) -> p c t i", i=2, t=PACK),
+                in0=b[k].rearrange("p (t c i) -> p c t i", t=PACK, i=2),
+                in1=table.rearrange("p t (c i) -> p c t i", i=2),
                 op=MULT,
             )
 

@@ -212,7 +212,7 @@ def tile_attend_gmla_cW_kernel(tc, qT, G, cT, wk, ts, cf, offs, out_0, out_1):
                 turn(w_bf[h][:, j * K : (j + 1) * K], w_banks[h], j)
         for h in range(2):
             unload(nc.scalar.copy, w_banks[h], 2, w_grouped[h][:])
-        dki_grouped = placed([P, PACK * K], BF16, "dki_grouped", 39872)
+        dki_grouped = held([P, PACK * K], BF16, "dki_grouped")
         dkf_words = dkf_grouped[:].bitcast(F32)
 
         def dki_turn(u, number):
@@ -227,6 +227,7 @@ def tile_attend_gmla_cW_kernel(tc, qT, G, cT, wk, ts, cf, offs, out_0, out_1):
                 in_=bank.bitcast(BF16).rearrange("p (r m) -> p m r", r=PACK),
             )
 
+        dki_unload(0, dki_turn(0, 0))
         dkf_codes = held([P, K], U32, "dkf_codes")
         dkf_scales = held([P, K], U8, "dkf_scales")
         for h in range(2):
@@ -304,7 +305,7 @@ def tile_attend_gmla_cW_kernel(tc, qT, G, cT, wk, ts, cf, offs, out_0, out_1):
         listed(0, "vector", placed([P, K], BF16, "c_listed0", 57344 + 1024))
         drain_on_vector(0, 28672)
         drain_on_scalar(1, 0, 33792)
-        drain_on_scalar(1, 1, 38912)
+        drain_on_scalar(1, 1, 37888)
         w_mx = w_mx + stationary("w23", w_grouped[1][:], 2, 57344 + 256)
         scatter_on_vector(0)
         scatter_on_scalar(1, 0)
@@ -315,24 +316,23 @@ def tile_attend_gmla_cW_kernel(tc, qT, G, cT, wk, ts, cf, offs, out_0, out_1):
             dc_halves[3, h] = dc[3][:, h * HALF : (h + 1) * HALF]
         dc_sb[2] = placed([P, K], F32, "dc_sb2", 33792 - 1984)
         nc.scalar.copy(out=dc_sb[2][:], in_=dc[2])
-        drain_on_scalar(3, 0, 33792 + 64)
-        dki_banks = [dki_turn(0, 5), dki_turn(1, 4)]
+        drain_on_scalar(3, 0, 33984)
+        drain_on_scalar(3, 1, 41984)
+        dki_bank = dki_turn(1, 4)
         scatter_on_scalar(1, 1)
-        c_quantize(0, 1, 28672)
+        c_quantize(0, 1, 33856)
         scatter_on_vector(2)
         scatter_on_scalar(3, 0)
-        dki_unload(0, dki_banks[0])
-        drain_on_scalar(3, 1, 37952)
-        dki_unload(1, dki_banks[1])
+        dki_unload(1, dki_bank)
         scatter_on_scalar(3, 1)
-        for j, offset in ((1, 31296), (2, 32320), (3, 33344)):
+        for j, offset in ((1, 37888 - 960), (2, 37888 + 64), (3, 106496)):
             listed(j, "vector", placed([P, K], BF16, "c_listed%d" % j, offset))
         dki_codes = held([P, K], U32, "dki_codes")
         dki_scales = held([P, K], U8, "dki_scales")
         quantize(dki_grouped[:], E5M2, dki_codes[:], dki_scales[:])
         dki_mx = (dki_codes[:], dki_scales[:])
-        c_turned(1, 2, 3, 36800)
-        c_turned(3, 1, 2, 38848)
+        c_turned(1, 2, 3, 41984 - 1984)
+        c_turned(3, 1, 2, 41984 + 64)
         wk_gradient(0, 0)
         c_quantize(1, 2, 65536)
         wk_gradient(1, 6)

@@ -129,7 +129,7 @@ def tile_attend_gmla_cW_kernel(tc, qT, G, cT, wk, ts, cf, offs, out_0, out_1):
             nc.vector.memset(windows[j][:].bitcast(I32), 0)
 
         q_bank = [bank_tile("q_bank0", 0), bank_tile("q_bank1", 3)]
-        q_grouped = [placed([P, 2 * K], BF16, "q_grouped0", 102400), placed([P, 2 * K], BF16, "q_grouped1", 16384)]
+        q_grouped = [placed([P, 2 * K], BF16, "q_grouped0", 131072), placed([P, 2 * K], BF16, "q_grouped1", 16384)]
         for j in range(2):
             q_bf = held([P, K], BF16, "q_bf%d" % j)
             nc.scalar.copy(out=q_bf[:], in_=q_raw[0][:, j * K : (j + 1) * K])
@@ -180,16 +180,16 @@ def tile_attend_gmla_cW_kernel(tc, qT, G, cT, wk, ts, cf, offs, out_0, out_1):
         load_latents(0, 94208)
         q_mx = stationary("q01", q_grouped[0][:], 2)
         g_mx = g_quantize(0, g_grouped0)
-        g_grouped1 = placed([P, 2 * K], BF16, "g_grouped1", 102400)
+        g_grouped1 = placed([P, 2 * K], BF16, "g_grouped1", 131072)
         g_interleave(1, g_grouped1)
         q_mx = q_mx + stationary("q23", q_grouped[1][:], 2)
         g_mx = g_mx + g_quantize(1, g_grouped1)
-        load_latents(1, 102400)
+        load_latents(1, 131136)
         w_bf = [placed([P, 2 * K], BF16, "w01_bf", 16384 - 1984), placed([P, 2 * K], BF16, "w23_bf", 16384 + 64)]
         nc.vector.tensor_copy(w_bf[0][:], wk_raw[0][:])
         b = [scores(k) for k in range(PACK)]
 
-        windows[3] = placed([P, TOKENS], F32, "window3", 0)
+        windows[3] = placed([P, TOKENS], F32, "window3", 122944)
         nc.gpsimd.memset(windows[3][:].bitcast(I32), 0)
 
         dkf_grouped = held([P, PACK * K], BF16, "dkf_grouped")
@@ -325,7 +325,7 @@ def tile_attend_gmla_cW_kernel(tc, qT, G, cT, wk, ts, cf, offs, out_0, out_1):
         scatter_on_scalar(3, 0)
         dki_unload(1, dki_bank)
         scatter_on_scalar(3, 1)
-        for j, offset in ((1, 37888 - 960), (2, 37888 + 64), (3, 106496)):
+        for j, offset in ((1, 37888 - 960), (2, 37888 + 64), (3, 135232)):
             listed(j, "vector", placed([P, K], BF16, "c_listed%d" % j, offset))
         dki_codes = held([P, K], U32, "dki_codes")
         dki_scales = held([P, K], U8, "dki_scales")

from contextlib import ExitStack

import concourse.mybir as mybir
from concourse.masks import make_identity

F32 = mybir.dt.float32
BF16 = mybir.dt.bfloat16
I32 = mybir.dt.int32
U32 = mybir.dt.uint32
U16 = mybir.dt.uint16
U8 = mybir.dt.uint8
E4M3 = mybir.dt.float8_e4m3fn_x4
E5M2 = mybir.dt.float8_e5m2_x4
MULT = mybir.AluOpType.mult
COPY = mybir.ActivationFunctionType.Copy

P = 128
PACK = 4
K = P * PACK
HALF = K // 2
TOKENS = 2048
BANK_BYTES = 2048
FLOPS = 3 * 2 * K * K * K


def tile_attend_gmla_cW_kernel(tc, qT, G, cT, wk, ts, cf, offs, out_0, out_1):
    nc = tc.nc
    with ExitStack() as ctx:
        keep = ctx.enter_context(tc.tile_pool(name="keep", bufs=1))
        laid = ctx.enter_context(tc.tile_pool(name="laid", bufs=1))
        psum = ctx.enter_context(tc.psum_pool(name="psum", bufs=1))

        def held(shape, dtype, name):
            return keep.tile(shape, dtype, name=name, align_bytes=64)

        def placed(shape, dtype, name, offset):
            return laid.tile(shape, dtype, name=name, align_bytes=64, offset=offset)

        def bank_tile(name, number, count=1):
            return psum.tile([P, count * K], F32, name=name, offset=number * BANK_BYTES)[:]

        def quantize(grouped, fmt, codes, scales):
            nc.vector.quantize_mx(out=codes.bitcast(fmt), scales=scales, in_=grouped)

        def turn(rows, bank, place, dealt=False):
            words = rows.bitcast(F32)
            for u in range(2):
                first = (2 * place + u) * P
                picked = words[:, u * P : (u + 1) * P] if dealt else words[:, u : HALF : 2]
                nc.tensor.transpose(bank[:, first : first + P], picked, identity[:])

        def cast_dealt(engine_copy, rows, raw, count):
            engine_copy(
                out=rows.rearrange("p (j u w e) -> p j u w e", j=count, u=2, e=2),
                in_=raw.rearrange("p (j w u e) -> p j u w e", j=count, u=2, e=2),
            )

        def unload(engine_copy, bank, count, grouped):
            engine_copy(
                out=grouped.bitcast(F32).rearrange("p (j r u) -> p j r u", j=count, u=2),
                in_=bank[:, 0 : count * 2 * P].rearrange("p (j u r) -> p j r u", j=count, u=2),
            )

        def stationary(name, grouped, count, scales_offset=None):
            codes = held([P, count * P], U32, name + "_codes")
            if scales_offset is None:
                scales = held([P, count * P], U8, name + "_scales")
            else:
                scales = placed([P, count * P], U8, name + "_scales", scales_offset)
            quantize(grouped, E4M3, codes[:], scales[:])
            return [(codes[:, j * P : (j + 1) * P], scales[:, j * P : (j + 1) * P]) for j in range(count)]

        def product(bank, still, moving):
            nc.tensor.matmul_mx(
                out=bank,
                lhsT=still[0].bitcast(E4M3),
                lhsT_scale=still[1],
                rhs=moving[0].bitcast(E5M2),
                rhs_scale=moving[1],
                start=True,
                stop=True,
            )
            return bank

        identity = held([P, P], F32, "identity")
        make_identity(nc, identity[:])

        ts_window = placed([P, TOKENS], F32, "ts_window", 77824)
        nc.vector.memset(ts_window[0 : P - 1, :].bitcast(I32), 0)
        nc.scalar.dma_start(ts_window[P - 1 : P, :], ts[0:1, :])
        cf_sb = held([P, PACK], F32, "cf_sb")
        nc.scalar.dma_start(cf_sb[:], cf.rearrange("(p t) o -> p (t o)", t=PACK))
        offsets = keep.tile([P, K // 16], U16, name="offsets")
        q_rows = qT.rearrange("(m t) r -> m (t r)", t=PACK)
        q_raw = [placed([P, 2 * K], F32, "q_raw0", 0), placed([P, 2 * K], F32, "q_raw1", 90112)]
        nc.sync.dma_start(offsets[:], offs)
        nc.sync.dma_start(q_raw[0][:], q_rows[:, 0 : 2 * K])
        nc.sync.dma_start(q_raw[1][:], q_rows[:, 2 * K : 4 * K])
        g_rows = G.rearrange("(p j) i -> p j i", j=PACK)
        g_raw = []
        for h in range(2):
            raw = held([P, PACK, HALF], F32, "g_raw1") if h else placed([P, PACK, HALF], F32, "g_raw0", 94208)
            nc.sync.dma_start(raw[:], g_rows[:, :, h * HALF : (h + 1) * HALF])
            g_raw.append(raw)
        wk_rows = wk.rearrange("(p j) f -> p (j f)", j=PACK)
        wk_raw = {}
        c_raw = {}

        def load_wk(h, offset):
            wk_raw[h] = placed([P, 2 * K], F32, "wk_raw%d" % h, offset)
            nc.sync.dma_start(wk_raw[h][:], wk_rows[:, h * 2 * K : (h + 1) * 2 * K])

        def load_latents(j, offset):
            c_raw[j] = placed([P, TOKENS], F32, "c_raw%d" % j, offset)
            nc.sync.dma_start(c_raw[j][:], cT[j * P : (j + 1) * P, :])

        out_0_rows = out_0.rearrange("(p j) n -> p j n", j=PACK)

        windows = {0: held([P, TOKENS], F32, "window0")}
        nc.vector.memset(windows[0][:].bitcast(I32), 0)

        ts_listed = held([P, K], F32, "ts_listed")
        nc.vector.tensor_copy(ts_listed[:], ts_window[:].indirect(offsets[:]))
        ts_bank = bank_tile("ts_bank", 2)
        for r in range(PACK):
            nc.tensor.transpose(ts_bank[:, r * P : (r + 1) * P], ts_listed[:, r * P : (r + 1) * P], identity[:])
        for j in (1, 2):
            windows[j] = placed([P, TOKENS], F32, "window%d" % j, 73728 + (j - 1) * 8192)
            nc.vector.memset(windows[j][:].bitcast(I32), 0)

        q_bank = [bank_tile("q_bank0", 0), bank_tile("q_bank1", 3)]
        q_grouped = [placed([P, 2 * K], BF16, "q_grouped0", 131072), placed([P, 2 * K], BF16, "q_grouped1", 16384)]
        for j in range(2):
            q_bf = held([P, K], BF16, "q_bf%d" % j)
            nc.scalar.copy(out=q_bf[:], in_=q_raw[0][:, j * K : (j + 1) * K])
            turn(q_bf[:], q_bank[0], j)
        q_bf = held([P, 2 * K], BF16, "q_bf23")
        nc.scalar.copy(out=q_bf[:], in_=q_raw[1][:])
        load_wk(0, 0)
        load_wk(1, 90112)
        ts_columns = held([P, PACK], F32, "ts_columns")
        nc.scalar.copy(out=ts_columns[:], in_=ts_bank[:, P - 1 : K : P])
        unload(nc.scalar.copy, q_bank[0], 2, q_grouped[0][:])
        bank = q_bank[1]
        for j in range(2):
            turn(q_bf[:, j * K : (j + 1) * K], bank, j)
        spread_bank = bank_tile("ts_spread", 1)
        ts_spread = [spread_bank[:, h * HALF : (h + 1) * HALF] for h in range(2)]
        for r in range(PACK):
            nc.tensor.transpose(spread_bank[:, r * P : (r + 1) * P], ts_columns[:, r : r + 1].to_broadcast([P, P]), identity[:])
        factors = [placed([P, PACK * HALF], F32, "factors0", 110592), placed([P, PACK * HALF], F32, "factors1", 57344)]

        def factor_rows(h, t):
            nc.scalar.activation(factors[h][:, t * HALF : (t + 1) * HALF], ts_spread[h], COPY, scale=cf_sb[:, t : t + 1])

        unload(nc.scalar.copy, bank, 2, q_grouped[1][:])
        for n in range(2 * PACK):
            factor_rows(n // PACK, n % PACK)

        def g_interleave(h, grouped):
            nc.vector.tensor_copy(
                out=grouped[:].rearrange("p (c i t) -> p c t i", i=4, t=PACK),
                in_=g_raw[h][:].rearrange("p t (c i) -> p c t i", i=4),
            )

        def g_quantize(h, grouped):
            codes = held([P, HALF], U32, "g_codes%d" % h)
            scales = held([P, HALF], U8, "g_scales%d" % h)
            quantize(grouped[:], E5M2, codes[:], scales[:])
            return [(codes[:, k * P : (k + 1) * P], scales[:, k * P : (k + 1) * P]) for k in range(2)]

        def scores(k):
            bank = bank_tile("b%d" % k, 4 + k)
            for t in range(PACK):
                product(bank[:, t * P : (t + 1) * P], q_mx[t], g_mx[k])
            return bank

        g_grouped0 = placed([P, 2 * K], BF16, "g_grouped0", 22528)
        g_interleave(0, g_grouped0)
        load_latents(0, 94208)
        q_mx = stationary("q01", q_grouped[0][:], 2)
        g_mx = g_quantize(0, g_grouped0)
        g_grouped1 = placed([P, 2 * K], BF16, "g_grouped1", 131072)
        g_interleave(1, g_grouped1)
        q_mx = q_mx + stationary("q23", q_grouped[1][:], 2)
        g_mx = g_mx + g_quantize(1, g_grouped1)
        load_latents(1, 131136)
        w_bf = [placed([P, 2 * K], BF16, "w01_bf", 16384 - 1984), placed([P, 2 * K], BF16, "w23_bf", 16384 + 64)]
        nc.vector.tensor_copy(w_bf[0][:], wk_raw[0][:])
        b = [scores(k) for k in range(PACK)]

        windows[3] = placed([P, TOKENS], F32, "window3", 122944)
        nc.gpsimd.memset(windows[3][:].bitcast(I32), 0)

        dkf_grouped = held([P, PACK * K], BF16, "dkf_grouped")
        for k in range(PACK):
            table = factors[k // 2][:].rearrange("p (t i) -> p t i", t=PACK)[:, :, k % 2 * P : (k % 2 + 1) * P]
            nc.vector.tensor_tensor(
                out=dkf_grouped[:, k * K : (k + 1) * K].rearrange("p (c i t) -> p c t i", i=2, t=PACK),
                in0=b[k].rearrange("p (t c i) -> p c t i", t=PACK, i=2),
                in1=table.rearrange("p t (c i) -> p c t i", i=2),
                op=MULT,
            )

        load_latents(2, 110592)

        nc.scalar.copy(out=w_bf[1][:], in_=wk_raw[1][:])
        w_grouped = [placed([P, 2 * K], BF16, "w0_grouped", 65536), held([P, 2 * K], BF16, "w1_grouped")]
        w_banks = [bank_tile("w_bank%d" % h, 2 + h) for h in range(2)]
        for h in range(2):
            for j in range(2):
                turn(w_bf[h][:, j * K : (j + 1) * K], w_banks[h], j)
        for h in range(2):
            unload(nc.scalar.copy, w_banks[h], 2, w_grouped[h][:])
        dki_grouped = held([P, PACK * K], BF16, "dki_grouped")
        dkf_words = dkf_grouped[:].bitcast(F32)

        def dki_turn(u, number):
            bank = bank_tile("dki_bank%d" % u, number)
            for r in range(PACK):
                nc.tensor.transpose(bank[:, r * P : (r + 1) * P], dkf_words[:, 2 * r + u : 2 * K : 2 * PACK], identity[:])
            return bank

        def dki_unload(u, bank):
            nc.scalar.copy(
                out=dki_grouped[:, u * 2 * K : (u + 1) * 2 * K].rearrange("p (m r) -> p m r", r=PACK),
                in_=bank.bitcast(BF16).rearrange("p (r m) -> p m r", r=PACK),
            )

        dki_unload(0, dki_turn(0, 0))
        dkf_codes = held([P, K], U32, "dkf_codes")
        dkf_scales = held([P, K], U8, "dkf_scales")
        for h in range(2):
            cols = slice(h * HALF, (h + 1) * HALF)
            quantize(dkf_grouped[:, h * 2 * K : (h + 1) * 2 * K], E5M2, dkf_codes[:, cols], dkf_scales[:, cols])
        dkf_mx = (dkf_codes[:], dkf_scales[:])
        w_mx = stationary("w01", w_grouped[0][:], 2, 57344)
        load_latents(3, 65536)
        dc = {0: product(bank_tile("dc0", 4), w_mx[0], dkf_mx)}
        dc_halves = {}
        for h in range(2):
            cols = slice(h * HALF, (h + 1) * HALF)
            dc_halves[1, h] = product(bank_tile("dc1_%d" % h, 5 + h)[:, 0:HALF], w_mx[1], (dkf_codes[:, cols], dkf_scales[:, cols]))

        c_listed = {}

        def listed(j, engine, tile):
            c_listed[j] = tile
            if engine == "vector":
                nc.vector.tensor_copy(tile[:], c_raw[j][:].indirect(offsets[:]))
            else:
                nc.scalar.activation(tile[:], c_raw[j][:].indirect(offsets[:]), COPY)

        def store_window(j):
            nc.sync.dma_start(out_0_rows[:, j, :], windows[j][:])

        def drain_on_vector(j, offset):
            dc_sb[j] = placed([P, K], F32, "dc_sb%d" % j, offset)
            nc.vector.tensor_copy(dc_sb[j][:], dc[j])

        def scatter_on_vector(j):
            nc.vector.tensor_copy(windows[j][:].indirect(offsets[:]), dc_sb[j][:])
            store_window(j)

        def drain_on_scalar(j, h, offset):
            dc_sb[j, h] = placed([P, HALF], F32, "dc_sb%d_%d" % (j, h), offset)
            nc.scalar.copy(out=dc_sb[j, h][:], in_=dc_halves[j, h])

        def scatter_on_scalar(j, h):
            nc.scalar.activation(windows[j][:].indirect(offsets[:, h * HALF // 16 : (h + 1) * HALF // 16]), dc_sb[j, h][:], COPY)
            if h == 1:
                store_window(j)

        c_grouped = {}

        def c_turned(first, count, number, offset=None):
            bank = bank_tile("c_bank%d" % first, number)
            for j in range(count):
                turn(c_listed[first + j][:], bank, j)
            if offset is None:
                c_grouped[first] = held([P, count * K], BF16, "c_grouped%d" % first)
            else:
                c_grouped[first] = placed([P, count * K], BF16, "c_grouped%d" % first, offset)
            unload(nc.scalar.copy, bank, count, c_grouped[first][:])

        sums = {}

        c_mx = {}

        def c_quantize(first, count, scales_offset=None):
            for j, operand in enumerate(stationary("c%d" % first, c_grouped[first][:], count, scales_offset)):
                c_mx[first + j] = operand

        def wk_gradient(j, number):
            sums[j] = product(bank_tile("sums%d" % j, number), c_mx[j], dki_mx)

        def store_wk_gradient(j, engine_copy, offset=None):
            result = held([P, K], F32, "result%d" % j) if offset is None else placed([P, K], F32, "result%d" % j, offset)
            engine_copy(
                out=result[:].rearrange("p (m u e) -> p m u e", u=2, e=2), in_=sums[j].rearrange("p (u m e) -> p m u e", u=2, e=2)
            )
            nc.sync.dma_start(out_1[j * P : (j + 1) * P, :], result[:])

        dc_sb = {}
        listed(0, "vector", placed([P, K], BF16, "c_listed0", 57344 + 1024))
        drain_on_vector(0, 28672)
        drain_on_scalar(1, 0, 33792)
        drain_on_scalar(1, 1, 37888)
        w_mx = w_mx + stationary("w23", w_grouped[1][:], 2, 57344 + 256)
        scatter_on_vector(0)
        scatter_on_scalar(1, 0)
        c_turned(0, 1, 5)
        dc[2] = product(bank_tile("dc2", 4), w_mx[2], dkf_mx)
        dc[3] = product(bank_tile("dc3", 7), w_mx[3], dkf_mx)
        for h in range(2):
            dc_halves[3, h] = dc[3][:, h * HALF : (h + 1) * HALF]
        dc_sb[2] = placed([P, K], F32, "dc_sb2", 33792 - 1984)
        nc.scalar.copy(out=dc_sb[2][:], in_=dc[2])
        drain_on_scalar(3, 0, 33984)
        drain_on_scalar(3, 1, 41984)
        dki_bank = dki_turn(1, 4)
        scatter_on_scalar(1, 1)
        c_quantize(0, 1, 33856)
        scatter_on_vector(2)
        scatter_on_scalar(3, 0)
        dki_unload(1, dki_bank)
        scatter_on_scalar(3, 1)
        for j, offset in ((1, 37888 - 960), (2, 37888 + 64), (3, 135232)):
            listed(j, "vector", placed([P, K], BF16, "c_listed%d" % j, offset))
        dki_codes = held([P, K], U32, "dki_codes")
        dki_scales = held([P, K], U8, "dki_scales")
        quantize(dki_grouped[:], E5M2, dki_codes[:], dki_scales[:])
        dki_mx = (dki_codes[:], dki_scales[:])
        c_turned(1, 2, 3, 41984 - 1984)
        c_turned(3, 1, 2, 41984 + 64)
        wk_gradient(0, 0)
        c_quantize(1, 2, 65536)
        wk_gradient(1, 6)
        wk_gradient(2, 1)
        c_quantize(3, 1)
        wk_gradient(3, 5)
        store_wk_gradient(0, nc.scalar.copy)
        store_wk_gradient(1, nc.scalar.copy)
        store_wk_gradient(2, nc.vector.tensor_copy)
        store_wk_gradient(3, nc.scalar.copy)
